import numpy as np, ml_dtypes
CORES = [40,64,80,88,96,104,120,144]
N = 8
import mx_ref
BF = ml_dtypes.bfloat16
def pick(q, e):
    c = np.concatenate([q[0].reshape(128, -1, 4), np.zeros((128, 1, 4), np.uint8)], axis=1); s = np.concatenate([q[1], np.ones((16, 1), np.uint8)], axis=1)
    return (np.ascontiguousarray(c[:, e].reshape(128, -1)), np.ascontiguousarray(s[:, e]))
def join(*qs):
    return (np.concatenate([q[0] for q in qs], axis=1), np.concatenate([q[1] for q in qs], axis=1))
def put(q, e, v):
    c, s = q[0].reshape(128, -1, 4).copy(), q[1].copy(); c[:, e] = v[0].reshape(128, -1, 4); s[:, e] = v[1]
    return (c.reshape(128, -1), s)
def pk(c, s):
    return (np.ascontiguousarray(c), mx_ref.live(s))
def emit(q):
    return q[0], q[1]
def cols(t, e):
    v = np.concatenate([t.reshape(128, -1, 4), np.zeros((128, 1, 4), BF)], axis=1)
    return np.ascontiguousarray(v[:, e]).reshape(128, -1)
def tile(rs):
    return np.stack(rs, axis=2).reshape(128, -1).astype(BF)
def cut(t, i, w=512):
    return t[:, w * i:w * i + w]
def f(rng, *shape):
    return mx_ref.flush((rng.standard_normal(shape, dtype=np.float32) * np.exp2(rng.integers(-2, 3, shape[:-1] + (1,)))).astype(BF))
def wide(rng, *shape, cols=0):
    v = rng.standard_normal(shape, dtype=np.float32) * np.exp2(rng.integers(-12, 13, shape)).astype(np.float32)
    if cols: v *= np.repeat(np.exp2(rng.integers(-cols, cols + 1, shape[:-2] + (1, shape[-1] // 4))) * (rng.random(shape[:-2] + (1, shape[-1] // 4)) > 0.0625), 4, axis=-1).astype(np.float32)
    return mx_ref.flush(v.astype(BF))
T, CAPP, CB, DF = 128, 32, 16, 64
LEVELS = np.array([0, 16, 32, 64], np.float32)
def taken(first, a):
    return np.concatenate([s * T + np.flatnonzero(first[s] == a)[:CAPP] for s in range(N)])
def plain(rng):
    rt, r2 = np.array(f(rng, 128, 512)), np.zeros((128, 512), BF)
    rt[:, 4 * N:] = 0
    v = f(rng, 128, 4 * N + 4).astype(np.float32).reshape(128, N + 1, 4)
    v = v - np.mean(v, axis=(0, 2), keepdims=True)
    r2[:, :4 * N + 4] = mx_ref.flush(v.reshape(128, -1).astype(BF))
    return {"x": np.array(f(rng, N, 128, 4 * T)), "rt": np.stack([rt] * N), "w": np.array(f(rng, N, 128, 2048)), "r2": np.stack([r2] * N), "vx": f(rng, N, 128, 512), "vh": f(rng, N, 128, 512)}
def planned(rng, A, B, V, dead=None, same=False):
    d = plain(rng)
    rt, r2, wt = d["rt"], d["r2"], d["w"].reshape(N, 128, 4, 128, 4)
    rt[:, 120:] = 0
    r2[:, :4 * N + 4] = 0
    wt[:, 120:] = 0
    for k in range(N + 1):
        r2[:, 4 * k:4 * k + 4, 4 * k:4 * k + 4] = 32
        wt[:, 120 + k // 4, :, 4 * k:4 * k + 4, k % 4] = 64
    k = N + 1
    wt[:, 120 + k // 4, :, :, k % 4] = -64
    if same:
        p = f(rng, 128, 4 * N)
        x = np.stack([cols(p, A[s]) for s in range(N)])
    else: x = f(rng, N, 128, 4 * T)
    x = np.array(x, np.float32).reshape(N, 128, T, 4)
    g = rt[0].astype(np.float32).reshape(128, 128, 4)
    for s in range(N): x[s] = x[s] + g[:, A[s]]
    x[:, 120:] = 0
    s, j = np.nonzero(B >= 0)
    b = B[s, j]
    x[s, 120 + b // 4, j, b % 4] = 64
    x[:, 120 + N // 4, :, N % 4] = LEVELS[V]
    if dead is not None: x[:, 120 + k // 4, :, k % 4] = np.where(dead, 256, 0)
    d["x"] = np.array(mx_ref.flush(x.reshape(N, 128, 4 * T).astype(BF)))
    return d
def choose(rng, A):
    B, V = (A + 1 + rng.integers(0, N - 1, A.shape)) % N, np.zeros((N, T), int)
    for a in range(N):
        k = taken(A, a)
        V.flat[k] = 3
        k = rng.permutation(k)[:DF]
        V.flat[k] = 0
        B.flat[k] = np.resize(rng.permutation([b for b in range(N) if b != a]), len(k))
    return B, V
def setup_inputs(rng):
    return plain(rng)
def setup_inputs_crowd(rng):
    h, A = int(rng.integers(1, N - 1)), []
    o = (int(rng.choice([i for i in range(1, N) if i not in (h, h + 1)])), h)
    for s in range(N):
        one, two, e = (s + o[0]) % N, (s + o[1]) % N, int(rng.integers(1, 9))
        rest = [a for a in range(N) if a not in (one, two, (two + 1) % N)]
        A.append(rng.permutation(np.concatenate([np.full(CAPP, one), np.full(CAPP + e, two), np.resize(rng.permutation(rest), T - 2 * CAPP - e)])))
    A = np.stack(A)
    B, V = choose(rng, A)
    for a in range(N):
        one, two, e = (a + o[0]) % N, (a + o[1]) % N, int(rng.integers(1, CB // 4 + 1))
        rest = [b for b in range(N) if b not in (a, one, two)]
        k = taken(A, a)
        k = rng.permutation(k[V.reshape(-1)[k] == 0])
        B.flat[k] = np.concatenate([np.full(CB, one), np.full(CB + e, two), np.resize(rng.permutation(rest), len(k) - 2 * CB - e)])
    return planned(rng, A, B, V)
def setup_inputs_few(rng):
    none, less, even, full = rng.permutation(N)[:4]
    act, n = [a for a in range(N) if a not in (none, less, even, full)] or [full], DF // (2 * N)
    fix = np.concatenate([np.full(n, less), np.full(2 * n, even), np.full(CAPP + 4, full)])
    A = np.stack([rng.permutation(np.concatenate([fix, np.resize(rng.permutation(act), T - len(fix))])) for s in range(N)])
    B, V = choose(rng, A)
    m = (A == less) | (A == even)
    V[m] = rng.integers(0, 4, int(np.count_nonzero(m)))
    k = taken(A, full)
    V.flat[k] = 3
    k = np.concatenate([k[-16::5], rng.permutation(k[:-16])[:DF - 4]])
    V.flat[k] = 0
    B.flat[k] = np.resize(rng.permutation([b for b in range(N) if b != full]), DF)
    d = planned(rng, A, B, V)
    p, t = 120 + (N + 2) // 4, (N + 2) % 4
    d["x"][:, p, t::4] = 64
    d["w"].reshape(N, 128, 4, 128, 4)[:, p, :, 4 * N + 4:4 * N + 8, t] = 64
    d["r2"][:, 4 * N + 4:4 * N + 8] = 0
    d["r2"][:, 4 * N + 4:4 * N + 8, :4 * N] = -64
    d["x"] = (d["x"].astype(np.float32) * np.float32(2.0 ** 21)).astype(BF)
    d["r2"] = (d["r2"].astype(np.float32) * np.float32(2.0 ** 24)).astype(BF)
    return d
def setup_inputs_ties(rng):
    lo, hi = np.sort(rng.permutation(N)[:2])
    k = int(rng.choice([i for i in range(N - 1) if i != hi]))
    act = [a for a in range(N) if a != hi]
    A = np.stack([rng.permutation(np.resize(rng.permutation(act), T)) for s in range(N)])
    B, V, c = np.zeros((N, T), int), np.full((N, T), 3), 3 * (DF // 6)
    for a in act:
        g = rng.permutation(taken(A, a))
        n = (len(g) - 2 * c) // 3
        B.flat[g] = (a + 1) % N
        V.flat[g[:c]] = 0
        B.flat[g[c:2 * c]] = (a + 2) % N
        V.flat[g[c:2 * c]] = 1
        B.flat[g[2 * c:2 * c + 3 * n]] = (a + 3 + np.repeat(np.arange(n), 3) % (N - 3)) % N
        V.flat[g[2 * c:2 * c + 3 * n]] = 2
    d = planned(rng, A, B, V, same=True)
    d["rt"][:, :, 4 * hi:4 * hi + 4] = d["rt"][:, :, 4 * lo:4 * lo + 4]
    d["r2"][:, 4 * k + 4:4 * k + 8, 4 * k:4 * k + 4] = 32
    d["r2"][:, :, 4 * k + 4:4 * k + 8] = d["r2"][:, :, 4 * k:4 * k + 4]
    return d
def setup_inputs_zero(rng):
    A = np.stack([rng.permutation(np.resize(np.arange(N), T)) for s in range(N)])
    B, V, dead = (A + 1 + rng.integers(0, N - 1, A.shape)) % N, np.full((N, T), 3), np.zeros((N, T), bool)
    for a in range(N):
        k = rng.permutation(taken(A, a))
        z = DF // 2 if a % 2 else DF + DF // 8
        dead.flat[k[:z]] = True
        B.flat[k[:z]] = -1
        V.flat[k[:z]] = 0
        g = k[z:DF]
        if len(g):
            V.flat[g] = 1
            B.flat[g] = np.resize(rng.permutation([b for b in range(N) if b != a]), len(g))
        if a == 0: blank = k[:z:2]
    d = planned(rng, A, B, V, dead=dead)
    nil = np.where(d["rt"][0, :, :4].astype(np.float32) < 0, np.float32(0.0), np.float32(-0.0)).astype(BF)
    for i in blank: d["x"][i // T, :, 4 * (i % T):4 * (i % T) + 4] = nil
    return d
def setup_inputs_spread(rng):
    return {**plain(rng), "x": wide(rng, N, 128, 4 * T, cols=4)}
def check_inputs(d):
    b = []
    for k in ("x", "rt", "w", "r2", "vx", "vh"):
        v = np.abs(d[k].astype(np.float32))
        if not (np.isfinite(v).all() and ((v == 0) | (v >= 2.0 ** -30) & (v <= 2.0 ** 30)).all()): b.append("a value of " + k)
    for k, n in (("rt", N), ("r2", N + 1)):
        v = d[k].astype(np.float32)
        if (v[:, :, 4 * n:] != 0).any(): b.append(k + " has numbers behind its first columns")
        if (v != v[:1]).any(): b.append(k + " differs between ranks")
    return b
def reference(x, rt, w, r2, vx, vh):
    q = [mx_ref.quantize(np.ascontiguousarray(x[s])) for s in range(N)]
    every = join(*q)
    first = np.stack([np.argmax(mx_ref.matmul(mx_ref.quantize(np.ascontiguousarray(rt[s])), q[s])[:N] + np.float32(0.0), axis=0) for s in range(N)])
    who, at, made = np.full((N, N * CB), -1), np.full((N, N * CB), -1), []
    for a in range(N):
        k = taken(first, a)
        t = pick(every, np.concatenate([k, np.full(N * CAPP - len(k), -1)]))
        z = [mx_ref.matmul(mx_ref.quantize(np.ascontiguousarray(cut(w[a], i))), t) for i in range(4)]
        h = mx_ref.quantize(np.ascontiguousarray(tile([np.maximum(v, np.float32(0.0)) * np.float32(0.0625) for v in z])))
        made.append(h)
        e = mx_ref.matmul(mx_ref.quantize(np.ascontiguousarray(r2[a])), h)[:N + 1, :len(k)] + np.float32(0.0)
        late = np.sort(np.argsort(e[N], kind="stable")[:DF])
        e[a] = -np.inf
        second = np.argmax(e[:N], axis=0)
        for b in range(N):
            m = late[second[late] == b][:CB]
            who[b, a * CB:a * CB + len(m)] = k[m]
            at[b, a * CB:a * CB + len(m)] = a * N * CAPP + m
    made = join(*made)
    y, oc, osc = np.zeros((N, 128, N * CB), np.float32), np.zeros((N, 128, 4 * N * CB), np.uint8), np.zeros((N, 16, N * CB), np.uint8)
    for b in range(N):
        t, h = pick(every, who[b]), pick(made, at[b])
        v = mx_ref.matmul(mx_ref.quantize(np.ascontiguousarray(vx[b])), t) + mx_ref.matmul(mx_ref.quantize(np.ascontiguousarray(vh[b])), h)
        y[b] = np.where(who[b] >= 0, v, np.float32(0.0))
        oc[b], osc[b] = emit(h)
    return {"y": y, "who": who.astype(np.float32).reshape(N, 1, N * CB), "oc": oc, "osc": osc}

@@ -1,0 +1,512 @@
+from concourse.bass import DstId, RemoteDMATransfer
+from concourse.mybir import dt, AluOpType, AxisListType, ActivationFunctionType
+
+F8, U8, U16, BF, F32, I32 = "float8_e4m3fn_x4", "uint8", "uint16", "bfloat16", "float32", "int32"
+DF, NR = 64, 8
+NS1, NS2 = 5, 3
+BIG = 1.0e29
+XH_H = 384
+
+
+def _sb(w, d):
+    return ("sbuf", [128, w], d)
+
+
+SCRATCH = {
+    "xt": _sb(512, BF), "rte": _sb(512, BF), "wt": _sb(2048, BF), "r2m": _sb(512, BF), "r2r": _sb(512, BF),
+    "vxt": _sb(512, BF), "vht": _sb(512, BF), "zt": _sb(512, BF), "ht": _sb(1024, BF),
+    "xq": _sb(256, F8), "xs": _sb(256, U8), "rq": _sb(128, F8), "rs": _sb(128, U8), "wq": _sb(512, F8), "ws": _sb(512, U8),
+    "mq": _sb(128, F8), "ms": _sb(128, U8), "eq": _sb(128, F8), "es": _sb(128, U8),
+    "vxq": _sb(128, F8), "vxs": _sb(128, U8), "vhq": _sb(128, F8), "vhs": _sb(128, U8),
+    "s1c": _sb(256, F8), "s1s": _sb(256, U8), "r1c": _sb(128, F8), "r1s": _sb(128, U8), "xh": _sb(768, F8), "xhs": _sb(768, U8),
+    "s2c": _sb(256, F8), "s2s": _sb(256, U8), "r2c": _sb(128, F8), "r2s": _sb(128, U8), "l2c": _sb(272, F8), "l2s": _sb(272, U8),
+    "hp": _sb(128, F8), "hps": _sb(128, U8),
+    "nld": ("dram", [128, 2], BF), "rl1": ("dram", [128, 2], BF), "lnd": ("dram", [8, 128, 2], BF),
+    "wgd": ("dram", [128, 1], F32), "rl2": ("dram", [128, 1], F32), "lwd": ("dram", [8, 128, 1], F32),
+    "p2": _sb(2, I32), "ia": _sb(16, I32), "cf": _sb(16, F32), "of1": _sb(2, U16), "of2": _sb(2, U16), "ofh": _sb(8, U16),
+    "vr": _sb(8, F32), "th1": _sb(8, F32), "th2": _sb(4, F32), "ones": _sb(128, BF), "fix": _sb(128, BF), "zrow": _sb(256, BF),
+    "d0r": _sb(128, F32), "d0": _sb(128, F32), "xa": _sb(32, F32), "xb": _sb(32, F32),
+    "mk1": _sb(32, F32), "mk1b": _sb(32, F32), "mk1a": _sb(32, F32), "mk2": _sb(32, F32),
+    "c127": _sb(128, BF), "tri": _sb(128, BF), "s128": _sb(256, F32), "oh32": _sb(8, F32),
+    "t1": _sb(128, F32), "rm": _sb(128, F32), "zb": _sb(144, BF), "oh": _sb(128, BF), "mr": _sb(128, BF), "cum": _sb(128, BF),
+    "js": _sb(1280, BF), "jv": _sb(1024, BF), "l1": _sb(8, F32), "lx1": _sb(32, F32), "lt1": _sb(32, F32), "mn1": _sb(16, F32),
+    "off1": _sb(16, U16), "nlp": _sb(32, BF), "nlt": _sb(32, BF),
+    "nrow": _sb(256, BF), "num": _sb(256, BF), "tv": _sb(512, BF), "inv": _sb(256, BF), "b2v": _sb(256, BF),
+    "wn": _sb(272, F32), "col": _sb(32, F32), "cc": _sb(512, F32), "lt": _sb(512, BF),
+    "rr": _sb(16, F32), "tvv": _sb(64, BF), "tvt": _sb(64, BF), "rowv": _sb(256, BF), "m2": _sb(256, BF), "cum2": _sb(256, BF),
+    "l2": _sb(8, F32), "l2v": _sb(1, F32), "lx2": _sb(32, F32), "lt2": _sb(32, F32), "mn2": _sb(16, F32),
+    "off2": _sb(16, U16), "offw": _sb(16, U16), "wg": _sb(256, F32), "wgp": _sb(128, F32),
+    "ys": _sb(128, F32),
+    "pw": ("psum", [128, 2048], F32), "pe": ("psum", [128, 1536], F32), "pz": ("psum", [128, 512], F32),
+}
+NDMA = 34
+SEMAPHORES = (["kv", "ks", "kt", "kp", "sent"] + [k + n for k in ("c", "s", "n", "rc", "rs", "rn") for n in "12"]
+              + ["d%d" % i for i in range(NDMA)])
+
+
+def split(engines, parts):
+    k = 1
+    while 2 * k * parts <= len(engines):
+        k *= 2
+    return [engines[k * i:k * i + k] for i in range(parts)]
+
+
+def plan(src, cores, topo):
+    direct = [d for d in cores if d != src and topo.may_write(src, d)]
+    cross = [d for d in cores if d != src and not topo.may_write(src, d)]
+    can = [c for c in topo.cores_of(src) if c != src and all(topo.may_write(c, d) for d in cross)]
+    can.sort(key=lambda c: (topo.die(c) == topo.die(src), c))
+    half = len(cores) // 2
+    helpers = {can[h]: (h, [d for d in cross if cores.index(d) // half == h]) for h in range(2)}
+    eng = {}
+    off = topo.engines(src, direct[0])
+    two, four = split(off, 4), split(off, 2)
+    for i, d in enumerate(direct):
+        eng["c1", d] = eng["c2", d] = two[i]
+        eng["s1", d] = eng["s2", d] = two[3] if i == 0 else four[i - 1]
+        eng["n1", d] = eng["n2", d] = off[i:i + 1]
+    for h in helpers:
+        k, serve = helpers[h]
+        on = topo.engines(src, h)
+        up = [e for e in on if e not in off]
+        eng["c1", h] = split(up, 2)[k]
+        eng["s1", h] = split(off, 2)[k]
+        eng["c2", h] = split(on, 2)[k]
+        eng["s2", h] = split(up, 2)[k]
+        eng["n1", h] = eng["n2", h] = up[k:k + 1]
+        for i, d in enumerate(serve):
+            out = topo.engines(h, d)
+            quarter = split(out, 2 * len(serve))
+            eng["c1", h, d], eng["s1", h, d] = quarter[i], quarter[len(serve) + i]
+            eng["c2", h, d] = eng["s2", h, d] = split(out, len(serve))[i]
+            eng["n1", h, d] = eng["n2", h, d] = quarter[len(serve) + i][:1]
+    return {"direct": direct, "helpers": helpers, "eng": eng}
+
+
+def bits(engines):
+    v = 0
+    for e in engines:
+        v |= 1 << e
+    return v
+
+
+def arrivals(kind, core, cores, topo):
+    n = 0
+    for s in cores:
+        if s != core:
+            p = plan(s, cores, topo)
+            if core in p["direct"]:
+                n += len(p["eng"][kind, core])
+            for h in p["helpers"]:
+                if core in p["helpers"][h][1]:
+                    n += len(p["eng"][kind, h, core])
+    return n
+
+
+def transfer(core, to, engines, sem, src, dst, topo):
+    rid, pid = topo.addr(to, core)
+    return RemoteDMATransfer(dst_ids=[DstId(rid=rid, pnc=pid)], dma_engine_mask=bits(engines), remote_sem=sem, src=src, dst=dst)
+
+
+def helper_program(g, core, T, topo):
+    home = [c for c in T.cores if c in topo.cores_of(core)]
+    if not home:
+        return
+    src = home[0]
+    p = plan(src, T.cores, topo)
+    if core not in p["helpers"]:
+        return
+    half, serve = p["helpers"][core]
+    s, sent = T.rank_of(src), 0
+
+    def columns(t, b):
+        return t[:, 32 * b:32 * b + 32]
+
+    for kind in ("c1", "n1", "s1", "c2", "s2", "n2"):
+        g.wait_ge(T.sem["r" + kind], len(p["eng"][kind, core]))
+        tr = []
+        for d in serve:
+            k = T.rank_of(d) % 4
+            if kind[1] == "2" and s == 0 and T.rank_of(d) == 1:
+                k = 0
+            if kind[0] == "n":
+                a, b = (T.rl1[:], T.lnd[s]) if kind == "n1" else (T.rl2[:], T.lwd[s])
+            elif kind[0] == "s":
+                a, b = (columns(T.r1s, k), columns(T.xhs, s)) if kind == "s1" else (columns(T.r2s, k), columns(T.l2s, s))
+            else:
+                a, b = (columns(T.r1c, k), columns(T.xh, s)) if kind == "c1" else (columns(T.r2c, k), columns(T.l2c, s))
+                a, b = a.bitcast(dt.uint8), b.bitcast(dt.uint8)
+            tr.append(transfer(core, d, p["eng"][kind, core, d], T.sem[kind], a, b, topo))
+            sent += len(p["eng"][kind, core, d])
+        g.remote_dma_fused(tr, local_sem=T.sem.sent)
+    g.wait_ge(T.sem.sent, sent)
+
+
+def rank_program(g, core, T, topo):
+    me = T.rank_of(core)
+    if me is None:
+        helper_program(g, core, T, topo)
+        return
+    A, AF = AluOpType, ActivationFunctionType
+    eng = {"v": g.vector, "s": g.scalar, "t": g.tensor, "p": g, "y": g.sync}
+    cnt = {q: 0 for q in eng}
+    seen = {q: {} for q in eng}
+    ndma = [0]
+    everything = {}
+
+    def wait(q, deps):
+        need, todo = {}, list(deps)
+        for d in todo:
+            if isinstance(d, list):
+                todo.extend(d)
+            else:
+                need[d[0]] = max(need.get(d[0], 0), d[1])
+        for sem in need:
+            if seen[q].get(sem, 0) < need[sem]:
+                eng[q].wait_ge(T.sem[sem], need[sem])
+                seen[q][sem] = need[sem]
+
+    def done(q, inst):
+        cnt[q] += 1
+        inst.then_inc(T.sem["k" + q], 1)
+        everything["k" + q] = cnt[q]
+        return ("k" + q, cnt[q])
+
+    def dma(q, out, in_, *deps):
+        wait(q, deps)
+        sem = "d%d" % ndma[0]
+        ndma[0] += 1
+        eng[q].dma_start(out, in_).then_inc(T.sem[sem], 16)
+        everything[sem] = 16
+        return (sem, 16)
+
+    def ts(out, in0, s1, op0, s2, op1, *deps):
+        wait("v", deps)
+        if op1 is None:
+            return done("v", g.vector.tensor_scalar(out, in0, s1, None, op0))
+        return done("v", g.vector.tensor_scalar(out, in0, s1, s2, op0, op1))
+
+    def tt(out, a, b, op, *deps):
+        wait("v", deps)
+        return done("v", g.vector.tensor_tensor(out, a, b, op))
+
+    def copy(out, in_, *deps):
+        wait("v", deps)
+        return done("v", g.vector.tensor_copy(out, in_))
+
+    def fill(ap, c, *deps):
+        wait("v", deps)
+        return done("v", g.vector.memset(ap, c))
+
+    def scan(out, a, b, init, op0, op1, *deps):
+        wait("v", deps)
+        return done("v", g.vector.tensor_tensor_scan(out, a, b, init, op0, op1))
+
+    def turn(out, in_, *deps):
+        wait("v", deps)
+        return done("v", g.vector.transpose(out, in_))
+
+    def total(out, in_, *deps):
+        wait("v", deps)
+        return done("v", g.vector.tensor_reduce(out, in_, AxisListType.X, A.add))
+
+    def quant(q, s, in_, *deps):
+        wait("v", deps)
+        return done("v", g.vector.quantize_mx(q, s, in_))
+
+    def act(out, in_, func, *deps, **kw):
+        wait("s", deps)
+        return done("s", g.scalar.activation(out, in_, func, **kw))
+
+    def mm(out, l, ls, r, rs, start, stop, *deps):
+        wait("t", deps)
+        return done("t", g.tensor.matmul_mx(out, l, ls, r, rs, start, stop))
+
+    def iota(out, pattern, base, cm):
+        return done("p", g.iota(out, pattern, base, cm, allow_small_or_imprecise_dtypes=True))
+
+    ld_x = dma("y", T.xt[:], T.x[:])
+    ld_r = dma("s", T.rte[:, 0:32], T.rt[:, 0:32])
+    ld_w = dma("y", T.wt[:], T.w[:], ld_x)
+    ld_2 = []
+    if me:
+        ld_2.append(dma("y", T.r2m[:, 0:4 * me], T.r2[:, 0:4 * me]))
+        ld_2.append(dma("y", T.r2m[:, 4 * me:4 * me + 4], T.r2[:, 4 * me - 4:4 * me]))
+        ld_2.append(dma("y", T.r2m[:, 4 * me + 4:36], T.r2[:, 4 * me + 4:36]))
+    else:
+        ld_2.append(dma("y", T.r2m[:, 0:4], T.r2[:, 4:8]))
+        ld_2.append(dma("y", T.r2m[:, 4:36], T.r2[:, 4:36]))
+    ld_e = dma("y", T.r2r[:, 0:4], T.r2[:, 32:36])
+    ld_vx = dma("y", T.vxt[:], T.vx[:])
+    ld_vh = dma("y", T.vht[:], T.vh[:])
+    place = {b: (b if me or b != 1 else 0) for b in range(NR)}
+
+    k_p2 = done("p", g.iota(T.p2[:], [[0, 2]], 0, 1))
+    k_xa = iota(T.xa[:], [[0, 2], [1, 2], [0, 8]], 0, 0)
+    k_xb = iota(T.xb[:], [[0, 4], [1, 8]], 0, 0)
+    k_vr = iota(T.vr[:], [[1, 8]], 0, 0)
+    k_d0r = iota(T.d0r[:], [[0, 16], [1, 8]], 0, 0)
+    k_zt = fill(T.zt[:], 0.0)
+    k_ones = fill(T.ones[:], 1.0)
+    k_zb = fill(T.zb[:], 0.0)
+    k_nlp = fill(T.nlp[:, 16:32], 0.0)
+
+    def bitsof(i, shift, mask):
+        d = T.ia[:, 2 * i:2 * i + 2]
+        wait("v", [k_p2])
+        if shift:
+            return done("v", g.vector.tensor_scalar(d, T.p2[:], shift, mask, A.arith_shift_right, A.bitwise_and))
+        return done("v", g.vector.tensor_scalar(d, T.p2[:], mask, None, A.bitwise_and))
+
+    cf = {n: T.cf[:, i:i + 1] for i, n in enumerate(("a7", "u", "uh", "ul", "q", "t", "t1", "fx", "t2", "b2", "p0", "h", "hq", "hq2"))}
+    ka, kuh, kul = bitsof(0, 0, 7), bitsof(2, 4, 1), bitsof(3, 3, 1)
+    k_of1 = copy(T.of1[:], T.ia[:, 0:2], ka)
+    c_a7 = copy(cf["a7"], T.ia[:, 0:1], ka)
+    c_uh = copy(cf["uh"], T.ia[:, 4:5], kuh)
+    c_ul = copy(cf["ul"], T.ia[:, 6:7], kul)
+    c_fx = ts(cf["fx"], cf["a7"], 0.0, A.is_equal, None, None, c_a7)
+    c_t = ts(cf["t"], cf["ul"], 16.0, A.mult, 0.5, A.add, c_ul)
+    k_mk1a = ts(T.mk1a[:], T.xa[:], cf["uh"], A.not_equal, 2000.0, A.mult, k_xa, c_uh)
+    k_mk1b = ts(T.mk1b[:], T.xb[:], NS1 - 0.5, A.is_lt, 128.0, A.mult, k_xb)
+    c_t1 = ts(cf["t1"], cf["uh"], 8.0, A.mult, cf["t"], A.add, c_t)
+    k_fix = ts(T.fix[:], T.ones[:], cf["fx"], A.mult, None, None, k_ones, c_fx)
+    k_th1 = ts(T.th1[:], T.vr[:], cf["t1"], A.add, None, None, k_vr, c_t1)
+    k_d0 = ts(T.d0[:], T.d0r[:], 0.0, A.is_equal, -BIG, A.mult, k_d0r)
+
+    t = ld_r
+    for w in (32, 64, 128, 256):
+        t = copy(T.rte[:, w:2 * w], T.rte[:, 0:w], t)
+    q_r = quant(T.rq[:], T.rs[:], T.rte[:], t)
+    q_x = quant(T.xq[:, 0:128], T.xs[:, 0:128], T.xt[:], ld_x)
+    m_g = mm(T.pw[:, 0:128], T.rq[:], T.rs[:], T.xq[:, 0:128], T.xs[:, 0:128], True, True, q_x)
+    k_zero1 = quant(T.xq[:, 128:256], T.xs[:, 128:256], T.zt[:], k_zt)
+    k_mk1 = tt(T.mk1[:], T.mk1a[:], T.mk1b[:], A.add, k_mk1b)
+    v_t1 = turn(T.t1[:], T.pw[:, 0:128], m_g)
+    v_rm = scan(T.rm[:], T.d0[:], T.t1[:], 0.0, A.add, A.max, v_t1, k_d0)
+    for k in range(4):
+        v_z = ts(T.zb[:, 1 + 32 * k:33 + 32 * k], T.rm[:, 32 * k:32 * k + 32], T.rm[:, 32 * k + 7:32 * k + 8], A.is_lt, None, None, v_rm, k_zb)
+    v_oh = tt(T.oh[:], T.zb[:, 0:128], T.zb[:, 1:129], A.subtract, v_z)
+    v_m = turn(T.mr[:], T.oh[:], v_oh)
+    v_c = scan(T.cum[:], T.fix[:], T.mr[:], 0.0, A.add, A.add, v_m, k_fix)
+    acc, part = [], {}
+    for v in range(NS1):
+        acc.append(act(T.js[:, 128 * v:128 * v + 128], T.cum[:], AF.Sign, v_c, k_th1, scale=-1.0, bias=T.th1[:, v:v + 1], accum_out=T.l1[:, v:v + 1]))
+    for v in range(NS1, 8):
+        part[v] = ts(T.jv[:, 128 * v:128 * v + 128], T.cum[:], T.th1[:, v:v + 1], A.is_le, 2.0, A.mult, v_c, k_th1)
+    for v in range(NS1, 8):
+        acc.append(total(T.l1[:, v:v + 1], T.jv[:, 128 * v:128 * v + 128], part[v]))
+    v_lx = tt(T.lx1[:], T.l1[:, 0:8].indirect(T.of1[:, 0:2]), T.mk1[:], A.add, acc, k_mk1, k_of1)
+    v_lt = turn(T.lt1[:], T.lx1[:], v_lx)
+    v_mn = tt(T.mn1[:], T.lt1[:, 0:16], T.lt1[:, 16:32], A.min, v_lt)
+    v_o0 = ts(T.off1[:, 0:16:2], T.mn1[:, 0:8], 0.5, A.mult, None, None, v_mn)
+    v_o1 = ts(T.off1[:, 1:16:2], T.mn1[:, 8:16], 0.5, A.mult, None, None, v_mn)
+    v_s1 = copy(T.s1c[:].bitcast(dt.uint32), T.xq[:].bitcast(dt.uint32).indirect(T.off1[:]), v_o1, v_o0, q_x, k_zero1)
+    a_n0 = act(T.nlp[:, 0:16:2], T.mn1[:, 0:8], AF.Copy, v_mn, scale=0.5)
+    a_n1 = act(T.nlp[:, 1:16:2], T.mn1[:, 8:16], AF.Copy, v_mn, scale=0.5)
+    a_s1 = act(T.s1s[:], T.xs[:].indirect(T.off1[:]), AF.Copy, v_o1)
+    w0 = 32 * me
+    a_own = act(T.xhs[:, w0:w0 + 32], T.xs[:].indirect(T.off1[:, 2 * me:2 * me + 2]), AF.Copy)
+    v_nt = turn(T.nlt[:], T.nlp[:], a_n1, k_nlp)
+    d_nl = dma("y", T.nld[:], T.nlt[0:16, 0:16], v_nt)
+    d_own = dma("y", T.lnd[me], T.nlt[0:16, 0:16])
+    v_own = copy(T.xh[:, w0:w0 + 32].bitcast(dt.uint32), T.xq[:].bitcast(dt.uint32).indirect(T.off1[:, 2 * me:2 * me + 2]))
+
+    p = plan(core, T.cores, topo)
+    sent = [0]
+
+    def send(kind, tos, src_of, dst_of, *deps):
+        wait("p", deps)
+        tr = []
+        for to in tos:
+            e = p["eng"][kind, to]
+            tr.append(transfer(core, to, e, T.sem[kind if to in p["direct"] else "r" + kind], src_of(to), dst_of(to), topo))
+            sent[0] += len(e)
+        g.remote_dma_fused(tr, local_sem=T.sem.sent)
+
+    def send_stage(stage, codes, scales, land_c, land_s, relay_c, relay_s, pl, dep_c, dep_s, numbers, land_n, relay_n, dep_n):
+        def part_of(t, to):
+            if to in p["direct"]:
+                b = pl[T.rank_of(to)]
+                return t[:, 32 * b:32 * b + 32]
+            h = p["helpers"][to][0]
+            return t[:, 128 * h:128 * h + 128]
+
+        def c_src(to):
+            return part_of(codes, to).bitcast(dt.uint8)
+
+        def c_dst(to):
+            return (land_c[:, w0:w0 + 32] if to in p["direct"] else relay_c[:]).bitcast(dt.uint8)
+
+        def s_src(to):
+            return part_of(scales, to)
+
+        def s_dst(to):
+            return land_s[:, w0:w0 + 32] if to in p["direct"] else relay_s[:]
+
+        def n_dst(to):
+            return land_n if to in p["direct"] else relay_n
+
+        hs, ds = sorted(p["helpers"]), p["direct"]
+        send("c" + stage, hs, c_src, c_dst, dep_c)
+        send("s" + stage, hs, s_src, s_dst, dep_s)
+        send("c" + stage, ds, c_src, c_dst)
+        if stage == "1":
+            send("n" + stage, hs + ds, lambda to: numbers, n_dst, dep_n)
+        send("s" + stage, ds[:1], s_src, s_dst)
+        send("s" + stage, ds[1:], s_src, s_dst)
+        if stage == "2":
+            send("n" + stage, hs + ds, lambda to: numbers, n_dst, dep_n)
+
+    send_stage("1", T.s1c, T.s1s, T.xh, T.xhs, T.r1c, T.r1s, {b: b for b in range(NR)}, v_s1, a_s1, T.nld[:], T.lnd[me], T.rl1[:], d_nl)
+
+    q_w = quant(T.wq[:], T.ws[:], T.wt[:], ld_w)
+    k_127 = fill(T.c127[:], 127.5)
+    k_s128 = iota(T.s128[:], [[128, 8], [0, 32]], 0, 0)
+    k_oh32 = iota(T.oh32[:], [[32, 8]], 0, 0)
+    wait("p", [k_127])
+    k_tri = done("p", g.affine_select(T.tri[:], T.c127[:], [[-1, 128]], A.is_gt, -1.0, 0, 1))
+    z2 = quant(T.xh[:, 256:384], T.xhs[:, 256:384], T.zt[:])
+    z3 = quant(T.xh[:, 640:768], T.xhs[:, 640:768], T.zt[:])
+    k_tv0 = fill(T.tv[:, 128:256], 0.0)
+    ku, kq, k0, k1, k2 = bitsof(1, 3, 3), bitsof(4, 0, 15), bitsof(5, 0, 1), bitsof(6, 1, 1), bitsof(7, 2, 1)
+    c_u = copy(cf["u"], T.ia[:, 2:3], ku)
+    c_q = copy(cf["q"], T.ia[:, 8:9], kq)
+    c_p0 = copy(cf["p0"], T.ia[:, 10:11], k0)
+    c_h = ts(cf["h"], T.ia[:, 12:13], float(XH_H), A.mult, 128.0, A.add, k1)
+    k_b2 = ts(cf["b2"], cf["a7"], 2.0, A.mult, 8.0, A.add)
+    k_of2 = ts(T.of2[:], T.ia[:, 14:16], 2.0, A.mult, cf["p0"], A.add, k2, c_p0)
+    c_t2 = ts(cf["t2"], cf["u"], 4.0, A.mult, 0.5, A.add, c_u)
+    c_hq = ts(cf["hq"], cf["q"], 2.0, A.mult, 2.0, A.add, c_q)
+    k_mk2 = ts(T.mk2[:], T.xa[:], cf["ul"], A.not_equal, 2000.0, A.mult)
+    k_th2 = ts(T.th2[:], T.vr[:, 0:4], cf["t2"], A.add, None, None, c_t2)
+    c_hq2 = tt(cf["hq2"], cf["hq"], cf["p0"], A.subtract, c_hq)
+    k_ofh = ts(T.ofh[:], T.oh32[:], cf["hq2"], A.add, None, None, k_oh32, c_hq2)
+    f_m = fill(T.r2m[:, 64:512], 0.0)
+    f_m2 = fill(T.r2m[:, 36:64], 0.0, ld_2)
+    q_m = quant(T.mq[:], T.ms[:], T.r2m[:], f_m2)
+    t = ld_e
+    for w in (4, 8, 16, 32, 64, 128, 256):
+        t = copy(T.r2r[:, w:2 * w], T.r2r[:, 0:w], t)
+    q_e = quant(T.eq[:], T.es[:], T.r2r[:], t)
+    k_zrow = fill(T.zrow[:], 0.0)
+    k_tvv = fill(T.tvv[:], 0.0)
+    k_wn = fill(T.wn[:, 256:272], -1.0)
+    k_l2 = fill(T.l2[:, 4:8], 0.0)
+    q_vx = quant(T.vxq[:], T.vxs[:], T.vxt[:], ld_vx)
+    q_vh = quant(T.vhq[:], T.vhs[:], T.vht[:], ld_vh)
+    dz = [dma("y", T.l2c[:, w0:w0 + 32].bitcast(dt.uint8), T.xh[:, 256:288].bitcast(dt.uint8), z2),
+          dma("y", T.l2s[:, w0:w0 + 32], T.xhs[:, 256:288]),
+          dma("y", T.l2c[:, 256:272].bitcast(dt.uint8), T.xh[:, 256:272].bitcast(dt.uint8)),
+          dma("y", T.l2s[:, 256:272], T.xhs[:, 256:272])]
+
+    n_in = {k: arrivals(k, core, T.cores, topo) for k in ("c1", "s1", "n1", "c2", "s2", "n2")}
+    d_nr = dma("y", T.nrow[0:1, 0:256], T.lnd[:, 16 * me:16 * me + 16, :], ("n1", n_in["n1"]), d_own)
+    wait("p", [d_nr])
+    g_num = done("p", g.partition_broadcast(T.num[:], T.nrow[0:1, 0:256], 128))
+    ready = [("c1", n_in["c1"]), ("s1", n_in["s1"]), v_own, a_own]
+    mw = []
+    for i in range(4):
+        mw.append(mm(T.pw[:, 512 * i:512 * i + 256], T.wq[:, 128 * i:128 * i + 128], T.ws[:, 128 * i:128 * i + 128],
+                     T.xh[:, 0:256], T.xhs[:, 0:256], True, True, q_w, ready, v_t1))
+    col = {n: T.col[:, 2 * i:2 * i + 2] for i, n in enumerate(("e8", "n2", "fe", "sc", "corr", "cc", "A", "F", "F2", "nI"))}
+
+    def one(n, h):
+        return col[n][:, h:h + 1]
+
+    rel = []
+    for i in range(4):
+        o, ps = T.ht[:, i:1024:4], T.pw[:, 512 * i:512 * i + 256]
+        if i % 2 == 0:
+            rel.append(ts(o, ps, 0.0, A.max, 0.0625, A.mult, mw[i]))
+        else:
+            rel.append(act(o, ps, AF.Relu, mw[i], scale=0.0625))
+    q_h = quant(T.xh[:, XH_H:XH_H + 256], T.xhs[:, XH_H:XH_H + 256], T.ht[:], rel)
+    for h in range(2):
+        a = XH_H + 128 * h
+        m_e = mm(T.pe[:, 512 * h:512 * h + 128], T.xh[:, a:a + 128], T.xhs[:, a:a + 128], T.mq[:], T.ms[:], True, True, q_h, q_m)
+    m_row = mm(T.pe[:, 1024:1280], T.eq[:], T.es[:], T.xh[:, XH_H:XH_H + 256], T.xhs[:, XH_H:XH_H + 256], True, True, q_e)
+    v_ta = tt(T.tv[:, 0:128], T.num[:, 0:128], T.tri[:], A.is_lt, g_num, k_tri)
+    v_tb = tt(T.tv[:, 384:512], T.num[:, 128:256], T.tri[:], A.is_lt)
+    v_tc = ts(T.tv[:, 256:384], T.num[:, 0:128], 127.5, A.is_lt, None, None)
+    a_va = act(T.inv[:], T.num[:], AF.Sign, g_num, scale=-1.0, bias=127.5, accum_out=one("nI", 0))
+    key = T.pe[:, 8:1024:512]
+    f = 0.6 * 2.0 ** -23
+    v_fe = ts(col["fe"], key, f, A.mult, None, None, m_e)
+    v_n2 = ts(col["n2"], key, -f, A.mult, 1e-30, A.max)
+    v_e8 = copy(col["e8"], key)
+    v_sc = tt(col["sc"], col["fe"], col["n2"], A.max, v_n2)
+    ac = []
+    for h in range(2):
+        ac.append(act(T.cc[:, 256 * h:256 * h + 256], T.tv[:, 256 * h:256 * h + 256], AF.Identity, v_sc, v_tc, k_tv0,
+                      scale=one("sc", h), bias=one("e8", h)))
+    v_ni = ts(one("nI", 1), one("nI", 0), -0.5, A.mult, 128.0, A.add, a_va)
+    for h in range(2):
+        v_r = scan(T.rr[:, 8 * h:8 * h + 8], T.d0[:, 0:8], T.pe[:, 512 * h:512 * h + 8], 0.0, A.add, A.max)
+    v_co = ts(col["corr"], col["e8"], 0.0, A.is_gt, one("nI", 1), A.mult, v_ni)
+    v_cc = ts(col["cc"], col["corr"], DF - 0.5, A.add, None, None, v_co)
+    for h in range(2):
+        a_f = act(T.js[:, 768 + 8 * h:776 + 8 * h], T.rr[:, 8 * h:8 * h + 8], AF.Sign, v_r, scale=-1.0, bias=T.rr[:, 8 * h + 7:8 * h + 8], accum_out=one("F", h))
+    vl = []
+    for h in range(2):
+        vl.append(tt(T.lt[:, 256 * h:256 * h + 256], T.pe[:, 1024:1280], T.cc[:, 256 * h:256 * h + 256], A.is_lt, ac[h], m_row))
+    a_a = act(T.js[:, 1024:1280], T.lt[:, 0:256], AF.Copy, vl[0], accum_out=one("A", 0))
+    v_f2 = ts(col["F2"], col["F"], 2.0, A.mult, 8.0, A.add, a_f)
+    v_a1 = total(one("A", 1), T.lt[:, 256:512], vl[1])
+    v_v0 = ts(T.tvv[:, 0:1], one("A", 0), one("cc", 0), A.is_gt, one("F2", 0), A.add, a_a, v_cc, v_f2, k_tvv)
+    v_v1 = ts(T.tvv[:, 32:33], one("A", 1), one("cc", 1), A.is_gt, one("F2", 1), A.add, v_a1)
+    v_tv = turn(T.tvt[:], T.tvv[:], v_v0, v_v1)
+    wait("p", [v_tv])
+    b = [done("p", g.partition_broadcast(T.rowv[:, 64 * q:64 * q + 64], T.tvt[32 * q:32 * q + 1, 0:64], 128)) for q in range(4)]
+    v_b2 = ts(T.b2v[:], T.num[:], 127.5, A.is_lt, cf["b2"], A.mult, k_b2)
+    for q in range(4):
+        for h in range(2):
+            k = 128 * h + 32 * q
+            v_m2 = tt(T.m2[:, k:k + 32], T.rowv[:, 64 * q + 32 * h:64 * q + 32 * h + 32], T.b2v[:, k:k + 32], A.is_equal, b[q], v_b2)
+    v_c2 = scan(T.cum2[:], T.zrow[:], T.m2[:], 0.0, A.add, A.add, v_m2, k_zrow)
+    acc = []
+    for v in range(NS2):
+        acc.append(act(T.js[:, 256 * v:256 * v + 256], T.cum2[:], AF.Sign, v_c2, k_th2, scale=-1.0, bias=T.th2[:, v:v + 1], accum_out=T.l2[:, v:v + 1]))
+    v_p = ts(T.jv[:, 0:256], T.cum2[:], T.th2[:, NS2:NS2 + 1], A.is_le, 2.0, A.mult, v_c2, v_lx)
+    v_p = total(T.l2v[:], T.jv[:, 0:256], v_p)
+    v_p = ts(T.l2[:, NS2:NS2 + 1], T.l2v[:], -256.0, A.add, None, None, v_p)
+    v_lx = tt(T.lx2[:], T.l2[:, 0:8].indirect(T.of2[:, 0:2]), T.mk2[:], A.add, acc, v_p, k_mk2, k_of2, k_l2)
+    v_lt = turn(T.lt2[:], T.lx2[:], v_lx)
+    v_m0 = tt(T.mn2[:, 0:8], T.lt2[:, 0:8], T.lt2[:, 8:16], A.min, v_lt)
+    v_m1 = tt(T.mn2[:, 8:16], T.lt2[:, 16:24], T.lt2[:, 24:32], A.min)
+    v_o0 = ts(T.off2[:, 0:16:2], T.mn2[:, 0:8], 0.5, A.mult, cf["h"], A.add, v_m0, c_h)
+    v_o1 = ts(T.off2[:, 1:16:2], T.mn2[:, 8:16], 0.5, A.mult, cf["h"], A.add, v_m1)
+    v_s2 = copy(T.s2c[:].bitcast(dt.uint32), T.xh[:].bitcast(dt.uint32).indirect(T.off2[:]), v_o1, ready, q_h, z2, z3)
+    a_s2 = act(T.s2s[:], T.xhs[:].indirect(T.off2[:]), AF.Copy, v_o1, ready)
+    v_w0 = ts(T.offw[:, 0:16:2], T.mn2[:, 0:8], 0.5, A.mult, 128.0, A.add)
+    v_w1 = ts(T.offw[:, 1:16:2], T.mn2[:, 8:16], 0.5, A.mult, 128.0, A.add)
+    v_wn = tt(T.wn[:, 0:256], T.num[:], T.s128[:], A.add, k_s128)
+    v_wg = copy(T.wg[:], T.wn[:].indirect(T.offw[:]), v_wn, v_w1, k_wn)
+    v_g0 = copy(T.wgp[:, 0:128:2], T.wg[:, 0:256:4], v_wg)
+    v_g1 = copy(T.wgp[:, 1:128:2], T.wg[:, 1:256:4])
+    runs = [(0, 0, 128)] if me else [(0, 16, 16), (16, 0, 16), (32, 32, 96)]
+    d_wg, d_wo = [], []
+    for to, fr, n in runs:
+        d_wg.append(dma("y", T.wgd[to:to + n, 0], T.wgp[0:1, fr:fr + n], v_g1))
+        d_wo.append(dma("s", T.lwd[me, to:to + n, 0], T.wgp[0:1, fr:fr + n], v_g1))
+    send_stage("2", T.s2c, T.s2s, T.l2c, T.l2s, T.r2c, T.r2s, place, v_s2, a_s2, T.wgd[:], T.lwd[me], T.rl2[:], d_wg)
+
+    ready = [("c2", n_in["c2"]), ("s2", n_in["s2"]), dz]
+    out = (T.pz[:, 0:128], T.pw[:, 512:640])
+    my = []
+    for k in range(2):
+        a = 128 * k
+        mm(out[k], T.vxq[:], T.vxs[:], T.l2c[:, a:a + 128], T.l2s[:, a:a + 128], True, False, ready, q_vx, q_vh, rel)
+        my.append(mm(out[k], T.vhq[:], T.vhs[:], T.l2c[:, a + 2:a + 130], T.l2s[:, a + 2:a + 130], False, True))
+    a_hp = act(T.hps[:], T.l2s[:, 0:256].indirect(T.ofh[:]), AF.Copy, ready, k_ofh)
+    v_hp = copy(T.hp[:].bitcast(dt.uint32), T.l2c[:, 0:256].bitcast(dt.uint32).indirect(T.ofh[:]), ready, k_ofh)
+    for r in range(2):
+        v_y = copy(T.ys[:, r:64:2], T.pz[:, r:128:4], my[0])
+        a_y = act(T.ys[:, 64 + r:128:2], T.pw[:, 512 + r:640:4], AF.Copy, my[1])
+    dma("y", T.oc[:, 0:512], T.hp[:].bitcast(dt.uint8), v_hp)
+    for k in range(4):
+        dma("y", T.osc[4 * k:4 * k + 4, 0:128], T.hps[32 * k:32 * k + 4, 0:128], a_hp)
+    dma("y", T.y[:, 0:64], T.ys[:, 0:64], v_y)
+    dma("s", T.y[:, 64:128], T.ys[:, 64:128], a_y)
+    dma("s", T.who[0:1, 0:128], T.lwd[:, 16 * me:16 * me + 16, 0], ("n2", n_in["n2"]), d_wo)
+    g.wait_ge(T.sem.sent, sent[0])
+    wait("p", [(s, everything[s]) for s in everything])

@@ -31,15 +31,15 @@ SCRATCH = {
     "t1": _sb(128, F32), "rm": _sb(128, F32), "zb": _sb(144, BF), "oh": _sb(128, BF), "mr": _sb(128, BF), "cum": _sb(128, BF),
     "js": _sb(1280, BF), "jv": _sb(1024, BF), "l1": _sb(8, F32), "lx1": _sb(32, F32), "lt1": _sb(32, F32), "mn1": _sb(16, F32),
     "off1": _sb(16, U16), "nlp": _sb(32, BF), "nlt": _sb(32, BF),
-    "nrow": _sb(256, BF), "num": _sb(256, BF), "tv": _sb(512, BF), "inv": _sb(256, BF), "b2v": _sb(256, BF),
+    "nrow": _sb(256, BF), "num": _sb(256, BF), "ncol": _sb(8, BF), "tv": _sb(512, BF), "inv": _sb(256, BF), "sa": _sb(256, BF),
     "wn": _sb(272, F32), "col": _sb(32, F32), "cc": _sb(512, F32), "lt": _sb(512, BF),
-    "rr": _sb(16, F32), "tvv": _sb(64, BF), "tvt": _sb(64, BF), "rowv": _sb(256, BF), "m2": _sb(256, BF), "cum2": _sb(256, BF),
+    "rr": _sb(16, F32), "gw": _sb(64, F32), "tvv": _sb(64, BF), "tvt": _sb(64, BF), "m2": _sb(256, BF), "cum2": _sb(256, BF),
     "l2": _sb(8, F32), "l2v": _sb(1, F32), "lx2": _sb(32, F32), "lt2": _sb(32, F32), "mn2": _sb(16, F32),
     "off2": _sb(16, U16), "offw": _sb(16, U16), "wg": _sb(256, F32), "wgp": _sb(128, F32),
     "ys": _sb(128, F32),
     "pw": ("psum", [128, 2048], F32), "pe": ("psum", [128, 1536], F32), "pz": ("psum", [128, 512], F32),
 }
-NDMA = 34
+NDMA = 36
 SEMAPHORES = (["kv", "ks", "kt", "kp", "sent"] + [k + n for k in ("c", "s", "n", "rc", "rs", "rn") for n in "12"]
               + ["d%d" % i for i in range(NDMA)])
 
@@ -54,32 +54,34 @@ def split(engines, parts):
 def plan(src, cores, topo):
     direct = [d for d in cores if d != src and topo.may_write(src, d)]
     cross = [d for d in cores if d != src and not topo.may_write(src, d)]
-    can = [c for c in topo.cores_of(src) if c != src and all(topo.may_write(c, d) for d in cross)]
-    can.sort(key=lambda c: (topo.die(c) == topo.die(src), c))
+    others = sorted((c for c in topo.cores_of(src) if c != src), key=lambda c: (topo.die(c) == topo.die(src), c))
+    can = [c for c in others if all(topo.may_write(c, d) for d in cross)]
+    rest = [c for c in others if c not in can]
     half = len(cores) // 2
-    helpers = {can[h]: (h, [d for d in cross if cores.index(d) // half == h]) for h in range(2)}
-    eng = {}
+    eng, helpers = {}, {}
     off = topo.engines(src, direct[0])
-    two, four = split(off, 4), split(off, 2)
+    on = topo.engines(src, can[0])
+    up = [e for e in on if e not in off]
+    two = split(off, 4)
     for i, d in enumerate(direct):
         eng["c1", d] = eng["c2", d] = two[i]
-        eng["s1", d] = eng["s2", d] = two[3] if i == 0 else four[i - 1]
-        eng["n1", d] = eng["n2", d] = off[i:i + 1]
+        eng["n1", d] = eng["n2", d] = two[3]
+    for k in range(2):
+        far = [d for d in cross if cores.index(d) // half == k]
+        near = [d for d in direct if cores.index(d) // half == k]
+        a, b, c = can[k], can[2 + k], rest[k]
+        helpers[a], helpers[b], helpers[c] = ("c", k, far), ("s", k, far), ("s", k, near)
+        eng["c1", a], eng["c2", a] = split(up, 2)[k], split(on, 2)[k]
+        eng["n1", a] = eng["n2", a] = up[k:k + 1]
+        eng["s1", b] = eng["s2", b] = split(off, 2)[k]
+        eng["s1", c] = eng["s2", c] = split(up, 2)[k]
     for h in helpers:
-        k, serve = helpers[h]
-        on = topo.engines(src, h)
-        up = [e for e in on if e not in off]
-        eng["c1", h] = split(up, 2)[k]
-        eng["s1", h] = split(off, 2)[k]
-        eng["c2", h] = split(on, 2)[k]
-        eng["s2", h] = split(up, 2)[k]
-        eng["n1", h] = eng["n2", h] = up[k:k + 1]
+        what, k, serve = helpers[h]
         for i, d in enumerate(serve):
-            out = topo.engines(h, d)
-            quarter = split(out, 2 * len(serve))
-            eng["c1", h, d], eng["s1", h, d] = quarter[i], quarter[len(serve) + i]
-            eng["c2", h, d] = eng["s2", h, d] = split(out, len(serve))[i]
-            eng["n1", h, d] = eng["n2", h, d] = quarter[len(serve) + i][:1]
+            e = split(topo.engines(h, d), 2)[i]
+            eng[what + "1", h, d] = eng[what + "2", h, d] = e
+            if what == "c":
+                eng["n1", h, d] = eng["n2", h, d] = e[:1]
     return {"direct": direct, "helpers": helpers, "eng": eng}
 
 
@@ -95,11 +97,9 @@ def arrivals(kind, core, cores, topo):
     for s in cores:
         if s != core:
             p = plan(s, cores, topo)
-            if core in p["direct"]:
-                n += len(p["eng"][kind, core])
+            n += len(p["eng"].get((kind, core), []))
             for h in p["helpers"]:
-                if core in p["helpers"][h][1]:
-                    n += len(p["eng"][kind, h, core])
+                n += len(p["eng"].get((kind, h, core), []))
     return n
 
 
@@ -116,13 +116,13 @@ def helper_program(g, core, T, topo):
     p = plan(src, T.cores, topo)
     if core not in p["helpers"]:
         return
-    half, serve = p["helpers"][core]
+    what, half, serve = p["helpers"][core]
     s, sent = T.rank_of(src), 0
 
     def columns(t, b):
         return t[:, 32 * b:32 * b + 32]
 
-    for kind in ("c1", "n1", "s1", "c2", "s2", "n2"):
+    for kind in (("c1", "n1", "c2", "n2") if what == "c" else ("s1", "s2")):
         g.wait_ge(T.sem["r" + kind], len(p["eng"][kind, core]))
         tr = []
         for d in serve:
@@ -246,10 +246,15 @@ def rank_program(g, core, T, topo):
     k_xb = iota(T.xb[:], [[0, 4], [1, 8]], 0, 0)
     k_vr = iota(T.vr[:], [[1, 8]], 0, 0)
     k_d0r = iota(T.d0r[:], [[0, 16], [1, 8]], 0, 0)
+    k_s128 = iota(T.s128[:], [[128, 8], [0, 32]], 0, 0)
+    k_oh32 = iota(T.oh32[:], [[32, 8]], 0, 0)
     k_zt = fill(T.zt[:], 0.0)
     k_ones = fill(T.ones[:], 1.0)
     k_zb = fill(T.zb[:], 0.0)
     k_nlp = fill(T.nlp[:, 16:32], 0.0)
+    k_127 = fill(T.c127[:], 127.5)
+    wait("p", [k_127])
+    k_tri = done("p", g.affine_select(T.tri[:], T.c127[:], [[-1, 128]], A.is_gt, -1.0, 0, 1))
 
     def bitsof(i, shift, mask):
         d = T.ia[:, 2 * i:2 * i + 2]
@@ -258,7 +263,7 @@ def rank_program(g, core, T, topo):
             return done("v", g.vector.tensor_scalar(d, T.p2[:], shift, mask, A.arith_shift_right, A.bitwise_and))
         return done("v", g.vector.tensor_scalar(d, T.p2[:], mask, None, A.bitwise_and))
 
-    cf = {n: T.cf[:, i:i + 1] for i, n in enumerate(("a7", "u", "uh", "ul", "q", "t", "t1", "fx", "t2", "b2", "p0", "h", "hq", "hq2"))}
+    cf = {n: T.cf[:, i:i + 1] for i, n in enumerate(("a7", "u", "uh", "ul", "q", "t", "t1", "fx", "t2", "p0", "h", "hq", "hq2"))}
     ka, kuh, kul = bitsof(0, 0, 7), bitsof(2, 4, 1), bitsof(3, 3, 1)
     k_of1 = copy(T.of1[:], T.ia[:, 0:2], ka)
     c_a7 = copy(cf["a7"], T.ia[:, 0:1], ka)
@@ -266,21 +271,22 @@ def rank_program(g, core, T, topo):
     c_ul = copy(cf["ul"], T.ia[:, 6:7], kul)
     c_fx = ts(cf["fx"], cf["a7"], 0.0, A.is_equal, None, None, c_a7)
     c_t = ts(cf["t"], cf["ul"], 16.0, A.mult, 0.5, A.add, c_ul)
-    k_mk1a = ts(T.mk1a[:], T.xa[:], cf["uh"], A.not_equal, 2000.0, A.mult, k_xa, c_uh)
-    k_mk1b = ts(T.mk1b[:], T.xb[:], NS1 - 0.5, A.is_lt, 128.0, A.mult, k_xb)
-    c_t1 = ts(cf["t1"], cf["uh"], 8.0, A.mult, cf["t"], A.add, c_t)
+    c_t1 = ts(cf["t1"], cf["uh"], 8.0, A.mult, cf["t"], A.add, c_t, c_uh)
     k_fix = ts(T.fix[:], T.ones[:], cf["fx"], A.mult, None, None, k_ones, c_fx)
-    k_th1 = ts(T.th1[:], T.vr[:], cf["t1"], A.add, None, None, k_vr, c_t1)
-    k_d0 = ts(T.d0[:], T.d0r[:], 0.0, A.is_equal, -BIG, A.mult, k_d0r)
 
-    t = ld_r
-    for w in (32, 64, 128, 256):
-        t = copy(T.rte[:, w:2 * w], T.rte[:, 0:w], t)
+    t = copy(T.rte[:, 32:64], T.rte[:, 0:32], ld_r)
+    k_mk1a = ts(T.mk1a[:], T.xa[:], cf["uh"], A.not_equal, 2000.0, A.mult, k_xa, c_uh)
+    t = copy(T.rte[:, 64:128], T.rte[:, 0:64], t)
+    k_mk1b = ts(T.mk1b[:], T.xb[:], NS1 - 0.5, A.is_lt, 128.0, A.mult, k_xb)
+    t = copy(T.rte[:, 128:256], T.rte[:, 0:128], t)
+    k_th1 = ts(T.th1[:], T.vr[:], cf["t1"], A.add, None, None, k_vr, c_t1)
+    t = copy(T.rte[:, 256:512], T.rte[:, 0:256], t)
+    k_mk1 = tt(T.mk1[:], T.mk1a[:], T.mk1b[:], A.add, k_mk1b)
     q_r = quant(T.rq[:], T.rs[:], T.rte[:], t)
     q_x = quant(T.xq[:, 0:128], T.xs[:, 0:128], T.xt[:], ld_x)
     m_g = mm(T.pw[:, 0:128], T.rq[:], T.rs[:], T.xq[:, 0:128], T.xs[:, 0:128], True, True, q_x)
+    k_d0 = ts(T.d0[:], T.d0r[:], 0.0, A.is_equal, -BIG, A.mult, k_d0r)
     k_zero1 = quant(T.xq[:, 128:256], T.xs[:, 128:256], T.zt[:], k_zt)
-    k_mk1 = tt(T.mk1[:], T.mk1a[:], T.mk1b[:], A.add, k_mk1b)
     v_t1 = turn(T.t1[:], T.pw[:, 0:128], m_g)
     v_rm = scan(T.rm[:], T.d0[:], T.t1[:], 0.0, A.add, A.max, v_t1, k_d0)
     for k in range(4):
@@ -323,12 +329,12 @@ def rank_program(g, core, T, topo):
             sent[0] += len(e)
         g.remote_dma_fused(tr, local_sem=T.sem.sent)
 
-    def send_stage(stage, codes, scales, land_c, land_s, relay_c, relay_s, pl, dep_c, dep_s, numbers, land_n, relay_n, dep_n):
+    def send_stage(stage, codes, scales, land_c, relay_c, relay_s, pl, dep_c, dep_s, numbers, land_n, relay_n, dep_n):
         def part_of(t, to):
             if to in p["direct"]:
                 b = pl[T.rank_of(to)]
                 return t[:, 32 * b:32 * b + 32]
-            h = p["helpers"][to][0]
+            h = p["helpers"][to][1]
             return t[:, 128 * h:128 * h + 128]
 
         def c_src(to):
@@ -337,34 +343,25 @@ def rank_program(g, core, T, topo):
         def c_dst(to):
             return (land_c[:, w0:w0 + 32] if to in p["direct"] else relay_c[:]).bitcast(dt.uint8)
 
-        def s_src(to):
-            return part_of(scales, to)
-
-        def s_dst(to):
-            return land_s[:, w0:w0 + 32] if to in p["direct"] else relay_s[:]
-
-        def n_dst(to):
-            return land_n if to in p["direct"] else relay_n
-
-        hs, ds = sorted(p["helpers"]), p["direct"]
-        send("c" + stage, hs, c_src, c_dst, dep_c)
-        send("s" + stage, hs, s_src, s_dst, dep_s)
+        hc = [h for h in sorted(p["helpers"]) if p["helpers"][h][0] == "c"]
+        hs = [h for h in sorted(p["helpers"]) if p["helpers"][h][0] == "s"]
+        ds = p["direct"]
+        send("c" + stage, hc, c_src, c_dst, dep_c)
+        send("s" + stage, hs, lambda to: part_of(scales, to), lambda to: relay_s[:], dep_s)
         send("c" + stage, ds, c_src, c_dst)
-        if stage == "1":
-            send("n" + stage, hs + ds, lambda to: numbers, n_dst, dep_n)
-        send("s" + stage, ds[:1], s_src, s_dst)
-        send("s" + stage, ds[1:], s_src, s_dst)
-        if stage == "2":
-            send("n" + stage, hs + ds, lambda to: numbers, n_dst, dep_n)
+        wait("p", [dep_n])
+        kind = "n" + stage
+        tr = [transfer(core, h, p["eng"][kind, h], T.sem["r" + kind], numbers, relay_n, topo) for h in hc]
+        ids = [topo.addr(d, core) for d in ds]
+        e = p["eng"][kind, ds[0]]
+        tr.append(RemoteDMATransfer(dst_ids=[DstId(rid=r, pnc=c) for r, c in ids], dma_engine_mask=bits(e), remote_sem=T.sem[kind],
+                                    srcs=[numbers], dsts=[land_n for d in ds]))
+        sent[0] += len(e) + sum(len(p["eng"][kind, h]) for h in hc)
+        g.remote_dma_fused(tr, local_sem=T.sem.sent)
 
-    send_stage("1", T.s1c, T.s1s, T.xh, T.xhs, T.r1c, T.r1s, {b: b for b in range(NR)}, v_s1, a_s1, T.nld[:], T.lnd[me], T.rl1[:], d_nl)
+    send_stage("1", T.s1c, T.s1s, T.xh, T.r1c, T.r1s, {b: b for b in range(NR)}, v_s1, a_s1, T.nld[:], T.lnd[me], T.rl1[:], d_nl)
 
     q_w = quant(T.wq[:], T.ws[:], T.wt[:], ld_w)
-    k_127 = fill(T.c127[:], 127.5)
-    k_s128 = iota(T.s128[:], [[128, 8], [0, 32]], 0, 0)
-    k_oh32 = iota(T.oh32[:], [[32, 8]], 0, 0)
-    wait("p", [k_127])
-    k_tri = done("p", g.affine_select(T.tri[:], T.c127[:], [[-1, 128]], A.is_gt, -1.0, 0, 1))
     z2 = quant(T.xh[:, 256:384], T.xhs[:, 256:384], T.zt[:])
     z3 = quant(T.xh[:, 640:768], T.xhs[:, 640:768], T.zt[:])
     k_tv0 = fill(T.tv[:, 128:256], 0.0)
@@ -373,7 +370,6 @@ def rank_program(g, core, T, topo):
     c_q = copy(cf["q"], T.ia[:, 8:9], kq)
     c_p0 = copy(cf["p0"], T.ia[:, 10:11], k0)
     c_h = ts(cf["h"], T.ia[:, 12:13], float(XH_H), A.mult, 128.0, A.add, k1)
-    k_b2 = ts(cf["b2"], cf["a7"], 2.0, A.mult, 8.0, A.add)
     k_of2 = ts(T.of2[:], T.ia[:, 14:16], 2.0, A.mult, cf["p0"], A.add, k2, c_p0)
     c_t2 = ts(cf["t2"], cf["u"], 4.0, A.mult, 0.5, A.add, c_u)
     c_hq = ts(cf["hq"], cf["q"], 2.0, A.mult, 2.0, A.add, c_q)
@@ -389,7 +385,6 @@ def rank_program(g, core, T, topo):
         t = copy(T.r2r[:, w:2 * w], T.r2r[:, 0:w], t)
     q_e = quant(T.eq[:], T.es[:], T.r2r[:], t)
     k_zrow = fill(T.zrow[:], 0.0)
-    k_tvv = fill(T.tvv[:], 0.0)
     k_wn = fill(T.wn[:, 256:272], -1.0)
     k_l2 = fill(T.l2[:, 4:8], 0.0)
     q_vx = quant(T.vxq[:], T.vxs[:], T.vxt[:], ld_vx)
@@ -401,6 +396,7 @@ def rank_program(g, core, T, topo):
 
     n_in = {k: arrivals(k, core, T.cores, topo) for k in ("c1", "s1", "n1", "c2", "s2", "n2")}
     d_nr = dma("y", T.nrow[0:1, 0:256], T.lnd[:, 16 * me:16 * me + 16, :], ("n1", n_in["n1"]), d_own)
+    d_nc = [dma("y", T.ncol[:, h:h + 1], T.lnd[4 * h:4 * h + 4, 16 * me:16 * me + 16, :]) for h in range(2)]
     wait("p", [d_nr])
     g_num = done("p", g.partition_broadcast(T.num[:], T.nrow[0:1, 0:256], 128))
     ready = [("c1", n_in["c1"]), ("s1", n_in["s1"]), v_own, a_own]
@@ -408,7 +404,7 @@ def rank_program(g, core, T, topo):
     for i in range(4):
         mw.append(mm(T.pw[:, 512 * i:512 * i + 256], T.wq[:, 128 * i:128 * i + 128], T.ws[:, 128 * i:128 * i + 128],
                      T.xh[:, 0:256], T.xhs[:, 0:256], True, True, q_w, ready, v_t1))
-    col = {n: T.col[:, 2 * i:2 * i + 2] for i, n in enumerate(("e8", "n2", "fe", "sc", "corr", "cc", "A", "F", "F2", "nI"))}
+    col = {n: T.col[:, 2 * i:2 * i + 2] for i, n in enumerate(("e8", "n2", "fe", "sc", "corr", "cc", "A", "F", "b0", "b1", "nI"))}
 
     def one(n, h):
         return col[n][:, h:h + 1]
@@ -440,29 +436,31 @@ def rank_program(g, core, T, topo):
         ac.append(act(T.cc[:, 256 * h:256 * h + 256], T.tv[:, 256 * h:256 * h + 256], AF.Identity, v_sc, v_tc, k_tv0,
                       scale=one("sc", h), bias=one("e8", h)))
     v_ni = ts(one("nI", 1), one("nI", 0), -0.5, A.mult, 128.0, A.add, a_va)
+    v_b0 = ts(col["b0"], T.ncol[:, 0:2], 127.5, A.is_gt, -1000.0, A.mult, d_nc)
     for h in range(2):
         v_r = scan(T.rr[:, 8 * h:8 * h + 8], T.d0[:, 0:8], T.pe[:, 512 * h:512 * h + 8], 0.0, A.add, A.max)
     v_co = ts(col["corr"], col["e8"], 0.0, A.is_gt, one("nI", 1), A.mult, v_ni)
-    v_cc = ts(col["cc"], col["corr"], DF - 0.5, A.add, None, None, v_co)
     for h in range(2):
         a_f = act(T.js[:, 768 + 8 * h:776 + 8 * h], T.rr[:, 8 * h:8 * h + 8], AF.Sign, v_r, scale=-1.0, bias=T.rr[:, 8 * h + 7:8 * h + 8], accum_out=one("F", h))
-    vl = []
-    for h in range(2):
-        vl.append(tt(T.lt[:, 256 * h:256 * h + 256], T.pe[:, 1024:1280], T.cc[:, 256 * h:256 * h + 256], A.is_lt, ac[h], m_row))
+    vl = [tt(T.lt[:, 0:256], T.pe[:, 1024:1280], T.cc[:, 0:256], A.is_lt, ac[0], m_row)]
+    v_b1 = tt(col["b1"], col["corr"], col["b0"], A.add, v_co, v_b0)
+    vl.append(tt(T.lt[:, 256:512], T.pe[:, 1024:1280], T.cc[:, 256:512], A.is_lt, ac[1]))
     a_a = act(T.js[:, 1024:1280], T.lt[:, 0:256], AF.Copy, vl[0], accum_out=one("A", 0))
-    v_f2 = ts(col["F2"], col["F"], 2.0, A.mult, 8.0, A.add, a_f)
-    v_a1 = total(one("A", 1), T.lt[:, 256:512], vl[1])
-    v_v0 = ts(T.tvv[:, 0:1], one("A", 0), one("cc", 0), A.is_gt, one("F2", 0), A.add, a_a, v_cc, v_f2, k_tvv)
-    v_v1 = ts(T.tvv[:, 32:33], one("A", 1), one("cc", 1), A.is_gt, one("F2", 1), A.add, v_a1)
+    v_cc = ts(col["cc"], col["b1"], DF - 0.5, A.add, None, None, v_b1)
+    v_a1 = scan(T.sa[:], T.zrow[:], T.lt[:, 256:512], 0.0, A.add, A.add, vl[1], k_zrow)
+    for h in range(2):
+        v_gw = ts(T.gw[:, 32 * h:32 * h + 32], T.xb[:], one("F", h), A.is_equal, one("cc", h), A.mult, a_f, v_cc)
+    v_v1 = ts(T.tvv[:, 32:64], T.gw[:, 32:64], T.sa[:, 255:256], A.is_gt, None, None, v_gw, v_a1)
+    v_v0 = ts(T.tvv[:, 0:32], T.gw[:, 0:32], one("A", 0), A.is_gt, None, None, a_a)
     v_tv = turn(T.tvt[:], T.tvv[:], v_v0, v_v1)
-    wait("p", [v_tv])
-    b = [done("p", g.partition_broadcast(T.rowv[:, 64 * q:64 * q + 64], T.tvt[32 * q:32 * q + 1, 0:64], 128)) for q in range(4)]
-    v_b2 = ts(T.b2v[:], T.num[:], 127.5, A.is_lt, cf["b2"], A.mult, k_b2)
+    bc = []
     for q in range(4):
         for h in range(2):
-            k = 128 * h + 32 * q
-            v_m2 = tt(T.m2[:, k:k + 32], T.rowv[:, 64 * q + 32 * h:64 * q + 32 * h + 32], T.b2v[:, k:k + 32], A.is_equal, b[q], v_b2)
-    v_c2 = scan(T.cum2[:], T.zrow[:], T.m2[:], 0.0, A.add, A.add, v_m2, k_zrow)
+            o, i = T.m2[0:32, 128 * h + 32 * q:128 * h + 32 * q + 32], T.tvt[32 * q:32 * q + 32, 32 * h:32 * h + 32]
+            bc.append(copy(o, i, v_tv) if q < 2 else act(o, i, AF.Copy, v_tv))
+    v_c0 = scan(T.cum2[0:32, :], T.zrow[0:32, :], T.m2[0:32, :], 0.0, A.add, A.add, bc)
+    v_c2 = [act(T.cum2[64:96, :], T.cum2[0:32, :], AF.Copy, v_c0), copy(T.cum2[32:64, :], T.cum2[0:32, :], v_c0),
+            copy(T.cum2[96:128, :], T.cum2[0:32, :])]
     acc = []
     for v in range(NS2):
         acc.append(act(T.js[:, 256 * v:256 * v + 256], T.cum2[:], AF.Sign, v_c2, k_th2, scale=-1.0, bias=T.th2[:, v:v + 1], accum_out=T.l2[:, v:v + 1]))
@@ -488,7 +486,7 @@ def rank_program(g, core, T, topo):
     for to, fr, n in runs:
         d_wg.append(dma("y", T.wgd[to:to + n, 0], T.wgp[0:1, fr:fr + n], v_g1))
         d_wo.append(dma("s", T.lwd[me, to:to + n, 0], T.wgp[0:1, fr:fr + n], v_g1))
-    send_stage("2", T.s2c, T.s2s, T.l2c, T.l2s, T.r2c, T.r2s, place, v_s2, a_s2, T.wgd[:], T.lwd[me], T.rl2[:], d_wg)
+    send_stage("2", T.s2c, T.s2s, T.l2c, T.r2c, T.r2s, place, v_s2, a_s2, T.wgd[:], T.lwd[me], T.rl2[:], d_wg)
 
     ready = [("c2", n_in["c2"]), ("s2", n_in["s2"]), dz]
     out = (T.pz[:, 0:128], T.pw[:, 512:640])

@@ -3,9 +3,10 @@ from concourse.mybir import dt, AluOpType, AxisListType, ActivationFunctionType
 
 F8, U8, U16, BF, F32, I32 = "float8_e4m3fn_x4", "uint8", "uint16", "bfloat16", "float32", "int32"
 DF, NR = 64, 8
-NS1, NS2 = 5, 3
 BIG = 1.0e29
+XW = 138
 XH_H = 384
+SEG = 144
 
 
 def _sb(w, d):
@@ -13,35 +14,34 @@ def _sb(w, d):
 
 
 SCRATCH = {
-    "xt": _sb(512, BF), "rte": _sb(512, BF), "wt": _sb(2048, BF), "r2m": _sb(512, BF), "r2r": _sb(512, BF),
+    "xt": _sb(4 * XW, BF), "wt": _sb(2048, BF), "r2l": _sb(48, BF), "r2m": _sb(1536, BF),
     "vxt": _sb(512, BF), "vht": _sb(512, BF), "zt": _sb(512, BF), "ht": _sb(1024, BF),
-    "xq": _sb(256, F8), "xs": _sb(256, U8), "rq": _sb(128, F8), "rs": _sb(128, U8), "wq": _sb(512, F8), "ws": _sb(512, U8),
-    "mq": _sb(128, F8), "ms": _sb(128, U8), "eq": _sb(128, F8), "es": _sb(128, U8),
+    "xq": _sb(XW, F8), "xs": _sb(XW, U8), "wq": _sb(512, F8), "ws": _sb(512, U8), "mq": _sb(384, F8), "ms": _sb(384, U8),
     "vxq": _sb(128, F8), "vxs": _sb(128, U8), "vhq": _sb(128, F8), "vhs": _sb(128, U8),
-    "s1c": _sb(256, F8), "s1s": _sb(256, U8), "r1c": _sb(128, F8), "r1s": _sb(128, U8), "xh": _sb(768, F8), "xhs": _sb(768, U8),
-    "s2c": _sb(256, F8), "s2s": _sb(256, U8), "r2c": _sb(128, F8), "r2s": _sb(128, U8), "l2c": _sb(272, F8), "l2s": _sb(272, U8),
+    "s1c": _sb(256, F8), "s1s": _sb(256, U8), "r1c": _sb(64, F8), "r1s": _sb(64, U8), "xh": _sb(768, F8), "xhs": _sb(768, U8),
+    "s2c": _sb(256, F8), "s2s": _sb(256, U8), "r2c": _sb(64, F8), "r2s": _sb(64, U8), "l2c": _sb(272, F8), "l2s": _sb(272, U8),
     "hp": _sb(128, F8), "hps": _sb(128, U8),
-    "nld": ("dram", [128, 2], BF), "rl1": ("dram", [128, 2], BF), "lnd": ("dram", [8, 128, 2], BF),
-    "wgd": ("dram", [128, 1], F32), "rl2": ("dram", [128, 1], F32), "lwd": ("dram", [8, 128, 1], F32),
-    "p2": _sb(2, I32), "ia": _sb(16, I32), "cf": _sb(16, F32), "of1": _sb(2, U16), "of2": _sb(2, U16), "ofh": _sb(8, U16),
-    "vr": _sb(8, F32), "th1": _sb(8, F32), "th2": _sb(4, F32), "ones": _sb(128, BF), "fix": _sb(128, BF), "zrow": _sb(256, BF),
-    "d0r": _sb(128, F32), "d0": _sb(128, F32), "xa": _sb(32, F32), "xb": _sb(32, F32),
-    "mk1": _sb(32, F32), "mk1b": _sb(32, F32), "mk1a": _sb(32, F32), "mk2": _sb(32, F32),
-    "c127": _sb(128, BF), "tri": _sb(128, BF), "s128": _sb(256, F32), "oh32": _sb(8, F32),
-    "t1": _sb(128, F32), "rm": _sb(128, F32), "zb": _sb(144, BF), "oh": _sb(128, BF), "mr": _sb(128, BF), "cum": _sb(128, BF),
-    "js": _sb(1280, BF), "jv": _sb(1024, BF), "l1": _sb(8, F32), "lx1": _sb(32, F32), "lt1": _sb(32, F32), "mn1": _sb(16, F32),
-    "off1": _sb(16, U16), "nlp": _sb(32, BF), "nlt": _sb(32, BF),
-    "nrow": _sb(256, BF), "num": _sb(256, BF), "ncol": _sb(8, BF), "tv": _sb(512, BF), "inv": _sb(256, BF), "sa": _sb(256, BF),
-    "wn": _sb(272, F32), "col": _sb(32, F32), "cc": _sb(512, F32), "lt": _sb(512, BF),
-    "rr": _sb(16, F32), "gw": _sb(64, F32), "tvv": _sb(64, BF), "tvt": _sb(64, BF), "m2": _sb(256, BF), "cum2": _sb(256, BF),
-    "l2": _sb(8, F32), "l2v": _sb(1, F32), "lx2": _sb(32, F32), "lt2": _sb(32, F32), "mn2": _sb(16, F32),
-    "off2": _sb(16, U16), "offw": _sb(16, U16), "wg": _sb(256, F32), "wgp": _sb(128, F32),
+    "rlk": ("dram", [128, 1], BF), "lk": ("dram", [8, 128, 1], BF), "rl1": ("dram", [128, 1], BF), "lnd": ("dram", [8, 128, 1], BF),
+    "rl2": ("dram", [128, 1], F32), "lwd": ("dram", [8, 128, 1], F32),
+    "p2": _sb(2, I32), "ia": _sb(16, I32), "cf": _sb(16, F32), "ofs": _sb(24, U16), "ofh": _sb(8, U16),
+    "ta": _sb(96, F32), "tb": _sb(96, F32), "th1": _sb(8, F32), "th2": _sb(4, F32), "xa": _sb(32, F32), "xb1": _sb(32, F32),
+    "xb2": _sb(32, F32), "mk": _sb(32, F32), "ones": _sb(128, BF), "tri": _sb(128, BF), "oh32": _sb(8, F32), "tc": _sb(64, F32),
+    "td": _sb(64, F32), "er": _sb(32, F32), "dm": _sb(32, F32), "s128": _sb(272, BF), "neg": _sb(16, F32), "d16": _sb(16, F32),
+    "thr": _sb(4, F32),
+    "rm": _sb(8, F32), "f1": _sb(8, F32), "oh": _sb(32, BF), "mr": _sb(128, BF), "cum": _sb(128, BF),
+    "js": _sb(1024, BF), "jv": _sb(512, BF), "sv": _sb(512, BF), "l1": _sb(8, F32), "lx1": _sb(32, F32), "lt1": _sb(32, F32),
+    "mn1": _sb(16, F32), "off1": _sb(16, U16), "nt": _sb(16, BF),
+    "crow": _sb(16, BF), "cb": _sb(32, BF), "cw": _sb(24, F32), "gq": _sb(16, F32), "nrow": _sb(256, BF), "num": _sb(272, BF),
+    "col": _sb(16, F32), "g4": _sb(4, F32), "cc": _sb(256, F32), "lt": _sb(4 * SEG, BF), "sg": _sb(128, BF), "sa": _sb(2 * SEG, BF),
+    "rr": _sb(16, F32), "tvv": _sb(64, BF), "m2": _sb(256, BF), "cum2": _sb(256, BF), "jv2": _sb(512, BF), "sv2": _sb(512, BF),
+    "l2": _sb(8, F32), "lx2": _sb(32, F32), "lt2": _sb(32, F32), "mn2": _sb(16, F32), "off2": _sb(16, U16), "offw": _sb(16, U16),
+    "wa": _sb(32, F32), "wb": _sb(32, F32), "wc": _sb(32, F32),
     "ys": _sb(128, F32),
     "pw": ("psum", [128, 2048], F32), "pe": ("psum", [128, 1536], F32), "pz": ("psum", [128, 512], F32),
 }
-NDMA = 36
-SEMAPHORES = (["kv", "ks", "kt", "kp", "sent"] + [k + n for k in ("c", "s", "n", "rc", "rs", "rn") for n in "12"]
-              + ["d%d" % i for i in range(NDMA)])
+NDMA = 30
+KINDS = ("k1", "c1", "s1", "n1", "c2", "s2", "n2")
+SEMAPHORES = ["kv", "ks", "kt", "kp", "sent"] + list(KINDS) + ["r" + k for k in KINDS] + ["d%d" % i for i in range(NDMA)]
 
 
 def split(engines, parts):
@@ -52,37 +52,38 @@ def split(engines, parts):
 
 
 def plan(src, cores, topo):
-    direct = [d for d in cores if d != src and topo.may_write(src, d)]
-    cross = [d for d in cores if d != src and not topo.may_write(src, d)]
+    near = [d for d in cores if d == src or topo.may_write(src, d)]
+    far = [d for d in cores if d not in near]
+    order = far + near
+    direct = [d for d in near if d != src]
     others = sorted((c for c in topo.cores_of(src) if c != src), key=lambda c: (topo.die(c) == topo.die(src), c))
-    can = [c for c in others if all(topo.may_write(c, d) for d in cross)]
+    can = [c for c in others if all(topo.may_write(c, d) for d in far)]
     rest = [c for c in others if c not in can]
-    half = len(cores) // 2
-    eng, helpers = {}, {}
     off = topo.engines(src, direct[0])
-    on = topo.engines(src, can[0])
-    up = [e for e in on if e not in off]
-    two = split(off, 4)
-    for i, d in enumerate(direct):
-        eng["c1", d] = eng["c2", d] = two[i]
-        eng["n1", d] = eng["n2", d] = two[3]
+    every = topo.engines(src, can[0])
+    up = [e for e in every if e not in off]
+    a, b, c = can[0:2], can[2:4], rest[0:2]
+
+    def fan(h, tos, first=0):
+        es = split(topo.engines(h, tos[0]), len(tos))
+        return [(d, es[i], order.index(d) - first) for i, d in enumerate(tos)]
+
+    on = {}
     for k in range(2):
-        far = [d for d in cross if cores.index(d) // half == k]
-        near = [d for d in direct if cores.index(d) // half == k]
-        a, b, c = can[k], can[2 + k], rest[k]
-        helpers[a], helpers[b], helpers[c] = ("c", k, far), ("s", k, far), ("s", k, near)
-        eng["c1", a], eng["c2", a] = split(up, 2)[k], split(on, 2)[k]
-        eng["n1", a] = eng["n2", a] = up[k:k + 1]
-        eng["s1", b] = eng["s2", b] = split(off, 2)[k]
-        eng["s1", c] = eng["s2", c] = split(up, 2)[k]
-    for h in helpers:
-        what, k, serve = helpers[h]
-        for i, d in enumerate(serve):
-            e = split(topo.engines(h, d), 2)[i]
-            eng[what + "1", h, d] = eng[what + "2", h, d] = e
-            if what == "c":
-                eng["n1", h, d] = eng["n2", h, d] = e[:1]
-    return {"direct": direct, "helpers": helpers, "eng": eng}
+        f2, n2 = far[2 * k:2 * k + 2], [d for d in near[2 * k:2 * k + 2] if d != src]
+        on[a[k]] = [("k1", fan(a[k], f2[:1])), ("c1", fan(a[k], f2, 2 * k)), ("c2", fan(a[k], f2, 2 * k))]
+        on[b[k]] = [("k1", fan(b[k], f2[1:])), ("s1", fan(b[k], f2, 2 * k)), ("s2", fan(b[k], f2, 2 * k))]
+        on[c[k]] = [("k1", fan(c[k], n2)), ("s1", fan(c[k], n2, 4 + 2 * k)), ("s2", fan(c[k], n2, 4 + 2 * k))]
+    on[b[0]].insert(2, ("n1", fan(b[0], far)))
+    on[c[0]].insert(2, ("n1", fan(c[0], direct)))
+    on[b[1]].append(("n2", fan(b[1], far + direct)))
+    q4, h2, o2, u2, o4 = split(every, 4), split(every, 2), split(off, 2), split(up, 2), split(off, 4)
+    out = {"ka": [(h, q4[i], 0, 0) for i, h in enumerate(a + b)], "kb": [(h, h2[i], 0, 0) for i, h in enumerate(c)],
+           "c": [(h, h2[i], 2 * i, 2) for i, h in enumerate(a)],
+           "s": [(h, o2[i], 2 * i, 2) for i, h in enumerate(b)] + [(h, u2[i], 4 + 2 * i, 2) for i, h in enumerate(c)],
+           "d": [(d, (o2[0], o4[2], o4[3])[i], order.index(d), 1) for i, d in enumerate(direct)],
+           "n1": [(b[0], u2[0], 0, 0), (c[0], u2[1], 1, 0)], "n2": [(b[1], up, 0, 0)]}
+    return {"order": order, "out": out, "on": on}
 
 
 def bits(engines):
@@ -97,9 +98,10 @@ def arrivals(kind, core, cores, topo):
     for s in cores:
         if s != core:
             p = plan(s, cores, topo)
-            n += len(p["eng"].get((kind, core), []))
-            for h in p["helpers"]:
-                n += len(p["eng"].get((kind, h, core), []))
+            if kind[0] == "c":
+                n += sum(len(e) for d, e, x, y in p["out"]["d"] if d == core)
+            for h in p["on"]:
+                n += sum(len(e) for k, ws in p["on"][h] if k == kind for d, e, x in ws if d == core)
     return n
 
 
@@ -114,30 +116,29 @@ def helper_program(g, core, T, topo):
         return
     src = home[0]
     p = plan(src, T.cores, topo)
-    if core not in p["helpers"]:
+    if core not in p["on"]:
         return
-    what, half, serve = p["helpers"][core]
     s, sent = T.rank_of(src), 0
 
     def columns(t, b):
         return t[:, 32 * b:32 * b + 32]
 
-    for kind in (("c1", "n1", "c2", "n2") if what == "c" else ("s1", "s2")):
-        g.wait_ge(T.sem["r" + kind], len(p["eng"][kind, core]))
+    for kind, writes in p["on"][core]:
+        keys = {"k": ("ka", "kb"), "c": ("c",), "s": ("s",), "n": (kind,)}[kind[0]]
+        g.wait_ge(T.sem["r" + kind], sum(len(e) for k in keys for h, e, x, y in p["out"][k] if h == core))
         tr = []
-        for d in serve:
-            k = T.rank_of(d) % 4
-            if kind[1] == "2" and s == 0 and T.rank_of(d) == 1:
-                k = 0
-            if kind[0] == "n":
+        for d, e, k in writes:
+            if kind == "k1":
+                a, b = T.rlk[:], T.lk[plan(d, T.cores, topo)["order"].index(src)]
+            elif kind[0] == "n":
                 a, b = (T.rl1[:], T.lnd[s]) if kind == "n1" else (T.rl2[:], T.lwd[s])
             elif kind[0] == "s":
                 a, b = (columns(T.r1s, k), columns(T.xhs, s)) if kind == "s1" else (columns(T.r2s, k), columns(T.l2s, s))
             else:
                 a, b = (columns(T.r1c, k), columns(T.xh, s)) if kind == "c1" else (columns(T.r2c, k), columns(T.l2c, s))
                 a, b = a.bitcast(dt.uint8), b.bitcast(dt.uint8)
-            tr.append(transfer(core, d, p["eng"][kind, core, d], T.sem[kind], a, b, topo))
-            sent += len(p["eng"][kind, core, d])
+            tr.append(transfer(core, d, e, T.sem[kind], a, b, topo))
+            sent += len(e)
         g.remote_dma_fused(tr, local_sem=T.sem.sent)
     g.wait_ge(T.sem.sent, sent)
 
@@ -153,6 +154,11 @@ def rank_program(g, core, T, topo):
     seen = {q: {} for q in eng}
     ndma = [0]
     everything = {}
+    p = plan(core, T.cores, topo)
+    perm = [T.rank_of(d) for d in p["order"]]
+    jme = perm.index(me)
+    ime = jme - 4
+    w0 = 32 * me
 
     def wait(q, deps):
         need, todo = {}, list(deps)
@@ -206,10 +212,6 @@ def rank_program(g, core, T, topo):
         wait("v", deps)
         return done("v", g.vector.transpose(out, in_))
 
-    def total(out, in_, *deps):
-        wait("v", deps)
-        return done("v", g.vector.tensor_reduce(out, in_, AxisListType.X, A.add))
-
     def quant(q, s, in_, *deps):
         wait("v", deps)
         return done("v", g.vector.quantize_mx(q, s, in_))
@@ -225,36 +227,30 @@ def rank_program(g, core, T, topo):
     def iota(out, pattern, base, cm):
         return done("p", g.iota(out, pattern, base, cm, allow_small_or_imprecise_dtypes=True))
 
-    ld_x = dma("y", T.xt[:], T.x[:])
-    ld_r = dma("s", T.rte[:, 0:32], T.rt[:, 0:32])
+    def pick(out, win, off, *deps):
+        return copy(out.bitcast(dt.uint32), win.bitcast(dt.uint32).indirect(off), *deps)
+
+    def spick(out, win, off, *deps):
+        return act(out, win.indirect(off), AF.Copy, *deps)
+
+    ld_x = dma("y", T.xt[:, 0:512], T.x[:])
+    ld_r = dma("s", T.xt[:, 520:552], T.rt[:, 0:32])
     ld_w = dma("y", T.wt[:], T.w[:], ld_x)
-    ld_2 = []
-    if me:
-        ld_2.append(dma("y", T.r2m[:, 0:4 * me], T.r2[:, 0:4 * me]))
-        ld_2.append(dma("y", T.r2m[:, 4 * me:4 * me + 4], T.r2[:, 4 * me - 4:4 * me]))
-        ld_2.append(dma("y", T.r2m[:, 4 * me + 4:36], T.r2[:, 4 * me + 4:36]))
-    else:
-        ld_2.append(dma("y", T.r2m[:, 0:4], T.r2[:, 4:8]))
-        ld_2.append(dma("y", T.r2m[:, 4:36], T.r2[:, 4:36]))
-    ld_e = dma("y", T.r2r[:, 0:4], T.r2[:, 32:36])
-    ld_vx = dma("y", T.vxt[:], T.vx[:])
-    ld_vh = dma("y", T.vht[:], T.vh[:])
-    place = {b: (b if me or b != 1 else 0) for b in range(NR)}
+    ld_2 = dma("y", T.r2l[:, 0:36], T.r2[:, 0:36])
 
     k_p2 = done("p", g.iota(T.p2[:], [[0, 2]], 0, 1))
+    k_ta = [iota(T.ta[:, 0:32], [[8, 2], [0, 8], [16, 2]], 0, 1), iota(T.ta[:, 32:64], [[1, 2], [0, 16]], 0, 0)]
     k_xa = iota(T.xa[:], [[0, 2], [1, 2], [0, 8]], 0, 0)
-    k_xb = iota(T.xb[:], [[0, 4], [1, 8]], 0, 0)
-    k_vr = iota(T.vr[:], [[1, 8]], 0, 0)
-    k_d0r = iota(T.d0r[:], [[0, 16], [1, 8]], 0, 0)
-    k_s128 = iota(T.s128[:], [[128, 8], [0, 32]], 0, 0)
+    k_xb = [iota(T.xb1[:, 4 * t:4 * t + 4], [[perm[2 * t + 1] - perm[2 * t], 2], [0, 2]], perm[2 * t], 0) for t in range(4)]
+    k_ta2 = iota(T.ta[:, 64:96], [[4, 2], [0, 8], [8, 2]], 0, 1)
     k_oh32 = iota(T.oh32[:], [[32, 8]], 0, 0)
+    k_er = iota(T.er[:], [[2, 8], [0, 2], [1, 2]], 0, 0)
+    k_z0 = fill(T.xt[:, 512:520], 0.0)
     k_zt = fill(T.zt[:], 0.0)
     k_ones = fill(T.ones[:], 1.0)
-    k_zb = fill(T.zb[:], 0.0)
-    k_nlp = fill(T.nlp[:, 16:32], 0.0)
-    k_127 = fill(T.c127[:], 127.5)
-    wait("p", [k_127])
-    k_tri = done("p", g.affine_select(T.tri[:], T.c127[:], [[-1, 128]], A.is_gt, -1.0, 0, 1))
+    k_cum = fill(T.cum[:], 0.0)
+    wait("p", [k_ones])
+    k_tri = done("p", g.affine_select(T.tri[:], T.ones[:], [[-1, 128]], A.is_gt, 0.0, 0, 1))
 
     def bitsof(i, shift, mask):
         d = T.ia[:, 2 * i:2 * i + 2]
@@ -263,248 +259,236 @@ def rank_program(g, core, T, topo):
             return done("v", g.vector.tensor_scalar(d, T.p2[:], shift, mask, A.arith_shift_right, A.bitwise_and))
         return done("v", g.vector.tensor_scalar(d, T.p2[:], mask, None, A.bitwise_and))
 
-    cf = {n: T.cf[:, i:i + 1] for i, n in enumerate(("a7", "u", "uh", "ul", "q", "t", "t1", "fx", "t2", "p0", "h", "hq", "hq2"))}
-    ka, kuh, kul = bitsof(0, 0, 7), bitsof(2, 4, 1), bitsof(3, 3, 1)
-    k_of1 = copy(T.of1[:], T.ia[:, 0:2], ka)
-    c_a7 = copy(cf["a7"], T.ia[:, 0:1], ka)
-    c_uh = copy(cf["uh"], T.ia[:, 4:5], kuh)
-    c_ul = copy(cf["ul"], T.ia[:, 6:7], kul)
-    c_fx = ts(cf["fx"], cf["a7"], 0.0, A.is_equal, None, None, c_a7)
-    c_t = ts(cf["t"], cf["ul"], 16.0, A.mult, 0.5, A.add, c_ul)
-    c_t1 = ts(cf["t1"], cf["uh"], 8.0, A.mult, cf["t"], A.add, c_t, c_uh)
-    k_fix = ts(T.fix[:], T.ones[:], cf["fx"], A.mult, None, None, k_ones, c_fx)
+    def bit(i):
+        return T.ia[:, 2 * i:2 * i + 2]
 
-    t = copy(T.rte[:, 32:64], T.rte[:, 0:32], ld_r)
-    k_mk1a = ts(T.mk1a[:], T.xa[:], cf["uh"], A.not_equal, 2000.0, A.mult, k_xa, c_uh)
-    t = copy(T.rte[:, 64:128], T.rte[:, 0:64], t)
-    k_mk1b = ts(T.mk1b[:], T.xb[:], NS1 - 0.5, A.is_lt, 128.0, A.mult, k_xb)
-    t = copy(T.rte[:, 128:256], T.rte[:, 0:128], t)
-    k_th1 = ts(T.th1[:], T.vr[:], cf["t1"], A.add, None, None, k_vr, c_t1)
-    t = copy(T.rte[:, 256:512], T.rte[:, 0:256], t)
-    k_mk1 = tt(T.mk1[:], T.mk1a[:], T.mk1b[:], A.add, k_mk1b)
-    q_r = quant(T.rq[:], T.rs[:], T.rte[:], t)
-    q_x = quant(T.xq[:, 0:128], T.xs[:, 0:128], T.xt[:], ld_x)
-    m_g = mm(T.pw[:, 0:128], T.rq[:], T.rs[:], T.xq[:, 0:128], T.xs[:, 0:128], True, True, q_x)
-    k_d0 = ts(T.d0[:], T.d0r[:], 0.0, A.is_equal, -BIG, A.mult, k_d0r)
-    k_zero1 = quant(T.xq[:, 128:256], T.xs[:, 128:256], T.zt[:], k_zt)
-    v_t1 = turn(T.t1[:], T.pw[:, 0:128], m_g)
-    v_rm = scan(T.rm[:], T.d0[:], T.t1[:], 0.0, A.add, A.max, v_t1, k_d0)
-    for k in range(4):
-        v_z = ts(T.zb[:, 1 + 32 * k:33 + 32 * k], T.rm[:, 32 * k:32 * k + 32], T.rm[:, 32 * k + 7:32 * k + 8], A.is_lt, None, None, v_rm, k_zb)
-    v_oh = tt(T.oh[:], T.zb[:, 0:128], T.zb[:, 1:129], A.subtract, v_z)
-    v_m = turn(T.mr[:], T.oh[:], v_oh)
-    v_c = scan(T.cum[:], T.fix[:], T.mr[:], 0.0, A.add, A.add, v_m, k_fix)
-    acc, part = [], {}
-    for v in range(NS1):
-        acc.append(act(T.js[:, 128 * v:128 * v + 128], T.cum[:], AF.Sign, v_c, k_th1, scale=-1.0, bias=T.th1[:, v:v + 1], accum_out=T.l1[:, v:v + 1]))
-    for v in range(NS1, 8):
-        part[v] = ts(T.jv[:, 128 * v:128 * v + 128], T.cum[:], T.th1[:, v:v + 1], A.is_le, 2.0, A.mult, v_c, k_th1)
-    for v in range(NS1, 8):
-        acc.append(total(T.l1[:, v:v + 1], T.jv[:, 128 * v:128 * v + 128], part[v]))
-    v_lx = tt(T.lx1[:], T.l1[:, 0:8].indirect(T.of1[:, 0:2]), T.mk1[:], A.add, acc, k_mk1, k_of1)
-    v_lt = turn(T.lt1[:], T.lx1[:], v_lx)
-    v_mn = tt(T.mn1[:], T.lt1[:, 0:16], T.lt1[:, 16:32], A.min, v_lt)
-    v_o0 = ts(T.off1[:, 0:16:2], T.mn1[:, 0:8], 0.5, A.mult, None, None, v_mn)
-    v_o1 = ts(T.off1[:, 1:16:2], T.mn1[:, 8:16], 0.5, A.mult, None, None, v_mn)
-    v_s1 = copy(T.s1c[:].bitcast(dt.uint32), T.xq[:].bitcast(dt.uint32).indirect(T.off1[:]), v_o1, v_o0, q_x, k_zero1)
-    a_n0 = act(T.nlp[:, 0:16:2], T.mn1[:, 0:8], AF.Copy, v_mn, scale=0.5)
-    a_n1 = act(T.nlp[:, 1:16:2], T.mn1[:, 8:16], AF.Copy, v_mn, scale=0.5)
-    a_s1 = act(T.s1s[:], T.xs[:].indirect(T.off1[:]), AF.Copy, v_o1)
-    w0 = 32 * me
-    a_own = act(T.xhs[:, w0:w0 + 32], T.xs[:].indirect(T.off1[:, 2 * me:2 * me + 2]), AF.Copy)
-    v_nt = turn(T.nlt[:], T.nlp[:], a_n1, k_nlp)
-    d_nl = dma("y", T.nld[:], T.nlt[0:16, 0:16], v_nt)
-    d_own = dma("y", T.lnd[me], T.nlt[0:16, 0:16])
-    v_own = copy(T.xh[:, w0:w0 + 32].bitcast(dt.uint32), T.xq[:].bitcast(dt.uint32).indirect(T.off1[:, 2 * me:2 * me + 2]))
+    of = {n: T.ofs[:, 2 * i:2 * i + 2] for i, n in enumerate(("s1", "v1", "s2", "v2", "n1", "n2", "ord", "gl", "z"))}
+    k3 = bitsof(0, 0, 3)
+    k_r2m = fill(T.r2m[:, 0:1024], 0.0)
+    k_tb = turn(T.tb[:, 0:64], T.ta[:, 0:64], k_ta)
+    k_of1 = [copy(of["s1"], bit(0), k3), ts(of["v1"], bit(0), 128.0, A.mult, 127.0, A.add)]
+    k_th1 = ts(T.th1[:], T.tb[:, 0:8], 0.5, A.add, None, None, k_tb)
+    k_mk = ts(T.mk[:], T.xa[:], T.tb[:, 32:33], A.not_equal, 2000.0, A.mult, k_xa)
+    k_xb1 = copy(T.xb1[:, 16:32], T.xb1[:, 0:16], k_xb)
 
-    p = plan(core, T.cores, topo)
+    q_x = quant(T.xq[:], T.xs[:], T.xt[:], ld_x, ld_r, k_z0)
+    m_g = mm(T.pz[:, 0:128], T.xq[:, 0:128], T.xs[:, 0:128], T.xq[:, XW - 128:XW], T.xs[:, XW - 128:XW], True, True, q_x)
+    v_rm = scan(T.rm[:], T.zt[:, 0:8], T.pz[:, 120:128], -BIG, A.add, A.max, m_g, k_zt)
+    a_f = act(T.js[:, 0:8], T.rm[:], AF.Sign, v_rm, scale=-1.0, bias=T.rm[:, 7:8], accum_out=T.f1[:, 0:1])
+    v_oh = ts(T.oh[:], T.xb1[:], T.f1[:, 0:1], A.is_equal, None, None, a_f, k_xb1)
+    v_m = turn(T.mr[:, 0:32], T.oh[:], v_oh)
+    bc = [copy(T.mr[0:32, 32:64], T.mr[32:64, 0:32], v_m), act(T.mr[0:32, 96:128], T.mr[96:128, 0:32], AF.Copy, v_m),
+          copy(T.mr[0:32, 64:96], T.mr[64:96, 0:32])]
+    v_c = scan(T.cum[0:32, :], T.zt[0:32, 0:128], T.mr[0:32, :], 0.0, A.add, A.add, bc, k_cum)
+
+    def lists(n, cum, th, w, jv, sv, l, lx, lt, mn, ofs, ofv, dep, consts):
+        sa = [act(T.js[:, w * k:w * k + w], cum, AF.Sign, dep, consts, scale=-1.0, bias=th[:, 2 * k:2 * k + 1], accum_out=l[:, k:k + 1])
+              for k in range(n)]
+        pa = [ts(jv[:, w * k:w * k + w], cum, th[:, 2 * k + 1:2 * k + 2], A.is_le, 2.0, A.mult, dep, consts) for k in range(n)]
+        pb = [scan(sv[:, w * k:w * k + w], T.zt[:, 0:w], jv[:, w * k:w * k + w], -float(w), A.add, A.add, pa[k]) for k in range(n)]
+        x1 = tt(lx[:, 1:32:2], sv[:].indirect(ofv[:, 0:1]), T.mk[:, 1:32:2], A.add, pb)
+        x0 = tt(lx[:, 0:32:2], l[:, 0:n].indirect(ofs[:, 0:1]), T.mk[:, 0:32:2], A.add, sa)
+        t = turn(lt[0:32, :], lx[0:32, :], x0, x1)
+        return [tt(mn[0:32, :], lt[0:32, 0:16], lt[0:32, 16:32], A.min, t), tt(mn[32:64, :], lt[0:32, 0:16], lt[0:32, 16:32], A.min)]
+
+    v_mn = lists(4, T.cum[:], T.th1, 128, T.jv, T.sv, T.l1, T.lx1, T.lt1, T.mn1, of["s1"], of["v1"], v_c, [k_th1, k_mk, k_of1])
+    v_o = [ts(T.off1[64 * k:64 * k + 64, :], T.mn1[0:64, :], 0.5, A.mult, 64.0, A.add, v_mn) for k in range(2)]
+    a_mn = act(T.mn1[64:128, :], T.mn1[0:64, :], AF.Copy, v_mn)
+    v_s1, a_s1 = [], []
+    for k in range(2):
+        v_s1.append(pick(T.s1c[:, 128 * k:128 * k + 128], T.xq[:], T.off1[:, 8 * k:8 * k + 8], v_o))
+        a_s1.append(spick(T.s1s[:, 128 * k:128 * k + 128], T.xs[:], T.off1[:, 8 * k:8 * k + 8], v_o))
+    kg, k0 = bitsof(1, 4, 7), bitsof(2, 0, 1)
+    c_g = copy(T.cf[:, 0:1], T.ia[:, 2:3], kg)
+    k_n1 = ts(of["n1"], bit(2), 8.0, A.mult, T.cf[:, 0:1], A.add, k0, c_g)
+    v_own = pick(T.xh[:, w0:w0 + 32], T.xq[:], T.off1[:, 2 * jme:2 * jme + 2])
+    a_nt = act(T.nt[:], T.mn1[:].indirect(of["n1"][:, 0:1]), AF.Identity, a_mn, k_n1, scale=0.5, bias=64.0)
+    a_own = spick(T.xhs[:, w0:w0 + 32], T.xs[:], T.off1[:, 2 * jme:2 * jme + 2])
+
     sent = [0]
 
-    def send(kind, tos, src_of, dst_of, *deps):
+    def send(key, kind, src_of, dst, *deps):
         wait("p", deps)
         tr = []
-        for to in tos:
-            e = p["eng"][kind, to]
-            tr.append(transfer(core, to, e, T.sem[kind if to in p["direct"] else "r" + kind], src_of(to), dst_of(to), topo))
+        for to, e, first, n in p["out"][key]:
+            tr.append(transfer(core, to, e, T.sem[kind], src_of(first, n), dst, topo))
             sent[0] += len(e)
         g.remote_dma_fused(tr, local_sem=T.sem.sent)
 
-    def send_stage(stage, codes, scales, land_c, relay_c, relay_s, pl, dep_c, dep_s, numbers, land_n, relay_n, dep_n):
-        def part_of(t, to):
-            if to in p["direct"]:
-                b = pl[T.rank_of(to)]
-                return t[:, 32 * b:32 * b + 32]
-            h = p["helpers"][to][1]
-            return t[:, 128 * h:128 * h + 128]
+    def send_stage(st, codes, scales, land, relay_c, relay_s, dep_c, dep_s):
+        def c_src(first, n):
+            return codes[:, 32 * first:32 * (first + n)].bitcast(dt.uint8)
 
-        def c_src(to):
-            return part_of(codes, to).bitcast(dt.uint8)
+        send("c", "rc" + st, c_src, relay_c[:].bitcast(dt.uint8), dep_c[0])
+        send("s", "rs" + st, lambda first, n: scales[:, 32 * first:32 * (first + n)], relay_s[:], dep_s)
+        send("d", "c" + st, c_src, land[:, w0:w0 + 32].bitcast(dt.uint8), dep_c)
 
-        def c_dst(to):
-            return (land_c[:, w0:w0 + 32] if to in p["direct"] else relay_c[:]).bitcast(dt.uint8)
-
-        hc = [h for h in sorted(p["helpers"]) if p["helpers"][h][0] == "c"]
-        hs = [h for h in sorted(p["helpers"]) if p["helpers"][h][0] == "s"]
-        ds = p["direct"]
-        send("c" + stage, hc, c_src, c_dst, dep_c)
-        send("s" + stage, hs, lambda to: part_of(scales, to), lambda to: relay_s[:], dep_s)
-        send("c" + stage, ds, c_src, c_dst)
-        wait("p", [dep_n])
-        kind = "n" + stage
-        tr = [transfer(core, h, p["eng"][kind, h], T.sem["r" + kind], numbers, relay_n, topo) for h in hc]
-        ids = [topo.addr(d, core) for d in ds]
-        e = p["eng"][kind, ds[0]]
-        tr.append(RemoteDMATransfer(dst_ids=[DstId(rid=r, pnc=c) for r, c in ids], dma_engine_mask=bits(e), remote_sem=T.sem[kind],
-                                    srcs=[numbers], dsts=[land_n for d in ds]))
-        sent[0] += len(e) + sum(len(p["eng"][kind, h]) for h in hc)
-        g.remote_dma_fused(tr, local_sem=T.sem.sent)
-
-    send_stage("1", T.s1c, T.s1s, T.xh, T.r1c, T.r1s, {b: b for b in range(NR)}, v_s1, a_s1, T.nld[:], T.lnd[me], T.rl1[:], d_nl)
+    for key in ("ka", "kb"):
+        send(key, "rk1", lambda first, n: T.cum[:, 127:128], T.rlk[:], v_c)
+    send_stage("1", T.s1c, T.s1s, T.xh, T.r1c, T.r1s, v_s1, a_s1)
+    send("n1", "rn1", lambda first, n: T.nt[:, first:first + 1], T.rl1[:], a_nt)
 
     q_w = quant(T.wq[:], T.ws[:], T.wt[:], ld_w)
     z2 = quant(T.xh[:, 256:384], T.xhs[:, 256:384], T.zt[:])
     z3 = quant(T.xh[:, 640:768], T.xhs[:, 640:768], T.zt[:])
-    k_tv0 = fill(T.tv[:, 128:256], 0.0)
-    ku, kq, k0, k1, k2 = bitsof(1, 3, 3), bitsof(4, 0, 15), bitsof(5, 0, 1), bitsof(6, 1, 1), bitsof(7, 2, 1)
-    c_u = copy(cf["u"], T.ia[:, 2:3], ku)
-    c_q = copy(cf["q"], T.ia[:, 8:9], kq)
-    c_p0 = copy(cf["p0"], T.ia[:, 10:11], k0)
-    c_h = ts(cf["h"], T.ia[:, 12:13], float(XH_H), A.mult, 128.0, A.add, k1)
-    k_of2 = ts(T.of2[:], T.ia[:, 14:16], 2.0, A.mult, cf["p0"], A.add, k2, c_p0)
-    c_t2 = ts(cf["t2"], cf["u"], 4.0, A.mult, 0.5, A.add, c_u)
-    c_hq = ts(cf["hq"], cf["q"], 2.0, A.mult, 2.0, A.add, c_q)
-    k_mk2 = ts(T.mk2[:], T.xa[:], cf["ul"], A.not_equal, 2000.0, A.mult)
-    k_th2 = ts(T.th2[:], T.vr[:, 0:4], cf["t2"], A.add, None, None, c_t2)
-    c_hq2 = tt(cf["hq2"], cf["hq"], cf["p0"], A.subtract, c_hq)
-    k_ofh = ts(T.ofh[:], T.oh32[:], cf["hq2"], A.add, None, None, k_oh32, c_hq2)
-    f_m = fill(T.r2m[:, 64:512], 0.0)
-    f_m2 = fill(T.r2m[:, 36:64], 0.0, ld_2)
-    q_m = quant(T.mq[:], T.ms[:], T.r2m[:], f_m2)
-    t = ld_e
+    nb = me - 1 if me else 1
+    for h in range(2):
+        o = 512 * h + 32 * h
+        t = act(T.r2m[:, o:o + 32], T.r2l[:, 0:32], AF.Copy, ld_2, k_r2m)
+        for c in (64, 80):
+            act(T.r2m[:, o + 4 * c:o + 4 * c + 4], T.r2l[:, 32:36], AF.Copy)
+        act(T.r2m[:, o + 4 * me:o + 4 * me + 4], T.r2l[:, 4 * nb:4 * nb + 4], AF.Copy, t)
+    t = act(T.r2m[:, 1024:1028], T.r2l[:, 32:36], AF.Copy)
     for w in (4, 8, 16, 32, 64, 128, 256):
-        t = copy(T.r2r[:, w:2 * w], T.r2r[:, 0:w], t)
-    q_e = quant(T.eq[:], T.es[:], T.r2r[:], t)
-    k_zrow = fill(T.zrow[:], 0.0)
-    k_wn = fill(T.wn[:, 256:272], -1.0)
-    k_l2 = fill(T.l2[:, 4:8], 0.0)
-    q_vx = quant(T.vxq[:], T.vxs[:], T.vxt[:], ld_vx)
-    q_vh = quant(T.vhq[:], T.vhs[:], T.vht[:], ld_vh)
-    dz = [dma("y", T.l2c[:, w0:w0 + 32].bitcast(dt.uint8), T.xh[:, 256:288].bitcast(dt.uint8), z2),
-          dma("y", T.l2s[:, w0:w0 + 32], T.xhs[:, 256:288]),
-          dma("y", T.l2c[:, 256:272].bitcast(dt.uint8), T.xh[:, 256:272].bitcast(dt.uint8)),
-          dma("y", T.l2s[:, 256:272], T.xhs[:, 256:272])]
+        t = act(T.r2m[:, 1024 + w:1024 + 2 * w], T.r2m[:, 1024:1024 + w], AF.Copy, t)
+    a_r2 = t
+    k1, kq, kb, k32 = bitsof(3, 1, 1), bitsof(4, 0, 15), bitsof(5, 5, 3), bitsof(6, 0, 31)
+    k_tb2 = turn(T.tb[:, 64:96], T.ta[:, 64:96], k_ta2)
+    cf = {n: T.cf[:, i + 1:i + 2] for i, n in enumerate(("q", "p0", "h", "hq", "hq2", "g1", "g2", "i"))}
+    for b in range(NR):
+        fill(T.tc[32 * (b // 2):32 * (b // 2) + 32, 16 * (b % 2):16 * (b % 2) + 16], 2.0 * perm.index(b))
+    t = fill(T.tc[:, 32:64], 16.0)
+    for b in range(NR):
+        t2 = fill(T.tc[:, 32 + b:64:16], 2.0 * perm.index(b), t)
+    c_q = copy(cf["q"], T.ia[:, 8:9], kq, k1, kb, k32)
+    c_p0 = copy(cf["p0"], T.ia[:, 4:5])
+    c_h = ts(cf["h"], T.ia[:, 6:7], float(XH_H), A.mult, 128.0, A.add)
+    c_i = ts(cf["i"], T.ia[:, 12:13], -32.0, A.add, None, None)
+    c_g1 = ts(cf["g1"], T.ia[:, 6:7], -15.0, A.mult, 15.0, A.add)
+    k_of2 = [copy(of["s2"], bit(3)), ts(of["v2"], bit(3), 256.0, A.mult, 255.0, A.add), fill(of["z"], 0)]
+    k_td = turn(T.td[:], T.tc[:], t2)
+    k_th2 = ts(T.th2[:], T.tb[:, 64:68], 0.5, A.add, None, None, k_tb2)
+    c_hq = ts(cf["hq"], cf["q"], 2.0, A.mult, 2.0, A.add, c_q)
+    c_g2 = ts(cf["g2"], cf["p0"], 4.0, A.mult, cf["g1"], A.add, c_g1)
+    k_dm = ts(T.dm[:], T.er[:], cf["q"], A.is_equal, 0.5, A.mult, k_er)
+    c_hq2 = tt(cf["hq2"], cf["hq"], cf["p0"], A.subtract, c_hq)
+    k_gl = ts(of["gl"], bit(5), cf["g2"], A.add, None, None, c_g2)
+    k_n2 = ts(of["n2"], T.td[:, 0:2], cf["p0"], A.add, None, None, k_td)
+    k_ord = copy(of["ord"], T.td[:, 32:34])
+    k_ofh = ts(T.ofh[:], T.oh32[:], cf["hq2"], A.add, None, None, k_oh32, c_hq2)
+    k_xb2 = copy(T.xb2[:], T.xb1[:])
+    if me == 0:
+        for b, v in ((1, 0.0), (0, 99.0)):
+            for c in range(2):
+                k_xb2 = fill(T.xb2[:, 2 * perm.index(b) + c:32:16], v, k_xb2)
+    k_misc = [fill(T.cb[:, 16:32], 32.0), fill(T.num[:, 256:272], -1.0), fill(T.neg[:], -1.0), fill(T.cum2[:], 0.0),
+              fill(T.thr[:, 0:2], 0.0), fill(T.thr[:, 2:4], 1e-37), fill(T.d16[:], 0.0)]
+    for s in range(NR + 1):
+        k_s128 = fill(T.s128[:, 32 * s:min(32 * s + 32, 272)], 128.0 * (s % NR))
+    k_d16 = fill(T.d16[:, 0:16:8], -BIG, k_misc)
+    q_m = quant(T.mq[:], T.ms[:], T.r2m[:], a_r2)
+    dz = [pick(T.l2c[:, w0:w0 + 32], T.xh[:, 256:384], of["z"], z2, k_of2), pick(T.l2c[:, 256:272], T.xh[:, 256:384], of["z"][:, 0:1])]
 
-    n_in = {k: arrivals(k, core, T.cores, topo) for k in ("c1", "s1", "n1", "c2", "s2", "n2")}
-    d_nr = dma("y", T.nrow[0:1, 0:256], T.lnd[:, 16 * me:16 * me + 16, :], ("n1", n_in["n1"]), d_own)
-    d_nc = [dma("y", T.ncol[:, h:h + 1], T.lnd[4 * h:4 * h + 4, 16 * me:16 * me + 16, :]) for h in range(2)]
-    wait("p", [d_nr])
-    g_num = done("p", g.partition_broadcast(T.num[:], T.nrow[0:1, 0:256], 128))
+    n_in = {k: arrivals(k, core, T.cores, topo) for k in KINDS}
     ready = [("c1", n_in["c1"]), ("s1", n_in["s1"]), v_own, a_own]
-    mw = []
-    for i in range(4):
-        mw.append(mm(T.pw[:, 512 * i:512 * i + 256], T.wq[:, 128 * i:128 * i + 128], T.ws[:, 128 * i:128 * i + 128],
-                     T.xh[:, 0:256], T.xhs[:, 0:256], True, True, q_w, ready, v_t1))
-    col = {n: T.col[:, 2 * i:2 * i + 2] for i, n in enumerate(("e8", "n2", "fe", "sc", "corr", "cc", "A", "F", "b0", "b1", "nI"))}
+    d_k = dma("y", T.lk[jme, 0:16, 0], T.cum[0:16, 127:128], v_c)
+    d_n = dma("y", T.lnd[me, 32 * ime:32 * ime + 32, 0], T.nt[32 * ime:32 * ime + 32, 1:2], a_nt)
+    d_neg = dma("y", T.lwd[me, 16 * me:16 * me + 16, 0], T.neg[0:1, :], k_misc)
+    d_c = [dma("y", T.crow[0:1, 8 * k:8 * k + 8], T.lk[4 * k:4 * k + 4, 8 * k + 2 * ime:8 * k + 2 * ime + 2, 0], ("k1", n_in["k1"]), d_k)
+           for k in range(2)]
+    d_nr = dma("y", T.nrow[0:1, 0:256], T.lnd[:, 32 * ime:32 * ime + 32, 0], ("n1", n_in["n1"]), d_n)
+    ld_vx = dma("y", T.vxt[:], T.vx[:])
+    ld_vh = dma("y", T.vht[:], T.vh[:])
+    wait("p", [d_c])
+    g_cnt = done("p", g.partition_broadcast(T.cb[:, 0:16], T.crow[0:1, :], 128))
+    wait("p", [d_nr])
+    g_num = done("p", g.partition_broadcast(T.num[:, 0:256], T.nrow[0:1, 0:256], 128))
+
+    def wmm(out, i, a, n):
+        return mm(out, T.wq[:, 128 * i:128 * i + 128], T.ws[:, 128 * i:128 * i + 128], T.xh[:, a:a + n], T.xhs[:, a:a + n],
+                  True, True, q_w, ready, v_rm)
+
+    mw = [wmm(T.pw[:, 512 * i:512 * i + 256], i, 0, 256) for i in range(3)]
+    mw += [wmm(T.pw[:, 1536:1664], 3, 0, 128), wmm(T.pz[:, 0:128], 3, 128, 128)]
+    r0 = ts(T.ht[:, 0:1024:4], T.pw[:, 0:256], 0.0, A.max, 0.0625, A.mult, mw[0])
+    r1 = act(T.ht[:, 1:1024:4], T.pw[:, 512:768], AF.Relu, mw[1], scale=0.0625)
+    r2 = act(T.ht[:, 2:1024:4], T.pw[:, 1024:1280], AF.Relu, mw[2], scale=0.0625)
+    r3b = act(T.ht[:, 515:1024:4], T.pz[:, 0:128], AF.Relu, mw[4], scale=0.0625)
+    t = ts(T.cw[:, 0:16], T.cb[:].indirect(of["ord"][:, 0:1]), 32.0, A.min, 32.0, A.subtract, g_cnt, k_ord, k_misc)
+    t = scan(T.cw[:, 16:24], T.zt[:, 0:8], T.cw[:, 0:8], 0.0, A.add, A.add, t)
+    t = copy(T.gq[:], T.cw[:].indirect(of["gl"][:, 0:1]), t, k_gl)
+    col = {n: T.col[:, 2 * i:2 * i + 2] for i, n in enumerate(("e8", "sc", "F", "base", "d"))}
 
     def one(n, h):
         return col[n][:, h:h + 1]
 
-    rel = []
-    for i in range(4):
-        o, ps = T.ht[:, i:1024:4], T.pw[:, 512 * i:512 * i + 256]
-        if i % 2 == 0:
-            rel.append(ts(o, ps, 0.0, A.max, 0.0625, A.mult, mw[i]))
-        else:
-            rel.append(act(o, ps, AF.Relu, mw[i], scale=0.0625))
-    q_h = quant(T.xh[:, XH_H:XH_H + 256], T.xhs[:, XH_H:XH_H + 256], T.ht[:], rel)
+    r3a = ts(T.ht[:, 3:512:4], T.pw[:, 1536:1664], 0.0, A.max, 0.0625, A.mult, mw[3])
+    v_n4 = ts(T.gq[:, 6:8], T.gq[:, 0:2], -1.0, A.mult, T.cw[:, 23:24], A.add, t)
+    q_h = [quant(T.xh[:, XH_H:XH_H + 128], T.xhs[:, XH_H:XH_H + 128], T.ht[:, 0:512], r0, r1, r2, r3a)]
+    q_h.append(quant(T.xh[:, XH_H + 128:XH_H + 256], T.xhs[:, XH_H + 128:XH_H + 256], T.ht[:, 512:1024], r3b))
+    v_b = ts(col["base"], T.gq[:, 2:4], cf["i"], A.is_le, 1024.0, A.mult, c_i)
+    m_e, m_r = [], []
     for h in range(2):
         a = XH_H + 128 * h
-        m_e = mm(T.pe[:, 512 * h:512 * h + 128], T.xh[:, a:a + 128], T.xhs[:, a:a + 128], T.mq[:], T.ms[:], True, True, q_h, q_m)
-    m_row = mm(T.pe[:, 1024:1280], T.eq[:], T.es[:], T.xh[:, XH_H:XH_H + 256], T.xhs[:, XH_H:XH_H + 256], True, True, q_e)
-    v_ta = tt(T.tv[:, 0:128], T.num[:, 0:128], T.tri[:], A.is_lt, g_num, k_tri)
-    v_tb = tt(T.tv[:, 384:512], T.num[:, 128:256], T.tri[:], A.is_lt)
-    v_tc = ts(T.tv[:, 256:384], T.num[:, 0:128], 127.5, A.is_lt, None, None)
-    a_va = act(T.inv[:], T.num[:], AF.Sign, g_num, scale=-1.0, bias=127.5, accum_out=one("nI", 0))
-    key = T.pe[:, 8:1024:512]
+        m_e.append(mm(T.pe[:, 0:128], T.xh[:, a:a + 128], T.xhs[:, a:a + 128], T.mq[:, 128 * h:128 * h + 128],
+                      T.ms[:, 128 * h:128 * h + 128], h == 0, h == 1, q_h[h], q_m))
+        m_r.append(mm(T.pe[:, 512 + 512 * h:640 + 512 * h], T.mq[:, 256:384], T.ms[:, 256:384], T.xh[:, a:a + 128], T.xhs[:, a:a + 128],
+                      True, True))
+    row = [T.pe[:, 512 + 512 * h:640 + 512 * h] for h in range(2)]
+
+    def seg(k):
+        return T.lt[:, SEG * k:SEG * k + 128]
+
     f = 0.6 * 2.0 ** -23
-    v_fe = ts(col["fe"], key, f, A.mult, None, None, m_e)
-    v_n2 = ts(col["n2"], key, -f, A.mult, 1e-30, A.max)
-    v_e8 = copy(col["e8"], key)
-    v_sc = tt(col["sc"], col["fe"], col["n2"], A.max, v_n2)
-    ac = []
+    v_e8 = copy(col["e8"], T.pe[:, 64:80:8], m_e[1])
+    v_r = scan(T.rr[:], T.d16[:], T.pe[:, 0:16], 0.0, A.add, A.max, k_d16)
+    v_g4 = tt(T.g4[:], T.pe[:, 64:96:8], T.thr[:], A.is_ge)
+    a_sc = act(col["sc"], col["e8"], AF.Abs, v_e8, scale=f, bias=1e-37)
+    a_c0 = act(T.cc[:, 0:128], T.tri[:], AF.Identity, a_sc, k_tri, scale=one("sc", 0), bias=one("e8", 0))
+    a_sg = act(T.sg[:], row[1], AF.Sign, m_r[1], scale=-1.0, bias=one("e8", 0))
+    a_c1 = act(T.cc[:, 128:256], T.tri[:], AF.Identity, scale=one("sc", 1), bias=one("e8", 1))
+    a_l0 = act(seg(0), T.sg[:], AF.Relu, a_sg)
     for h in range(2):
-        ac.append(act(T.cc[:, 256 * h:256 * h + 256], T.tv[:, 256 * h:256 * h + 256], AF.Identity, v_sc, v_tc, k_tv0,
-                      scale=one("sc", h), bias=one("e8", h)))
-    v_ni = ts(one("nI", 1), one("nI", 0), -0.5, A.mult, 128.0, A.add, a_va)
-    v_b0 = ts(col["b0"], T.ncol[:, 0:2], 127.5, A.is_gt, -1000.0, A.mult, d_nc)
-    for h in range(2):
-        v_r = scan(T.rr[:, 8 * h:8 * h + 8], T.d0[:, 0:8], T.pe[:, 512 * h:512 * h + 8], 0.0, A.add, A.max)
-    v_co = ts(col["corr"], col["e8"], 0.0, A.is_gt, one("nI", 1), A.mult, v_ni)
-    for h in range(2):
-        a_f = act(T.js[:, 768 + 8 * h:776 + 8 * h], T.rr[:, 8 * h:8 * h + 8], AF.Sign, v_r, scale=-1.0, bias=T.rr[:, 8 * h + 7:8 * h + 8], accum_out=one("F", h))
-    vl = [tt(T.lt[:, 0:256], T.pe[:, 1024:1280], T.cc[:, 0:256], A.is_lt, ac[0], m_row)]
-    v_b1 = tt(col["b1"], col["corr"], col["b0"], A.add, v_co, v_b0)
-    vl.append(tt(T.lt[:, 256:512], T.pe[:, 1024:1280], T.cc[:, 256:512], A.is_lt, ac[1]))
-    a_a = act(T.js[:, 1024:1280], T.lt[:, 0:256], AF.Copy, vl[0], accum_out=one("A", 0))
-    v_cc = ts(col["cc"], col["b1"], DF - 0.5, A.add, None, None, v_b1)
-    v_a1 = scan(T.sa[:], T.zrow[:], T.lt[:, 256:512], 0.0, A.add, A.add, vl[1], k_zrow)
-    for h in range(2):
-        v_gw = ts(T.gw[:, 32 * h:32 * h + 32], T.xb[:], one("F", h), A.is_equal, one("cc", h), A.mult, a_f, v_cc)
-    v_v1 = ts(T.tvv[:, 32:64], T.gw[:, 32:64], T.sa[:, 255:256], A.is_gt, None, None, v_gw, v_a1)
-    v_v0 = ts(T.tvv[:, 0:32], T.gw[:, 0:32], one("A", 0), A.is_gt, None, None, a_a)
-    v_tv = turn(T.tvt[:], T.tvv[:], v_v0, v_v1)
+        a_f = act(T.js[:, 8 * h:8 * h + 8], T.rr[:, 8 * h:8 * h + 8], AF.Sign, v_r, scale=-1.0, bias=T.rr[:, 8 * h + 7:8 * h + 8], accum_out=one("F", h))
+    v_l1 = ts(seg(1), row[0], one("e8", 1), A.is_le, None, None, v_e8, m_r[0])
+    v_co = tt(T.lt[:, 128:4 * SEG:SEG], T.g4[:], T.gq[:, 4:8], A.mult, v_g4, v_n4)
+    v_l2 = tt(seg(2), row[0], T.cc[:, 0:128], A.is_lt, a_c0)
+    v_l3 = tt(seg(3), row[1], T.cc[:, 128:256], A.is_lt, a_c1)
+    v_a = []
+    for h in (0, 1):
+        v_a.append(scan(T.sa[:, SEG * h:SEG * h + 129], T.lt[:, SEG * h:SEG * h + 129], T.lt[:, SEG * (2 + h):SEG * (2 + h) + 129],
+                        one("base", h), A.add, A.add, v_b, v_co, (a_l0, v_l3)[h], v_l2))
+    v_d = ts(col["d"], T.sa[:, 128:2 * SEG:SEG], DF - 0.5, A.is_lt, None, None, v_a)
+    v_v = [ts(T.tvv[:, 32 * h:32 * h + 32], T.xb2[:], one("F", h), A.is_equal, one("d", h), A.mult, v_d, a_f, k_xb2) for h in range(2)]
+    v_t = [turn(T.m2[:, 128 * h:128 * h + 32], T.tvv[:, 32 * h:32 * h + 32], v_v[h]) for h in range(2)]
     bc = []
-    for q in range(4):
-        for h in range(2):
-            o, i = T.m2[0:32, 128 * h + 32 * q:128 * h + 32 * q + 32], T.tvt[32 * q:32 * q + 32, 32 * h:32 * h + 32]
-            bc.append(copy(o, i, v_tv) if q < 2 else act(o, i, AF.Copy, v_tv))
-    v_c0 = scan(T.cum2[0:32, :], T.zrow[0:32, :], T.m2[0:32, :], 0.0, A.add, A.add, bc)
-    v_c2 = [act(T.cum2[64:96, :], T.cum2[0:32, :], AF.Copy, v_c0), copy(T.cum2[32:64, :], T.cum2[0:32, :], v_c0),
-            copy(T.cum2[96:128, :], T.cum2[0:32, :])]
-    acc = []
-    for v in range(NS2):
-        acc.append(act(T.js[:, 256 * v:256 * v + 256], T.cum2[:], AF.Sign, v_c2, k_th2, scale=-1.0, bias=T.th2[:, v:v + 1], accum_out=T.l2[:, v:v + 1]))
-    v_p = ts(T.jv[:, 0:256], T.cum2[:], T.th2[:, NS2:NS2 + 1], A.is_le, 2.0, A.mult, v_c2, v_lx)
-    v_p = total(T.l2v[:], T.jv[:, 0:256], v_p)
-    v_p = ts(T.l2[:, NS2:NS2 + 1], T.l2v[:], -256.0, A.add, None, None, v_p)
-    v_lx = tt(T.lx2[:], T.l2[:, 0:8].indirect(T.of2[:, 0:2]), T.mk2[:], A.add, acc, v_p, k_mk2, k_of2, k_l2)
-    v_lt = turn(T.lt2[:], T.lx2[:], v_lx)
-    v_m0 = tt(T.mn2[:, 0:8], T.lt2[:, 0:8], T.lt2[:, 8:16], A.min, v_lt)
-    v_m1 = tt(T.mn2[:, 8:16], T.lt2[:, 16:24], T.lt2[:, 24:32], A.min)
-    v_o0 = ts(T.off2[:, 0:16:2], T.mn2[:, 0:8], 0.5, A.mult, cf["h"], A.add, v_m0, c_h)
-    v_o1 = ts(T.off2[:, 1:16:2], T.mn2[:, 8:16], 0.5, A.mult, cf["h"], A.add, v_m1)
-    v_s2 = copy(T.s2c[:].bitcast(dt.uint32), T.xh[:].bitcast(dt.uint32).indirect(T.off2[:]), v_o1, ready, q_h, z2, z3)
-    a_s2 = act(T.s2s[:], T.xhs[:].indirect(T.off2[:]), AF.Copy, v_o1, ready)
-    v_w0 = ts(T.offw[:, 0:16:2], T.mn2[:, 0:8], 0.5, A.mult, 128.0, A.add)
-    v_w1 = ts(T.offw[:, 1:16:2], T.mn2[:, 8:16], 0.5, A.mult, 128.0, A.add)
-    v_wn = tt(T.wn[:, 0:256], T.num[:], T.s128[:], A.add, k_s128)
-    v_wg = copy(T.wg[:], T.wn[:].indirect(T.offw[:]), v_wn, v_w1, k_wn)
-    v_g0 = copy(T.wgp[:, 0:128:2], T.wg[:, 0:256:4], v_wg)
-    v_g1 = copy(T.wgp[:, 1:128:2], T.wg[:, 1:256:4])
-    runs = [(0, 0, 128)] if me else [(0, 16, 16), (16, 0, 16), (32, 32, 96)]
-    d_wg, d_wo = [], []
-    for to, fr, n in runs:
-        d_wg.append(dma("y", T.wgd[to:to + n, 0], T.wgp[0:1, fr:fr + n], v_g1))
-        d_wo.append(dma("s", T.lwd[me, to:to + n, 0], T.wgp[0:1, fr:fr + n], v_g1))
-    send_stage("2", T.s2c, T.s2s, T.l2c, T.r2c, T.r2s, place, v_s2, a_s2, T.wgd[:], T.lwd[me], T.rl2[:], d_wg)
+    for q in range(1, 4):
+        bc.append(act(T.m2[0:32, 32 * q:32 * q + 32], T.m2[32 * q:32 * q + 32, 0:32], AF.Copy, v_t[0]))
+        bc.append(copy(T.m2[0:32, 128 + 32 * q:160 + 32 * q], T.m2[32 * q:32 * q + 32, 128:160], v_t[1]))
+    v_c2 = scan(T.cum2[0:32, :], T.zt[0:32, 0:256], T.m2[0:32, :], 0.0, A.add, A.add, bc)
+    v_mn = lists(2, T.cum2[:], T.th2, 256, T.jv2, T.sv2, T.l2, T.lx2, T.lt2, T.mn2, of["s2"], of["v2"], v_c2, [k_th2, k_of2])
+    v_o = [ts(T.off2[64 * k:64 * k + 64, :], T.mn2[0:64, :], 0.5, A.mult, T.cf[0:64, 3:4], A.add, v_mn, c_h) for k in range(2)]
+    a_mn = act(T.mn2[64:128, :], T.mn2[0:64, :], AF.Copy, v_mn)
+    v_s2, a_s2 = [], []
+    for k in range(2):
+        v_s2.append(pick(T.s2c[:, 128 * k:128 * k + 128], T.xh[:], T.off2[:, 8 * k:8 * k + 8], v_o, z3))
+        a_s2.append(spick(T.s2s[:, 128 * k:128 * k + 128], T.xhs[:], T.off2[:, 8 * k:8 * k + 8], v_o))
+    t = ts(T.offw[:], T.mn2[:].indirect(of["n2"][:, 0:1]), 0.5, A.mult, 128.0, A.add, a_mn, k_n2)
+    t = [tt(T.wa[:], T.s128[:].indirect(T.offw[:, 0:2]), T.dm[:], A.mult, t, k_s128, k_dm),
+         tt(T.wb[:], T.num[:].indirect(T.offw[:, 0:2]), T.dm[:], A.mult, g_num)]
+    v_w = scan(T.wc[:], T.wa[:], T.wb[:], 0.0, A.add, A.add, t)
+    send_stage("2", T.s2c, T.s2s, T.l2c, T.r2c, T.r2s, v_s2, a_s2)
+    send("n2", "rn2", lambda first, n: T.wc[:, 31:32], T.rl2[:], v_w)
+    q_vx = quant(T.vxq[:], T.vxs[:], T.vxt[:], ld_vx)
+    q_vh = quant(T.vhq[:], T.vhs[:], T.vht[:], ld_vh)
+    dz += [spick(T.l2s[:, w0:w0 + 32], T.xhs[:, 256:384], of["z"]), spick(T.l2s[:, 256:272], T.xhs[:, 256:384], of["z"][:, 0:1])]
 
     ready = [("c2", n_in["c2"]), ("s2", n_in["s2"]), dz]
     out = (T.pz[:, 0:128], T.pw[:, 512:640])
     my = []
     for k in range(2):
         a = 128 * k
-        mm(out[k], T.vxq[:], T.vxs[:], T.l2c[:, a:a + 128], T.l2s[:, a:a + 128], True, False, ready, q_vx, q_vh, rel)
+        mm(out[k], T.vxq[:], T.vxs[:], T.l2c[:, a:a + 128], T.l2s[:, a:a + 128], True, False, ready, q_vx, q_vh)
         my.append(mm(out[k], T.vhq[:], T.vhs[:], T.l2c[:, a + 2:a + 130], T.l2s[:, a + 2:a + 130], False, True))
-    a_hp = act(T.hps[:], T.l2s[:, 0:256].indirect(T.ofh[:]), AF.Copy, ready, k_ofh)
-    v_hp = copy(T.hp[:].bitcast(dt.uint32), T.l2c[:, 0:256].bitcast(dt.uint32).indirect(T.ofh[:]), ready, k_ofh)
-    for r in range(2):
-        v_y = copy(T.ys[:, r:64:2], T.pz[:, r:128:4], my[0])
-        a_y = act(T.ys[:, 64 + r:128:2], T.pw[:, 512 + r:640:4], AF.Copy, my[1])
+    a_hp = spick(T.hps[:], T.l2s[:, 0:256], T.ofh[:], ready, k_ofh)
+    v_hp = pick(T.hp[:], T.l2c[:, 0:256], T.ofh[:], ready, k_ofh)
+    for k in range(2):
+        for r in range(2):
+            v_y = copy(T.ys[:, 64 * k + r:64 * k + 64:2], out[k][:, r:128:4], my[k])
     dma("y", T.oc[:, 0:512], T.hp[:].bitcast(dt.uint8), v_hp)
+    dma("y", T.y[:], T.ys[:], v_y)
     for k in range(4):
-        dma("y", T.osc[4 * k:4 * k + 4, 0:128], T.hps[32 * k:32 * k + 4, 0:128], a_hp)
-    dma("y", T.y[:, 0:64], T.ys[:, 0:64], v_y)
-    dma("s", T.y[:, 64:128], T.ys[:, 64:128], a_y)
-    dma("s", T.who[0:1, 0:128], T.lwd[:, 16 * me:16 * me + 16, 0], ("n2", n_in["n2"]), d_wo)
+        dma("s", T.osc[4 * k:4 * k + 4, 0:128], T.hps[32 * k:32 * k + 4, 0:128], a_hp)
+    dma("s", T.who[0:1, 0:128], T.lwd[:, 16 * me:16 * me + 16, 0], ("n2", n_in["n2"]), d_neg)
     g.wait_ge(T.sem.sent, sent[0])
     wait("p", [(s, everything[s]) for s in everything])

@@ -5,7 +5,7 @@ F8, U8, U16, BF, F32, I32 = "float8_e4m3fn_x4", "uint8", "uint16", "bfloat16", "
 DF, NR = 64, 8
 BIG = 1.0e29
 XW = 138
-XH_H = 384
+XH_H = 272
 SEG = 144
 
 
@@ -14,28 +14,27 @@ def _sb(w, d):
 
 
 SCRATCH = {
-    "xt": _sb(4 * XW, BF), "wt": _sb(2048, BF), "r2l": _sb(48, BF), "r2m": _sb(1536, BF),
-    "vxt": _sb(512, BF), "vht": _sb(512, BF), "zt": _sb(512, BF), "ht": _sb(1024, BF),
-    "xq": _sb(XW, F8), "xs": _sb(XW, U8), "wq": _sb(512, F8), "ws": _sb(512, U8), "mq": _sb(384, F8), "ms": _sb(384, U8),
-    "vxq": _sb(128, F8), "vxs": _sb(128, U8), "vhq": _sb(128, F8), "vhs": _sb(128, U8),
-    "s1c": _sb(256, F8), "s1s": _sb(256, U8), "r1c": _sb(64, F8), "r1s": _sb(64, U8), "xh": _sb(768, F8), "xhs": _sb(768, U8),
+    "xt": _sb(4 * XW, BF), "wt": _sb(2048, BF), "r2l": _sb(48, BF), "r2m": _sb(1024, BF),
+    "vxt": _sb(512, BF), "vht": _sb(512, BF), "zt": _sb(256, BF), "ht": _sb(1024, BF),
+    "xq": _sb(XW, F8), "xs": _sb(XW, U8), "wq": _sb(512, F8), "ws": _sb(512, U8), "mq": _sb(256, F8), "ms": _sb(256, U8),
+    "eq": _sb(128, F8), "es": _sb(128, U8), "vxq": _sb(128, F8), "vxs": _sb(128, U8), "vhq": _sb(128, F8), "vhs": _sb(128, U8),
+    "s1c": _sb(256, F8), "s1s": _sb(256, U8), "r1c": _sb(64, F8), "r1s": _sb(64, U8), "xh": _sb(544, F8), "xhs": _sb(544, U8),
     "s2c": _sb(256, F8), "s2s": _sb(256, U8), "r2c": _sb(64, F8), "r2s": _sb(64, U8), "l2c": _sb(272, F8), "l2s": _sb(272, U8),
     "hp": _sb(128, F8), "hps": _sb(128, U8),
     "rlk": ("dram", [128, 1], BF), "lk": ("dram", [8, 128, 1], BF), "rl1": ("dram", [128, 1], BF), "lnd": ("dram", [8, 128, 1], BF),
     "rl2": ("dram", [128, 1], F32), "lwd": ("dram", [8, 128, 1], F32),
-    "p2": _sb(2, I32), "ia": _sb(16, I32), "cf": _sb(16, F32), "ofs": _sb(24, U16), "ofh": _sb(8, U16),
-    "ta": _sb(96, F32), "tb": _sb(96, F32), "th1": _sb(8, F32), "th2": _sb(4, F32), "xa": _sb(32, F32), "xb1": _sb(32, F32),
-    "xb2": _sb(32, F32), "mk": _sb(32, F32), "ones": _sb(128, BF), "tri": _sb(128, BF), "oh32": _sb(8, F32), "tc": _sb(64, F32),
-    "td": _sb(64, F32), "er": _sb(32, F32), "dm": _sb(32, F32), "s128": _sb(272, BF), "neg": _sb(16, F32), "d16": _sb(16, F32),
-    "thr": _sb(4, F32),
-    "rm": _sb(8, F32), "f1": _sb(8, F32), "oh": _sb(32, BF), "mr": _sb(128, BF), "cum": _sb(128, BF),
+    "ofs": _sb(24, U16), "ofh": _sb(8, U16), "ofe": _sb(8, U16), "ta": _sb(128, F32), "tb": _sb(128, F32), "tc": _sb(224, F32),
+    "td": _sb(224, F32), "ch": _sb(2, F32), "th1": _sb(8, F32), "th2": _sb(4, F32), "xa": _sb(32, F32), "xb1": _sb(32, F32),
+    "xb2": _sb(32, F32), "mk": _sb(32, F32), "ones": _sb(128, BF), "tri": _sb(128, BF), "oh32": _sb(8, F32),
+    "er": _sb(32, F32), "dm": _sb(32, F32), "s128": _sb(272, BF), "neg": _sb(16, F32), "d16": _sb(16, F32), "thr": _sb(4, F32),
+    "rm": _sb(8, F32), "f1": _sb(8, F32), "oh": _sb(128, BF), "mr": _sb(128, BF), "cum": _sb(128, BF),
     "js": _sb(1024, BF), "jv": _sb(512, BF), "sv": _sb(512, BF), "l1": _sb(8, F32), "lx1": _sb(32, F32), "lt1": _sb(32, F32),
     "mn1": _sb(16, F32), "off1": _sb(16, U16), "nt": _sb(16, BF),
-    "crow": _sb(16, BF), "cb": _sb(32, BF), "cw": _sb(24, F32), "gq": _sb(16, F32), "nrow": _sb(256, BF), "num": _sb(272, BF),
-    "col": _sb(16, F32), "g4": _sb(4, F32), "cc": _sb(256, F32), "lt": _sb(4 * SEG, BF), "sg": _sb(128, BF), "sa": _sb(2 * SEG, BF),
-    "rr": _sb(16, F32), "tvv": _sb(64, BF), "m2": _sb(256, BF), "cum2": _sb(256, BF), "jv2": _sb(512, BF), "sv2": _sb(512, BF),
-    "l2": _sb(8, F32), "lx2": _sb(32, F32), "lt2": _sb(32, F32), "mn2": _sb(16, F32), "off2": _sb(16, U16), "offw": _sb(16, U16),
-    "wa": _sb(32, F32), "wb": _sb(32, F32), "wc": _sb(32, F32),
+    "crow": _sb(16, BF), "cb": _sb(16, BF), "cw": _sb(24, F32), "gq": _sb(16, F32), "nrow": _sb(256, BF), "num": _sb(272, BF),
+    "col": _sb(16, F32), "g4": _sb(4, F32), "gw": _sb(64, F32), "cc": _sb(256, F32), "lt": _sb(4 * SEG, BF), "sg": _sb(128, BF),
+    "sa": _sb(2 * SEG, BF), "rr": _sb(16, F32), "tvv": _sb(64, BF), "m2": _sb(256, BF), "cum2": _sb(256, BF), "jv2": _sb(512, BF),
+    "sv2": _sb(512, BF), "l2": _sb(8, F32), "lx2": _sb(32, F32), "lt2": _sb(32, F32), "mn2": _sb(16, F32), "off2": _sb(16, U16),
+    "offw": _sb(16, U16), "wa": _sb(32, F32), "wb": _sb(32, F32), "wc": _sb(32, F32),
     "ys": _sb(128, F32),
     "pw": ("psum", [128, 2048], F32), "pe": ("psum", [128, 1536], F32), "pz": ("psum", [128, 512], F32),
 }
@@ -52,9 +51,10 @@ def split(engines, parts):
 
 
 def plan(src, cores, topo):
-    near = [d for d in cores if d == src or topo.may_write(src, d)]
-    far = [d for d in cores if d not in near]
-    order = far + near
+    first = [d for d in cores if d == cores[0] or topo.may_write(cores[0], d)]
+    order = first + [d for d in cores if d not in first]
+    near = [d for d in order if d == src or topo.may_write(src, d)]
+    far = [d for d in order if d not in near]
     direct = [d for d in near if d != src]
     others = sorted((c for c in topo.cores_of(src) if c != src), key=lambda c: (topo.die(c) == topo.die(src), c))
     can = [c for c in others if all(topo.may_write(c, d) for d in far)]
@@ -63,27 +63,28 @@ def plan(src, cores, topo):
     every = topo.engines(src, can[0])
     up = [e for e in every if e not in off]
     a, b, c = can[0:2], can[2:4], rest[0:2]
+    jf, jn = order.index(far[0]), order.index(near[0])
 
-    def fan(h, tos, first=0):
+    def fan(h, tos, base=0):
         es = split(topo.engines(h, tos[0]), len(tos))
-        return [(d, es[i], order.index(d) - first) for i, d in enumerate(tos)]
+        return [(d, es[i], order.index(d) - base) for i, d in enumerate(tos)]
 
     on = {}
     for k in range(2):
         f2, n2 = far[2 * k:2 * k + 2], [d for d in near[2 * k:2 * k + 2] if d != src]
-        on[a[k]] = [("k1", fan(a[k], f2[:1])), ("c1", fan(a[k], f2, 2 * k)), ("c2", fan(a[k], f2, 2 * k))]
-        on[b[k]] = [("k1", fan(b[k], f2[1:])), ("s1", fan(b[k], f2, 2 * k)), ("s2", fan(b[k], f2, 2 * k))]
-        on[c[k]] = [("k1", fan(c[k], n2)), ("s1", fan(c[k], n2, 4 + 2 * k)), ("s2", fan(c[k], n2, 4 + 2 * k))]
+        on[a[k]] = [("k1", fan(a[k], f2[:1])), ("c1", fan(a[k], f2, jf + 2 * k)), ("c2", fan(a[k], f2, jf + 2 * k))]
+        on[b[k]] = [("k1", fan(b[k], f2[1:])), ("s1", fan(b[k], f2, jf + 2 * k)), ("s2", fan(b[k], f2, jf + 2 * k))]
+        on[c[k]] = [("k1", fan(c[k], n2)), ("s1", fan(c[k], n2, jn + 2 * k)), ("s2", fan(c[k], n2, jn + 2 * k))]
     on[b[0]].insert(2, ("n1", fan(b[0], far)))
     on[c[0]].insert(2, ("n1", fan(c[0], direct)))
     on[b[1]].append(("n2", fan(b[1], far + direct)))
     q4, h2, o2, u2, o4 = split(every, 4), split(every, 2), split(off, 2), split(up, 2), split(off, 4)
     out = {"ka": [(h, q4[i], 0, 0) for i, h in enumerate(a + b)], "kb": [(h, h2[i], 0, 0) for i, h in enumerate(c)],
-           "c": [(h, h2[i], 2 * i, 2) for i, h in enumerate(a)],
-           "s": [(h, o2[i], 2 * i, 2) for i, h in enumerate(b)] + [(h, u2[i], 4 + 2 * i, 2) for i, h in enumerate(c)],
+           "c": [(h, h2[i], jf + 2 * i, 2) for i, h in enumerate(a)],
+           "s": [(h, o2[i], jf + 2 * i, 2) for i, h in enumerate(b)] + [(h, u2[i], jn + 2 * i, 2) for i, h in enumerate(c)],
            "d": [(d, (o2[0], o4[2], o4[3])[i], order.index(d), 1) for i, d in enumerate(direct)],
-           "n1": [(b[0], u2[0], 0, 0), (c[0], u2[1], 1, 0)], "n2": [(b[1], up, 0, 0)]}
-    return {"order": order, "out": out, "on": on}
+           "n1": [(b[0], u2[0], jf // 4, 0), (c[0], u2[1], jn // 4, 0)], "n2": [(b[1], up, 0, 0)]}
+    return {"order": order, "out": out, "on": on, "halves": (jf // 4, jn // 4)}
 
 
 def bits(engines):
@@ -129,7 +130,7 @@ def helper_program(g, core, T, topo):
         tr = []
         for d, e, k in writes:
             if kind == "k1":
-                a, b = T.rlk[:], T.lk[plan(d, T.cores, topo)["order"].index(src)]
+                a, b = T.rlk[:], T.lk[s]
             elif kind[0] == "n":
                 a, b = (T.rl1[:], T.lnd[s]) if kind == "n1" else (T.rl2[:], T.lwd[s])
             elif kind[0] == "s":
@@ -157,7 +158,7 @@ def rank_program(g, core, T, topo):
     p = plan(core, T.cores, topo)
     perm = [T.rank_of(d) for d in p["order"]]
     jme = perm.index(me)
-    ime = jme - 4
+    ime = jme % 4
     w0 = 32 * me
 
     def wait(q, deps):
@@ -220,6 +221,9 @@ def rank_program(g, core, T, topo):
         wait("s", deps)
         return done("s", g.scalar.activation(out, in_, func, **kw))
 
+    def sfill(out, n, c):
+        return act(out, T.zt[:, 0:n], AF.Identity, bias=c)
+
     def mm(out, l, ls, r, rs, start, stop, *deps):
         wait("t", deps)
         return done("t", g.tensor.matmul_mx(out, l, ls, r, rs, start, stop))
@@ -233,76 +237,70 @@ def rank_program(g, core, T, topo):
     def spick(out, win, off, *deps):
         return act(out, win.indirect(off), AF.Copy, *deps)
 
+    def pairs(out, vals, halves):
+        return [iota(out[:, 16 * m + 4 * t:16 * m + 4 * t + 4], [[vals[2 * t + 1] - vals[2 * t], 2], [0, 2]], vals[2 * t], 0)
+                for m in range(halves) for t in range(4)]
+
     ld_x = dma("y", T.xt[:, 0:512], T.x[:])
     ld_r = dma("s", T.xt[:, 520:552], T.rt[:, 0:32])
     ld_w = dma("y", T.wt[:], T.w[:], ld_x)
     ld_2 = dma("y", T.r2l[:, 0:36], T.r2[:, 0:36])
 
-    k_p2 = done("p", g.iota(T.p2[:], [[0, 2]], 0, 1))
-    k_ta = [iota(T.ta[:, 0:32], [[8, 2], [0, 8], [16, 2]], 0, 1), iota(T.ta[:, 32:64], [[1, 2], [0, 16]], 0, 0)]
+    k_ta = [iota(T.ta[:, 0:32], [[8, 2], [0, 8], [16, 2]], 0, 1), iota(T.ta[:, 32:64], [[1, 2], [0, 16]], 0, 0),
+            iota(T.ta[:, 64:96], [[0, 8], [1, 4]], 0, 0), iota(T.ta[:, 96:128], [[16, 2], [0, 8], [128, 2]], 0, 1)]
+    k_xb = pairs(T.xb1, perm, 1)
     k_xa = iota(T.xa[:], [[0, 2], [1, 2], [0, 8]], 0, 0)
-    k_xb = [iota(T.xb1[:, 4 * t:4 * t + 4], [[perm[2 * t + 1] - perm[2 * t], 2], [0, 2]], perm[2 * t], 0) for t in range(4)]
-    k_ta2 = iota(T.ta[:, 64:96], [[4, 2], [0, 8], [8, 2]], 0, 1)
-    k_oh32 = iota(T.oh32[:], [[32, 8]], 0, 0)
-    k_er = iota(T.er[:], [[2, 8], [0, 2], [1, 2]], 0, 0)
-    k_z0 = fill(T.xt[:, 512:520], 0.0)
+    k_tc = [iota(T.tc[:, 0:32], [[4, 2], [0, 8], [8, 2]], 0, 1), iota(T.tc[:, 32:64], [[0, 8], [1, 2], [0, 2]], 0, 0),
+            iota(T.tc[:, 64:96], [[0, 8], [-480, 2], [128, 2]], 480, 1), iota(T.tc[:, 96:128], [[1, 32]], -32, 0)]
+    of = {n: T.ofs[:, 2 * i:2 * i + 1] for i, n in enumerate(("s1", "v1", "s2", "v2", "n1", "n2", "gl"))}
+    ofz = T.ofs[:, 16:18]
     k_zt = fill(T.zt[:], 0.0)
-    k_ones = fill(T.ones[:], 1.0)
+    k_z0 = fill(T.xt[:, 512:520], 0.0)
     k_cum = fill(T.cum[:], 0.0)
-    wait("p", [k_ones])
-    k_tri = done("p", g.affine_select(T.tri[:], T.ones[:], [[-1, 128]], A.is_gt, 0.0, 0, 1))
-
-    def bitsof(i, shift, mask):
-        d = T.ia[:, 2 * i:2 * i + 2]
-        wait("v", [k_p2])
-        if shift:
-            return done("v", g.vector.tensor_scalar(d, T.p2[:], shift, mask, A.arith_shift_right, A.bitwise_and))
-        return done("v", g.vector.tensor_scalar(d, T.p2[:], mask, None, A.bitwise_and))
-
-    def bit(i):
-        return T.ia[:, 2 * i:2 * i + 2]
-
-    of = {n: T.ofs[:, 2 * i:2 * i + 2] for i, n in enumerate(("s1", "v1", "s2", "v2", "n1", "n2", "ord", "gl", "z"))}
-    k3 = bitsof(0, 0, 3)
-    k_r2m = fill(T.r2m[:, 0:1024], 0.0)
-    k_tb = turn(T.tb[:, 0:64], T.ta[:, 0:64], k_ta)
-    k_of1 = [copy(of["s1"], bit(0), k3), ts(of["v1"], bit(0), 128.0, A.mult, 127.0, A.add)]
-    k_th1 = ts(T.th1[:], T.tb[:, 0:8], 0.5, A.add, None, None, k_tb)
-    k_mk = ts(T.mk[:], T.xa[:], T.tb[:, 32:33], A.not_equal, 2000.0, A.mult, k_xa)
-    k_xb1 = copy(T.xb1[:, 16:32], T.xb1[:, 0:16], k_xb)
+    k_ones = fill(T.ones[:], 1.0)
+    k_ofz = [fill(ofz, 128), fill(T.ofe[:], 64)]
+    k_cum2 = fill(T.cum2[:], 0.0)
+    for k in range(4):
+        k_r2m = act(T.r2m[:, 256 * k:256 * k + 256], T.zt[:], AF.Copy, k_zt)
+    k_xb1 = act(T.xb1[:, 16:32], T.xb1[:, 0:16], AF.Copy, k_xb)
+    k_tb = turn(T.tb[:], T.ta[:], k_ta)
 
     q_x = quant(T.xq[:], T.xs[:], T.xt[:], ld_x, ld_r, k_z0)
+    k_of1 = [copy(of["s1"], T.tb[:, 64:65], k_tb), ts(of["v1"], T.tb[:, 64:65], 128.0, A.mult, 127.0, A.add)]
+    k_th1 = ts(T.th1[:], T.tb[:, 0:8], 0.5, A.add, None, None)
     m_g = mm(T.pz[:, 0:128], T.xq[:, 0:128], T.xs[:, 0:128], T.xq[:, XW - 128:XW], T.xs[:, XW - 128:XW], True, True, q_x)
-    v_rm = scan(T.rm[:], T.zt[:, 0:8], T.pz[:, 120:128], -BIG, A.add, A.max, m_g, k_zt)
+    v_rm = scan(T.rm[:], T.zt[:, 0:8], T.pz[:, 120:128], -BIG, A.add, A.max, m_g)
+    k_mk = ts(T.mk[:], T.xa[:], T.tb[:, 32:33], A.not_equal, 2000.0, A.mult, k_xa)
+    k_n1 = ts(of["n1"], T.tb[:, 96:97], 0.0625, A.mult, None, None)
     a_f = act(T.js[:, 0:8], T.rm[:], AF.Sign, v_rm, scale=-1.0, bias=T.rm[:, 7:8], accum_out=T.f1[:, 0:1])
-    v_oh = ts(T.oh[:], T.xb1[:], T.f1[:, 0:1], A.is_equal, None, None, a_f, k_xb1)
-    v_m = turn(T.mr[:, 0:32], T.oh[:], v_oh)
-    bc = [copy(T.mr[0:32, 32:64], T.mr[32:64, 0:32], v_m), act(T.mr[0:32, 96:128], T.mr[96:128, 0:32], AF.Copy, v_m),
-          copy(T.mr[0:32, 64:96], T.mr[64:96, 0:32])]
-    v_c = scan(T.cum[0:32, :], T.zt[0:32, 0:128], T.mr[0:32, :], 0.0, A.add, A.add, bc, k_cum)
+    v_oh = [ts(T.oh[0:32, 32 * q:32 * q + 32], T.xb1[32 * q:32 * q + 32, :], T.f1[32 * q:32 * q + 32, 0:1], A.is_equal, None, None, a_f)
+            for q in range(4)]
+    v_m = turn(T.mr[0:32, :], T.oh[0:32, :], v_oh)
+    v_c = scan(T.cum[0:32, :], T.zt[0:32, 0:128], T.mr[0:32, :], 0.0, A.add, A.add, v_m)
 
     def lists(n, cum, th, w, jv, sv, l, lx, lt, mn, ofs, ofv, dep, consts):
         sa = [act(T.js[:, w * k:w * k + w], cum, AF.Sign, dep, consts, scale=-1.0, bias=th[:, 2 * k:2 * k + 1], accum_out=l[:, k:k + 1])
               for k in range(n)]
         pa = [ts(jv[:, w * k:w * k + w], cum, th[:, 2 * k + 1:2 * k + 2], A.is_le, 2.0, A.mult, dep, consts) for k in range(n)]
         pb = [scan(sv[:, w * k:w * k + w], T.zt[:, 0:w], jv[:, w * k:w * k + w], -float(w), A.add, A.add, pa[k]) for k in range(n)]
-        x1 = tt(lx[:, 1:32:2], sv[:].indirect(ofv[:, 0:1]), T.mk[:, 1:32:2], A.add, pb)
-        x0 = tt(lx[:, 0:32:2], l[:, 0:n].indirect(ofs[:, 0:1]), T.mk[:, 0:32:2], A.add, sa)
+        x1 = tt(lx[:, 1:32:2], sv[:].indirect(ofv), T.mk[:, 1:32:2], A.add, pb)
+        x0 = tt(lx[:, 0:32:2], l[:, 0:n].indirect(ofs), T.mk[:, 0:32:2], A.add, sa)
         t = turn(lt[0:32, :], lx[0:32, :], x0, x1)
         return [tt(mn[0:32, :], lt[0:32, 0:16], lt[0:32, 16:32], A.min, t), tt(mn[32:64, :], lt[0:32, 0:16], lt[0:32, 16:32], A.min)]
 
-    v_mn = lists(4, T.cum[:], T.th1, 128, T.jv, T.sv, T.l1, T.lx1, T.lt1, T.mn1, of["s1"], of["v1"], v_c, [k_th1, k_mk, k_of1])
+    def picks(codes, scales, win, wins, off, *deps):
+        v, a = [], []
+        for k in p["halves"]:
+            v.append(pick(codes[:, 128 * k:128 * k + 128], win, off[:, 8 * k:8 * k + 8], *deps))
+            a.append(spick(scales[:, 128 * k:128 * k + 128], wins, off[:, 8 * k:8 * k + 8], *deps))
+        return v, a
+
+    v_mn = lists(4, T.cum[:], T.th1, 128, T.jv, T.sv, T.l1, T.lx1, T.lt1, T.mn1, of["s1"], of["v1"], v_c, [])
     v_o = [ts(T.off1[64 * k:64 * k + 64, :], T.mn1[0:64, :], 0.5, A.mult, 64.0, A.add, v_mn) for k in range(2)]
     a_mn = act(T.mn1[64:128, :], T.mn1[0:64, :], AF.Copy, v_mn)
-    v_s1, a_s1 = [], []
-    for k in range(2):
-        v_s1.append(pick(T.s1c[:, 128 * k:128 * k + 128], T.xq[:], T.off1[:, 8 * k:8 * k + 8], v_o))
-        a_s1.append(spick(T.s1s[:, 128 * k:128 * k + 128], T.xs[:], T.off1[:, 8 * k:8 * k + 8], v_o))
-    kg, k0 = bitsof(1, 4, 7), bitsof(2, 0, 1)
-    c_g = copy(T.cf[:, 0:1], T.ia[:, 2:3], kg)
-    k_n1 = ts(of["n1"], bit(2), 8.0, A.mult, T.cf[:, 0:1], A.add, k0, c_g)
+    v_s1, a_s1 = picks(T.s1c, T.s1s, T.xq[:], T.xs[:], T.off1, v_o)
     v_own = pick(T.xh[:, w0:w0 + 32], T.xq[:], T.off1[:, 2 * jme:2 * jme + 2])
-    a_nt = act(T.nt[:], T.mn1[:].indirect(of["n1"][:, 0:1]), AF.Identity, a_mn, k_n1, scale=0.5, bias=64.0)
+    a_nt = act(T.nt[:], T.mn1[:].indirect(of["n1"]), AF.Identity, a_mn, scale=0.5, bias=64.0)
     a_own = spick(T.xhs[:, w0:w0 + 32], T.xs[:], T.off1[:, 2 * jme:2 * jme + 2])
 
     sent = [0]
@@ -328,75 +326,62 @@ def rank_program(g, core, T, topo):
     send_stage("1", T.s1c, T.s1s, T.xh, T.r1c, T.r1s, v_s1, a_s1)
     send("n1", "rn1", lambda first, n: T.nt[:, first:first + 1], T.rl1[:], a_nt)
 
-    q_w = quant(T.wq[:], T.ws[:], T.wt[:], ld_w)
-    z2 = quant(T.xh[:, 256:384], T.xhs[:, 256:384], T.zt[:])
-    z3 = quant(T.xh[:, 640:768], T.xhs[:, 640:768], T.zt[:])
-    nb = me - 1 if me else 1
-    for h in range(2):
-        o = 512 * h + 32 * h
-        t = act(T.r2m[:, o:o + 32], T.r2l[:, 0:32], AF.Copy, ld_2, k_r2m)
-        for c in (64, 80):
-            act(T.r2m[:, o + 4 * c:o + 4 * c + 4], T.r2l[:, 32:36], AF.Copy)
-        act(T.r2m[:, o + 4 * me:o + 4 * me + 4], T.r2l[:, 4 * nb:4 * nb + 4], AF.Copy, t)
-    t = act(T.r2m[:, 1024:1028], T.r2l[:, 32:36], AF.Copy)
-    for w in (4, 8, 16, 32, 64, 128, 256):
-        t = act(T.r2m[:, 1024 + w:1024 + 2 * w], T.r2m[:, 1024:1024 + w], AF.Copy, t)
-    a_r2 = t
-    k1, kq, kb, k32 = bitsof(3, 1, 1), bitsof(4, 0, 15), bitsof(5, 5, 3), bitsof(6, 0, 31)
-    k_tb2 = turn(T.tb[:, 64:96], T.ta[:, 64:96], k_ta2)
-    cf = {n: T.cf[:, i + 1:i + 2] for i, n in enumerate(("q", "p0", "h", "hq", "hq2", "g1", "g2", "i"))}
-    for b in range(NR):
-        fill(T.tc[32 * (b // 2):32 * (b // 2) + 32, 16 * (b % 2):16 * (b % 2) + 16], 2.0 * perm.index(b))
-    t = fill(T.tc[:, 32:64], 16.0)
-    for b in range(NR):
-        t2 = fill(T.tc[:, 32 + b:64:16], 2.0 * perm.index(b), t)
-    c_q = copy(cf["q"], T.ia[:, 8:9], kq, k1, kb, k32)
-    c_p0 = copy(cf["p0"], T.ia[:, 4:5])
-    c_h = ts(cf["h"], T.ia[:, 6:7], float(XH_H), A.mult, 128.0, A.add)
-    c_i = ts(cf["i"], T.ia[:, 12:13], -32.0, A.add, None, None)
-    c_g1 = ts(cf["g1"], T.ia[:, 6:7], -15.0, A.mult, 15.0, A.add)
-    k_of2 = [copy(of["s2"], bit(3)), ts(of["v2"], bit(3), 256.0, A.mult, 255.0, A.add), fill(of["z"], 0)]
-    k_td = turn(T.td[:], T.tc[:], t2)
-    k_th2 = ts(T.th2[:], T.tb[:, 64:68], 0.5, A.add, None, None, k_tb2)
-    c_hq = ts(cf["hq"], cf["q"], 2.0, A.mult, 2.0, A.add, c_q)
-    c_g2 = ts(cf["g2"], cf["p0"], 4.0, A.mult, cf["g1"], A.add, c_g1)
-    k_dm = ts(T.dm[:], T.er[:], cf["q"], A.is_equal, 0.5, A.mult, k_er)
-    c_hq2 = tt(cf["hq2"], cf["hq"], cf["p0"], A.subtract, c_hq)
-    k_gl = ts(of["gl"], bit(5), cf["g2"], A.add, None, None, c_g2)
-    k_n2 = ts(of["n2"], T.td[:, 0:2], cf["p0"], A.add, None, None, k_td)
-    k_ord = copy(of["ord"], T.td[:, 32:34])
-    k_ofh = ts(T.ofh[:], T.oh32[:], cf["hq2"], A.add, None, None, k_oh32, c_hq2)
-    k_xb2 = copy(T.xb2[:], T.xb1[:])
+    k_tc += [iota(T.tc[:, 128:160], [[0, 2], [1, 16]], 0, 0), iota(T.tc[:, 160:192], [[0, 2], [4, 8], [1, 2]], 2, 0),
+             iota(T.tc[:, 192:224], [[16, 2], [0, 8], [8, 2]], 0, 1)]
+    k_er = iota(T.er[:], [[2, 8], [0, 2], [1, 2]], 0, 0)
+    k_tri = done("p", g.affine_select(T.tri[:], T.ones[:], [[-1, 128]], A.is_gt, 0.0, 0, 1))
+    xb2, k_xb2 = T.xb1, []
     if me == 0:
-        for b, v in ((1, 0.0), (0, 99.0)):
-            for c in range(2):
-                k_xb2 = fill(T.xb2[:, 2 * perm.index(b) + c:32:16], v, k_xb2)
-    k_misc = [fill(T.cb[:, 16:32], 32.0), fill(T.num[:, 256:272], -1.0), fill(T.neg[:], -1.0), fill(T.cum2[:], 0.0),
-              fill(T.thr[:, 0:2], 0.0), fill(T.thr[:, 2:4], 1e-37), fill(T.d16[:], 0.0)]
+        xb2, k_xb2 = T.xb2, pairs(T.xb2, [{0: 99, 1: 0}.get(b, b) for b in perm], 2)
+    q_w = quant(T.wq[:], T.ws[:], T.wt[:], ld_w)
+    ofz1 = T.ofs[:, 16:17]
+    z2 = [pick(T.xh[:, a:a + 16], T.xq[:], ofz1) for a in (256, XH_H + 256)]
+    nb = me - 1 if me else 1
+    t = [act(T.r2m[:, 544 * h:544 * h + 32], T.r2l[:, 0:32], AF.Copy, ld_2) for h in range(2)]
+    for h in range(2):
+        for c in (64, 80):
+            act(T.r2m[:, 544 * h + 4 * c:544 * h + 4 * c + 4], T.r2l[:, 32:36], AF.Copy)
+    for h in range(2):
+        a_r2 = act(T.r2m[:, 544 * h + 4 * me:544 * h + 4 * me + 4], T.r2l[:, 4 * nb:4 * nb + 4], AF.Copy, t)
+    z2 += [spick(T.xhs[:, a:a + 16], T.xs[:], ofz1) for a in (256, XH_H + 256)]
+    k_misc = [sfill(T.d16[:], 16, 0.0), sfill(T.num[:, 256:272], 16, -1.0), sfill(T.neg[:], 16, -1.0), sfill(T.thr[:, 0:2], 2, 0.0),
+              sfill(T.thr[:, 2:4], 2, 1e-37), sfill(T.cw[:, 8:16], 8, 0.0)]
     for s in range(NR + 1):
-        k_s128 = fill(T.s128[:, 32 * s:min(32 * s + 32, 272)], 128.0 * (s % NR))
-    k_d16 = fill(T.d16[:, 0:16:8], -BIG, k_misc)
+        sfill(T.s128[:, 32 * s:min(32 * s + 32, 272)], 32 if s < NR else 16, 128.0 * (s % NR))
     q_m = quant(T.mq[:], T.ms[:], T.r2m[:], a_r2)
-    dz = [pick(T.l2c[:, w0:w0 + 32], T.xh[:, 256:384], of["z"], z2, k_of2), pick(T.l2c[:, 256:272], T.xh[:, 256:384], of["z"][:, 0:1])]
+    wait("s", [k_misc])
+    k_d16 = sfill(T.d16[:, 0:16:8], 2, -BIG)
+    k_td = turn(T.td[:], T.tc[:], k_tc)
+    q_e = [pick(T.eq[:], T.mq[:, 0:128], T.ofe[:], q_m), spick(T.es[:], T.ms[:, 0:128], T.ofe[:], q_m)]
+    k_2 = [ts(of["gl"], T.td[:, 64:65], 0.03125, A.mult, None, None, k_td), ts(T.th2[:], T.td[:, 0:4], 0.5, A.add, None, None),
+           copy(of["s2"], T.td[:, 32:33]), ts(of["v2"], T.td[:, 32:33], 256.0, A.mult, 255.0, A.add),
+           ts(T.ch[:, 0:1], T.td[:, 32:33], float(XH_H), A.mult, 128.0, A.add),
+           ts(of["n2"], T.td[:, 192:193], 0.125, A.mult, None, None),
+           ts(T.dm[:], T.er[:], T.td[:, 128:129], A.is_equal, 0.5, A.mult, k_er)]
 
     n_in = {k: arrivals(k, core, T.cores, topo) for k in KINDS}
     ready = [("c1", n_in["c1"]), ("s1", n_in["s1"]), v_own, a_own]
-    d_k = dma("y", T.lk[jme, 0:16, 0], T.cum[0:16, 127:128], v_c)
-    d_n = dma("y", T.lnd[me, 32 * ime:32 * ime + 32, 0], T.nt[32 * ime:32 * ime + 32, 1:2], a_nt)
-    d_neg = dma("y", T.lwd[me, 16 * me:16 * me + 16, 0], T.neg[0:1, :], k_misc)
-    d_c = [dma("y", T.crow[0:1, 8 * k:8 * k + 8], T.lk[4 * k:4 * k + 4, 8 * k + 2 * ime:8 * k + 2 * ime + 2, 0], ("k1", n_in["k1"]), d_k)
-           for k in range(2)]
+    d_k = dma("y", T.lk[me, 0:16, 0], T.cum[0:16, 127:128], v_c)
+    d_n = dma("y", T.lnd[me, 32 * ime:32 * ime + 32, 0], T.nt[32 * ime:32 * ime + 32, jme // 4:jme // 4 + 1], a_nt)
+    d_c = dma("y", T.crow[0:1, :], T.lk[:, 2 * jme:2 * jme + 2, 0], ("k1", n_in["k1"]), d_k)
     d_nr = dma("y", T.nrow[0:1, 0:256], T.lnd[:, 32 * ime:32 * ime + 32, 0], ("n1", n_in["n1"]), d_n)
     ld_vx = dma("y", T.vxt[:], T.vx[:])
     ld_vh = dma("y", T.vht[:], T.vh[:])
+    d_neg = dma("y", T.lwd[me, 16 * jme:16 * jme + 16, 0], T.neg[0:1, :], k_misc)
     wait("p", [d_c])
-    g_cnt = done("p", g.partition_broadcast(T.cb[:, 0:16], T.crow[0:1, :], 128))
+    g_cnt = done("p", g.partition_broadcast(T.cb[:], T.crow[0:1, :], 128))
     wait("p", [d_nr])
     g_num = done("p", g.partition_broadcast(T.num[:, 0:256], T.nrow[0:1, 0:256], 128))
+    k_oh32 = iota(T.oh32[:], [[32, 8]], 0, 0)
 
     def wmm(out, i, a, n):
         return mm(out, T.wq[:, 128 * i:128 * i + 128], T.ws[:, 128 * i:128 * i + 128], T.xh[:, a:a + n], T.xhs[:, a:a + n],
                   True, True, q_w, ready, v_rm)
+
+    col = {n: T.col[:, 2 * i:2 * i + 2] for i, n in enumerate(("e8", "sc", "F", "base"))}
+
+    def one(n, h):
+        return col[n][:, h:h + 1]
 
     mw = [wmm(T.pw[:, 512 * i:512 * i + 256], i, 0, 256) for i in range(3)]
     mw += [wmm(T.pw[:, 1536:1664], 3, 0, 128), wmm(T.pz[:, 0:128], 3, 128, 128)]
@@ -404,84 +389,78 @@ def rank_program(g, core, T, topo):
     r1 = act(T.ht[:, 1:1024:4], T.pw[:, 512:768], AF.Relu, mw[1], scale=0.0625)
     r2 = act(T.ht[:, 2:1024:4], T.pw[:, 1024:1280], AF.Relu, mw[2], scale=0.0625)
     r3b = act(T.ht[:, 515:1024:4], T.pz[:, 0:128], AF.Relu, mw[4], scale=0.0625)
-    t = ts(T.cw[:, 0:16], T.cb[:].indirect(of["ord"][:, 0:1]), 32.0, A.min, 32.0, A.subtract, g_cnt, k_ord, k_misc)
-    t = scan(T.cw[:, 16:24], T.zt[:, 0:8], T.cw[:, 0:8], 0.0, A.add, A.add, t)
-    t = copy(T.gq[:], T.cw[:].indirect(of["gl"][:, 0:1]), t, k_gl)
-    col = {n: T.col[:, 2 * i:2 * i + 2] for i, n in enumerate(("e8", "sc", "F", "base", "d"))}
-
-    def one(n, h):
-        return col[n][:, h:h + 1]
-
+    t = ts(T.cw[:, 0:8], T.cb[:, 0:16:2], 32.0, A.min, 32.0, A.subtract, g_cnt)
     r3a = ts(T.ht[:, 3:512:4], T.pw[:, 1536:1664], 0.0, A.max, 0.0625, A.mult, mw[3])
-    v_n4 = ts(T.gq[:, 6:8], T.gq[:, 0:2], -1.0, A.mult, T.cw[:, 23:24], A.add, t)
+    t = scan(T.cw[:, 16:24], T.zt[:, 0:8], T.cw[:, 0:8], 0.0, A.add, A.add, t)
     q_h = [quant(T.xh[:, XH_H:XH_H + 128], T.xhs[:, XH_H:XH_H + 128], T.ht[:, 0:512], r0, r1, r2, r3a)]
     q_h.append(quant(T.xh[:, XH_H + 128:XH_H + 256], T.xhs[:, XH_H + 128:XH_H + 256], T.ht[:, 512:1024], r3b))
-    v_b = ts(col["base"], T.gq[:, 2:4], cf["i"], A.is_le, 1024.0, A.mult, c_i)
+    t = copy(T.gq[:], T.cw[:].indirect(of["gl"]), t)
+    v_n4 = ts(T.gq[:, 6:8], T.gq[:, 0:2], -1.0, A.mult, T.cw[:, 23:24], A.add, t)
+    v_b = ts(col["base"], T.gq[:, 2:4], T.td[:, 96:97], A.is_le, 1024.0, A.mult)
     m_e, m_r = [], []
     for h in range(2):
         a = XH_H + 128 * h
         m_e.append(mm(T.pe[:, 0:128], T.xh[:, a:a + 128], T.xhs[:, a:a + 128], T.mq[:, 128 * h:128 * h + 128],
-                      T.ms[:, 128 * h:128 * h + 128], h == 0, h == 1, q_h[h], q_m))
-        m_r.append(mm(T.pe[:, 512 + 512 * h:640 + 512 * h], T.mq[:, 256:384], T.ms[:, 256:384], T.xh[:, a:a + 128], T.xhs[:, a:a + 128],
-                      True, True))
+                      T.ms[:, 128 * h:128 * h + 128], h == 0, h == 1, q_h[h]))
+        m_r.append(mm(T.pe[:, 512 + 512 * h:640 + 512 * h], T.eq[:], T.es[:], T.xh[:, a:a + 128], T.xhs[:, a:a + 128], True, True))
     row = [T.pe[:, 512 + 512 * h:640 + 512 * h] for h in range(2)]
 
     def seg(k):
         return T.lt[:, SEG * k:SEG * k + 128]
 
     f = 0.6 * 2.0 ** -23
-    v_e8 = copy(col["e8"], T.pe[:, 64:80:8], m_e[1])
-    v_r = scan(T.rr[:], T.d16[:], T.pe[:, 0:16], 0.0, A.add, A.max, k_d16)
+    v_e8 = act(col["e8"], T.pe[:, 64:80:8], AF.Copy, m_e[1])
+    a_sc = act(col["sc"], T.pe[:, 64:80:8], AF.Abs, scale=f, bias=1e-37)
+    v_l1 = ts(seg(1), row[0], one("e8", 1), A.is_le, None, None, v_e8, m_r[0])
+    v_r = scan(T.rr[:], T.d16[:], T.pe[:, 0:16], 0.0, A.add, A.max, a_sc)
     v_g4 = tt(T.g4[:], T.pe[:, 64:96:8], T.thr[:], A.is_ge)
-    a_sc = act(col["sc"], col["e8"], AF.Abs, v_e8, scale=f, bias=1e-37)
     a_c0 = act(T.cc[:, 0:128], T.tri[:], AF.Identity, a_sc, k_tri, scale=one("sc", 0), bias=one("e8", 0))
     a_sg = act(T.sg[:], row[1], AF.Sign, m_r[1], scale=-1.0, bias=one("e8", 0))
     a_c1 = act(T.cc[:, 128:256], T.tri[:], AF.Identity, scale=one("sc", 1), bias=one("e8", 1))
     a_l0 = act(seg(0), T.sg[:], AF.Relu, a_sg)
     for h in range(2):
         a_f = act(T.js[:, 8 * h:8 * h + 8], T.rr[:, 8 * h:8 * h + 8], AF.Sign, v_r, scale=-1.0, bias=T.rr[:, 8 * h + 7:8 * h + 8], accum_out=one("F", h))
-    v_l1 = ts(seg(1), row[0], one("e8", 1), A.is_le, None, None, v_e8, m_r[0])
-    v_co = tt(T.lt[:, 128:4 * SEG:SEG], T.g4[:], T.gq[:, 4:8], A.mult, v_g4, v_n4)
     v_l2 = tt(seg(2), row[0], T.cc[:, 0:128], A.is_lt, a_c0)
+    v_co = tt(T.lt[:, 128:4 * SEG:SEG], T.g4[:], T.gq[:, 4:8], A.mult, v_g4)
     v_l3 = tt(seg(3), row[1], T.cc[:, 128:256], A.is_lt, a_c1)
     v_a = []
     for h in (0, 1):
         v_a.append(scan(T.sa[:, SEG * h:SEG * h + 129], T.lt[:, SEG * h:SEG * h + 129], T.lt[:, SEG * (2 + h):SEG * (2 + h) + 129],
-                        one("base", h), A.add, A.add, v_b, v_co, (a_l0, v_l3)[h], v_l2))
-    v_d = ts(col["d"], T.sa[:, 128:2 * SEG:SEG], DF - 0.5, A.is_lt, None, None, v_a)
-    v_v = [ts(T.tvv[:, 32 * h:32 * h + 32], T.xb2[:], one("F", h), A.is_equal, one("d", h), A.mult, v_d, a_f, k_xb2) for h in range(2)]
+                        one("base", h), A.add, A.add, v_co, (a_l0, v_l3)[h]))
+    v_g = [ts(T.gw[:, 32 * h:32 * h + 32], xb2[:], one("F", h), A.is_equal, DF - 0.5, A.mult, a_f, k_xb2) for h in range(2)]
+    v_v = [ts(T.tvv[:, 32 * h:32 * h + 32], T.gw[:, 32 * h:32 * h + 32], T.sa[:, SEG * h + 128:SEG * h + 129], A.is_gt, None, None, v_g[h])
+           for h in range(2)]
     v_t = [turn(T.m2[:, 128 * h:128 * h + 32], T.tvv[:, 32 * h:32 * h + 32], v_v[h]) for h in range(2)]
     bc = []
     for q in range(1, 4):
         bc.append(act(T.m2[0:32, 32 * q:32 * q + 32], T.m2[32 * q:32 * q + 32, 0:32], AF.Copy, v_t[0]))
         bc.append(copy(T.m2[0:32, 128 + 32 * q:160 + 32 * q], T.m2[32 * q:32 * q + 32, 128:160], v_t[1]))
     v_c2 = scan(T.cum2[0:32, :], T.zt[0:32, 0:256], T.m2[0:32, :], 0.0, A.add, A.add, bc)
-    v_mn = lists(2, T.cum2[:], T.th2, 256, T.jv2, T.sv2, T.l2, T.lx2, T.lt2, T.mn2, of["s2"], of["v2"], v_c2, [k_th2, k_of2])
-    v_o = [ts(T.off2[64 * k:64 * k + 64, :], T.mn2[0:64, :], 0.5, A.mult, T.cf[0:64, 3:4], A.add, v_mn, c_h) for k in range(2)]
+    v_mn = lists(2, T.cum2[:], T.th2, 256, T.jv2, T.sv2, T.l2, T.lx2, T.lt2, T.mn2, of["s2"], of["v2"], v_c2, [])
+    v_o = [ts(T.off2[64 * k:64 * k + 64, :], T.mn2[0:64, :], 0.5, A.mult, T.ch[0:64, 0:1], A.add, v_mn) for k in range(2)]
     a_mn = act(T.mn2[64:128, :], T.mn2[0:64, :], AF.Copy, v_mn)
-    v_s2, a_s2 = [], []
-    for k in range(2):
-        v_s2.append(pick(T.s2c[:, 128 * k:128 * k + 128], T.xh[:], T.off2[:, 8 * k:8 * k + 8], v_o, z3))
-        a_s2.append(spick(T.s2s[:, 128 * k:128 * k + 128], T.xhs[:], T.off2[:, 8 * k:8 * k + 8], v_o))
-    t = ts(T.offw[:], T.mn2[:].indirect(of["n2"][:, 0:1]), 0.5, A.mult, 128.0, A.add, a_mn, k_n2)
-    t = [tt(T.wa[:], T.s128[:].indirect(T.offw[:, 0:2]), T.dm[:], A.mult, t, k_s128, k_dm),
+    v_s2, a_s2 = picks(T.s2c, T.s2s, T.xh[:], T.xhs[:], T.off2, v_o)
+    t = ts(T.offw[:], T.mn2[:].indirect(of["n2"]), 0.5, A.mult, 128.0, A.add, a_mn)
+    t = [tt(T.wa[:], T.s128[:].indirect(T.offw[:, 0:2]), T.dm[:], A.mult, t),
          tt(T.wb[:], T.num[:].indirect(T.offw[:, 0:2]), T.dm[:], A.mult, g_num)]
     v_w = scan(T.wc[:], T.wa[:], T.wb[:], 0.0, A.add, A.add, t)
     send_stage("2", T.s2c, T.s2s, T.l2c, T.r2c, T.r2s, v_s2, a_s2)
     send("n2", "rn2", lambda first, n: T.wc[:, 31:32], T.rl2[:], v_w)
     q_vx = quant(T.vxq[:], T.vxs[:], T.vxt[:], ld_vx)
     q_vh = quant(T.vhq[:], T.vhs[:], T.vht[:], ld_vh)
-    dz += [spick(T.l2s[:, w0:w0 + 32], T.xhs[:, 256:384], of["z"]), spick(T.l2s[:, 256:272], T.xhs[:, 256:384], of["z"][:, 0:1])]
+    k_ofh = ts(T.ofh[:], T.oh32[:], T.td[:, 160:161], A.add, None, None, k_oh32)
+    dz = [pick(T.l2c[:, w0:w0 + 32], T.xq[:], ofz), pick(T.l2c[:, 256:272], T.xq[:], ofz1),
+          spick(T.l2s[:, w0:w0 + 32], T.xs[:], ofz), spick(T.l2s[:, 256:272], T.xs[:], ofz1)]
 
     ready = [("c2", n_in["c2"]), ("s2", n_in["s2"]), dz]
     out = (T.pz[:, 0:128], T.pw[:, 512:640])
     my = []
     for k in range(2):
         a = 128 * k
-        mm(out[k], T.vxq[:], T.vxs[:], T.l2c[:, a:a + 128], T.l2s[:, a:a + 128], True, False, ready, q_vx, q_vh)
+        mm(out[k], T.vxq[:], T.vxs[:], T.l2c[:, a:a + 128], T.l2s[:, a:a + 128], True, False, ready)
         my.append(mm(out[k], T.vhq[:], T.vhs[:], T.l2c[:, a + 2:a + 130], T.l2s[:, a + 2:a + 130], False, True))
-    a_hp = spick(T.hps[:], T.l2s[:, 0:256], T.ofh[:], ready, k_ofh)
-    v_hp = pick(T.hp[:], T.l2c[:, 0:256], T.ofh[:], ready, k_ofh)
+    a_hp = spick(T.hps[:], T.l2s[:, 0:256], T.ofh[:], ready)
+    v_hp = pick(T.hp[:], T.l2c[:, 0:256], T.ofh[:], ready)
     for k in range(2):
         for r in range(2):
             v_y = copy(T.ys[:, 64 * k + r:64 * k + 64:2], out[k][:, r:128:4], my[k])
@@ -489,6 +468,6 @@ def rank_program(g, core, T, topo):
     dma("y", T.y[:], T.ys[:], v_y)
     for k in range(4):
         dma("s", T.osc[4 * k:4 * k + 4, 0:128], T.hps[32 * k:32 * k + 4, 0:128], a_hp)
-    dma("s", T.who[0:1, 0:128], T.lwd[:, 16 * me:16 * me + 16, 0], ("n2", n_in["n2"]), d_neg)
+    dma("s", T.who[0:1, 0:128], T.lwd[:, 16 * jme:16 * jme + 16, 0], ("n2", n_in["n2"]), d_neg)
     g.wait_ge(T.sem.sent, sent[0])
     wait("p", [(s, everything[s]) for s in everything])

@@ -14,33 +14,34 @@ def _sb(w, d):
 
 
 SCRATCH = {
-    "xt": _sb(4 * XW, BF), "wt": _sb(2048, BF), "r2l": _sb(48, BF), "r2m": _sb(1024, BF),
+    "xt": _sb(4 * XW, BF), "wt": _sb(2048, BF), "r2l": _sb(48, BF), "r2m": _sb(512, BF),
     "vxt": _sb(512, BF), "vht": _sb(512, BF), "zt": _sb(256, BF), "ht": _sb(1024, BF),
-    "xq": _sb(XW, F8), "xs": _sb(XW, U8), "wq": _sb(512, F8), "ws": _sb(512, U8), "mq": _sb(256, F8), "ms": _sb(256, U8),
+    "xq": _sb(XW, F8), "xs": _sb(XW, U8), "wq": _sb(512, F8), "ws": _sb(512, U8), "mq": _sb(128, F8), "ms": _sb(128, U8),
     "eq": _sb(128, F8), "es": _sb(128, U8), "vxq": _sb(128, F8), "vxs": _sb(128, U8), "vhq": _sb(128, F8), "vhs": _sb(128, U8),
     "s1c": _sb(256, F8), "s1s": _sb(256, U8), "r1c": _sb(64, F8), "r1s": _sb(64, U8), "xh": _sb(544, F8), "xhs": _sb(544, U8),
     "s2c": _sb(256, F8), "s2s": _sb(256, U8), "r2c": _sb(64, F8), "r2s": _sb(64, U8), "l2c": _sb(272, F8), "l2s": _sb(272, U8),
     "hp": _sb(128, F8), "hps": _sb(128, U8),
     "rlk": ("dram", [128, 1], BF), "lk": ("dram", [8, 128, 1], BF), "rl1": ("dram", [128, 1], BF), "lnd": ("dram", [8, 128, 1], BF),
     "rl2": ("dram", [128, 1], F32), "lwd": ("dram", [8, 128, 1], F32),
-    "ofs": _sb(24, U16), "ofh": _sb(8, U16), "ofe": _sb(8, U16), "ta": _sb(128, F32), "tb": _sb(128, F32), "tc": _sb(224, F32),
-    "td": _sb(224, F32), "ch": _sb(2, F32), "th1": _sb(8, F32), "th2": _sb(4, F32), "xa": _sb(32, F32), "xb1": _sb(32, F32),
+    "ofs": _sb(24, U16), "ofh": _sb(8, U16), "ofe": _sb(8, U16), "ta": _sb(96, F32), "tb": _sb(96, F32), "tc": _sb(192, F32),
+    "td": _sb(192, F32), "ch": _sb(2, F32), "th1": _sb(8, F32), "th2": _sb(4, F32), "xa": _sb(32, F32), "xb1": _sb(32, F32),
     "xb2": _sb(32, F32), "mk": _sb(32, F32), "ones": _sb(128, BF), "tri": _sb(128, BF), "oh32": _sb(8, F32),
-    "er": _sb(32, F32), "dm": _sb(32, F32), "s128": _sb(272, BF), "neg": _sb(16, F32), "d16": _sb(16, F32), "thr": _sb(4, F32),
+    "er": _sb(32, F32), "dm": _sb(32, F32), "s128": _sb(272, BF), "neg": _sb(16, F32),
     "rm": _sb(8, F32), "f1": _sb(8, F32), "oh": _sb(128, BF), "mr": _sb(128, BF), "cum": _sb(128, BF),
-    "js": _sb(1024, BF), "jv": _sb(512, BF), "sv": _sb(512, BF), "l1": _sb(8, F32), "lx1": _sb(32, F32), "lt1": _sb(32, F32),
+    "js": _sb(1024, BF), "jv": _sb(8 * 132, BF), "sv": _sb(8 * 132, BF), "dp": _sb(132, BF), "lt1": _sb(32, BF),
     "mn1": _sb(16, F32), "off1": _sb(16, U16), "nt": _sb(16, BF),
-    "crow": _sb(16, BF), "cb": _sb(16, BF), "cw": _sb(24, F32), "gq": _sb(16, F32), "nrow": _sb(256, BF), "num": _sb(272, BF),
-    "col": _sb(16, F32), "g4": _sb(4, F32), "gw": _sb(64, F32), "cc": _sb(256, F32), "lt": _sb(4 * SEG, BF), "sg": _sb(128, BF),
-    "sa": _sb(2 * SEG, BF), "rr": _sb(16, F32), "tvv": _sb(64, BF), "m2": _sb(256, BF), "cum2": _sb(256, BF), "jv2": _sb(512, BF),
+    "crow": _sb(16, BF), "cb": _sb(16, BF), "cw": _sb(32, F32),
+    "gq": _sb(16, F32), "nrow": _sb(256, BF), "num": _sb(272, BF),
+    "col": _sb(16, F32), "gw": _sb(64, F32), "cc": _sb(256, F32), "lt": _sb(4 * SEG, BF), "sg": _sb(128, BF),
+    "sa": _sb(2 * SEG, BF), "rr": _sb(16, F32), "tvv": _sb(160, BF), "m2": _sb(256, BF), "cum2": _sb(256, BF), "jv2": _sb(512, BF),
     "sv2": _sb(512, BF), "l2": _sb(8, F32), "lx2": _sb(32, F32), "lt2": _sb(32, F32), "mn2": _sb(16, F32), "off2": _sb(16, U16),
     "offw": _sb(16, U16), "wa": _sb(32, F32), "wb": _sb(32, F32), "wc": _sb(32, F32),
     "ys": _sb(128, F32),
     "pw": ("psum", [128, 2048], F32), "pe": ("psum", [128, 1536], F32), "pz": ("psum", [128, 512], F32),
 }
 NDMA = 30
-KINDS = ("k1", "c1", "s1", "n1", "c2", "s2", "n2")
-SEMAPHORES = ["kv", "ks", "kt", "kp", "sent"] + list(KINDS) + ["r" + k for k in KINDS] + ["d%d" % i for i in range(NDMA)]
+SEMAPHORES = (["kv", "ks", "kt", "kp", "sent", "k1", "c1", "n1", "c2", "n2", "rk1", "rc1", "rs1", "rn1", "rc2", "rs2", "rn2"]
+              + ["d%d" % i for i in range(NDMA)])
 
 
 def split(engines, parts):
@@ -71,18 +72,18 @@ def plan(src, cores, topo):
 
     on = {}
     for k in range(2):
-        f2, n2 = far[2 * k:2 * k + 2], [d for d in near[2 * k:2 * k + 2] if d != src]
+        f2, j = far[2 * k:2 * k + 2], order.index(direct[k])
         on[a[k]] = [("k1", fan(a[k], f2[:1])), ("c1", fan(a[k], f2, jf + 2 * k)), ("c2", fan(a[k], f2, jf + 2 * k))]
         on[b[k]] = [("k1", fan(b[k], f2[1:])), ("s1", fan(b[k], f2, jf + 2 * k)), ("s2", fan(b[k], f2, jf + 2 * k))]
-        on[c[k]] = [("k1", fan(c[k], n2)), ("s1", fan(c[k], n2, jn + 2 * k)), ("s2", fan(c[k], n2, jn + 2 * k))]
+        on[c[k]] = [("k1", fan(c[k], direct[k::2])), ("s1", fan(c[k], direct[k:k + 1], j)), ("s2", fan(c[k], direct[k:k + 1], j))]
     on[b[0]].insert(2, ("n1", fan(b[0], far)))
     on[c[0]].insert(2, ("n1", fan(c[0], direct)))
     on[b[1]].append(("n2", fan(b[1], far + direct)))
-    q4, h2, o2, u2, o4 = split(every, 4), split(every, 2), split(off, 2), split(up, 2), split(off, 4)
+    h2, q4, u2 = split(every, 2), split(every, 4), split(up, 2)
     out = {"ka": [(h, q4[i], 0, 0) for i, h in enumerate(a + b)], "kb": [(h, h2[i], 0, 0) for i, h in enumerate(c)],
-           "c": [(h, h2[i], jf + 2 * i, 2) for i, h in enumerate(a)],
-           "s": [(h, o2[i], jf + 2 * i, 2) for i, h in enumerate(b)] + [(h, u2[i], jn + 2 * i, 2) for i, h in enumerate(c)],
-           "d": [(d, (o2[0], o4[2], o4[3])[i], order.index(d), 1) for i, d in enumerate(direct)],
+           "c": [(h, every, jf + 2 * i, 2) for i, h in enumerate(a)], "s": [(h, every, jf + 2 * i, 2) for i, h in enumerate(b)],
+           "sn": [(h, h2[i], order.index(direct[i]), 1) for i, h in enumerate(c)],
+           "dc": [(d, off, order.index(d), 1) for d in direct], "ds": [(direct[2], off, order.index(direct[2]), 1)],
            "n1": [(b[0], u2[0], jf // 4, 0), (c[0], u2[1], jn // 4, 0)], "n2": [(b[1], up, 0, 0)]}
     return {"order": order, "out": out, "on": on, "halves": (jf // 4, jn // 4)}
 
@@ -99,8 +100,8 @@ def arrivals(kind, core, cores, topo):
     for s in cores:
         if s != core:
             p = plan(s, cores, topo)
-            if kind[0] == "c":
-                n += sum(len(e) for d, e, x, y in p["out"]["d"] if d == core)
+            if kind[0] in "cs":
+                n += sum(len(e) for d, e, x, y in p["out"]["d" + kind[0]] if d == core)
             for h in p["on"]:
                 n += sum(len(e) for k, ws in p["on"][h] if k == kind for d, e, x in ws if d == core)
     return n
@@ -125,7 +126,7 @@ def helper_program(g, core, T, topo):
         return t[:, 32 * b:32 * b + 32]
 
     for kind, writes in p["on"][core]:
-        keys = {"k": ("ka", "kb"), "c": ("c",), "s": ("s",), "n": (kind,)}[kind[0]]
+        keys = {"k": ("ka", "kb"), "c": ("c",), "s": ("s", "sn"), "n": (kind,)}[kind[0]]
         g.wait_ge(T.sem["r" + kind], sum(len(e) for k in keys for h, e, x, y in p["out"][k] if h == core))
         tr = []
         for d, e, k in writes:
@@ -138,7 +139,7 @@ def helper_program(g, core, T, topo):
             else:
                 a, b = (columns(T.r1c, k), columns(T.xh, s)) if kind == "c1" else (columns(T.r2c, k), columns(T.l2c, s))
                 a, b = a.bitcast(dt.uint8), b.bitcast(dt.uint8)
-            tr.append(transfer(core, d, e, T.sem[kind], a, b, topo))
+            tr.append(transfer(core, d, e, T.sem[kind.replace("s", "c")], a, b, topo))
             sent += len(e)
         g.remote_dma_fused(tr, local_sem=T.sem.sent)
     g.wait_ge(T.sem.sent, sent)
@@ -237,65 +238,76 @@ def rank_program(g, core, T, topo):
     def spick(out, win, off, *deps):
         return act(out, win.indirect(off), AF.Copy, *deps)
 
-    def pairs(out, vals, halves):
-        return [iota(out[:, 16 * m + 4 * t:16 * m + 4 * t + 4], [[vals[2 * t + 1] - vals[2 * t], 2], [0, 2]], vals[2 * t], 0)
-                for m in range(halves) for t in range(4)]
-
     ld_x = dma("y", T.xt[:, 0:512], T.x[:])
     ld_r = dma("s", T.xt[:, 520:552], T.rt[:, 0:32])
     ld_w = dma("y", T.wt[:], T.w[:], ld_x)
     ld_2 = dma("y", T.r2l[:, 0:36], T.r2[:, 0:36])
 
     k_ta = [iota(T.ta[:, 0:32], [[8, 2], [0, 8], [16, 2]], 0, 1), iota(T.ta[:, 32:64], [[1, 2], [0, 16]], 0, 0),
-            iota(T.ta[:, 64:96], [[0, 8], [1, 4]], 0, 0), iota(T.ta[:, 96:128], [[16, 2], [0, 8], [128, 2]], 0, 1)]
-    k_xb = pairs(T.xb1, perm, 1)
+            iota(T.ta[:, 64:96], [[16, 2], [0, 8], [128, 2]], 0, 1)]
     k_xa = iota(T.xa[:], [[0, 2], [1, 2], [0, 8]], 0, 0)
-    k_tc = [iota(T.tc[:, 0:32], [[4, 2], [0, 8], [8, 2]], 0, 1), iota(T.tc[:, 32:64], [[0, 8], [1, 2], [0, 2]], 0, 0),
-            iota(T.tc[:, 64:96], [[0, 8], [-480, 2], [128, 2]], 480, 1), iota(T.tc[:, 96:128], [[1, 32]], -32, 0)]
-    of = {n: T.ofs[:, 2 * i:2 * i + 1] for i, n in enumerate(("s1", "v1", "s2", "v2", "n1", "n2", "gl"))}
+    k_tc = [iota(T.tc[:, 0:32], [[16, 2], [0, 8], [8, 2]], 0, 1), iota(T.tc[:, 32:64], [[0, 8], [1, 2], [0, 2]], 0, 0),
+            iota(T.tc[:, 96:128], [[1024, 32]], -31 * 1024, 0)]
+    k_tc += [iota(T.tc[:, 64 + 16 * m:80 + 16 * m], [[-480, 4], [256, 2], [128, 2]], 480, 1) for m in range(2)]
+    k_tc += [iota(T.tc[:, 128:160], [[0, 2], [1, 16]], 0, 0), iota(T.tc[:, 160:192], [[0, 2], [4, 8], [1, 2]], 2, 0)]
+    k_er = iota(T.er[:], [[2, 8], [0, 2], [1, 2]], 0, 0)
+    of = {n: T.ofs[:, 2 * i:2 * i + 1] for i, n in enumerate(("s2", "v2", "n1", "n2", "gl"))}
     ofz = T.ofs[:, 16:18]
     k_zt = fill(T.zt[:], 0.0)
     k_z0 = fill(T.xt[:, 512:520], 0.0)
     k_cum = fill(T.cum[:], 0.0)
     k_ones = fill(T.ones[:], 1.0)
-    k_ofz = [fill(ofz, 128), fill(T.ofe[:], 64)]
-    k_cum2 = fill(T.cum2[:], 0.0)
+    k_ofz = [fill(ofz, 128), fill(T.ofe[:], 8)]
+    fill(T.dp[:, 0:128], 0.0)
     for k in range(4):
+        fill(T.jv[:, 128 + k:8 * 132:132], 0.0)
+    k_cum2 = fill(T.cum2[:], 0.0)
+    wait("p", [k_ones])
+    k_tri = done("p", g.affine_select(T.tri[:], T.ones[:], [[-1, 128]], A.is_gt, 0.0, 0, 1))
+    for k in range(2):
         k_r2m = act(T.r2m[:, 256 * k:256 * k + 256], T.zt[:], AF.Copy, k_zt)
-    k_xb1 = act(T.xb1[:, 16:32], T.xb1[:, 0:16], AF.Copy, k_xb)
+    tabs = [(T.xb1, perm)] + ([] if me else [(T.xb2, [{0: 99, 1: 0}.get(b, b) for b in perm])])
+    for tab, vals in tabs:
+        t = [sfill(tab[:, 2 * j:2 * j + 2], 2, float(vals[j])) for j in range(NR)]
+    k_cw = sfill(T.cw[:, 8:16], 8, 0.0)
+    for tab, vals in tabs:
+        act(tab[:, 16:32], tab[:, 0:16], AF.Copy, t)
+    xb2 = tabs[-1][0]
     k_tb = turn(T.tb[:], T.ta[:], k_ta)
 
-    q_x = quant(T.xq[:], T.xs[:], T.xt[:], ld_x, ld_r, k_z0)
-    k_of1 = [copy(of["s1"], T.tb[:, 64:65], k_tb), ts(of["v1"], T.tb[:, 64:65], 128.0, A.mult, 127.0, A.add)]
-    k_th1 = ts(T.th1[:], T.tb[:, 0:8], 0.5, A.add, None, None)
+    q_x = quant(T.xq[:], T.xs[:], T.xt[:], k_z0, ld_r, ld_x)
+    k_th1 = ts(T.th1[:], T.tb[:, 0:8], 0.5, A.add, None, None, k_tb)
+    ts(T.dp[:, 128:129], T.tb[:, 32:33], 2048.0, A.mult, None, None)
+    ts(T.dp[:, 129:132:2], T.tb[:, 32:34], -4096.0, A.mult, 2048.0, A.add)
     m_g = mm(T.pz[:, 0:128], T.xq[:, 0:128], T.xs[:, 0:128], T.xq[:, XW - 128:XW], T.xs[:, XW - 128:XW], True, True, q_x)
     v_rm = scan(T.rm[:], T.zt[:, 0:8], T.pz[:, 120:128], -BIG, A.add, A.max, m_g)
-    k_mk = ts(T.mk[:], T.xa[:], T.tb[:, 32:33], A.not_equal, 2000.0, A.mult, k_xa)
-    k_n1 = ts(of["n1"], T.tb[:, 96:97], 0.0625, A.mult, None, None)
+    ts(T.dp[:, 130:131], T.tb[:, 32:33], 4096.0, A.mult, -2048.0, A.add)
+    k_n1 = ts(of["n1"], T.tb[:, 64:65], 0.0625, A.mult, None, None)
     a_f = act(T.js[:, 0:8], T.rm[:], AF.Sign, v_rm, scale=-1.0, bias=T.rm[:, 7:8], accum_out=T.f1[:, 0:1])
     v_oh = [ts(T.oh[0:32, 32 * q:32 * q + 32], T.xb1[32 * q:32 * q + 32, :], T.f1[32 * q:32 * q + 32, 0:1], A.is_equal, None, None, a_f)
             for q in range(4)]
     v_m = turn(T.mr[0:32, :], T.oh[0:32, :], v_oh)
     v_c = scan(T.cum[0:32, :], T.zt[0:32, 0:128], T.mr[0:32, :], 0.0, A.add, A.add, v_m)
 
-    def lists(n, cum, th, w, jv, sv, l, lx, lt, mn, ofs, ofv, dep, consts):
-        sa = [act(T.js[:, w * k:w * k + w], cum, AF.Sign, dep, consts, scale=-1.0, bias=th[:, 2 * k:2 * k + 1], accum_out=l[:, k:k + 1])
-              for k in range(n)]
-        pa = [ts(jv[:, w * k:w * k + w], cum, th[:, 2 * k + 1:2 * k + 2], A.is_le, 2.0, A.mult, dep, consts) for k in range(n)]
-        pb = [scan(sv[:, w * k:w * k + w], T.zt[:, 0:w], jv[:, w * k:w * k + w], -float(w), A.add, A.add, pa[k]) for k in range(n)]
-        x1 = tt(lx[:, 1:32:2], sv[:].indirect(ofv), T.mk[:, 1:32:2], A.add, pb)
-        x0 = tt(lx[:, 0:32:2], l[:, 0:n].indirect(ofs), T.mk[:, 0:32:2], A.add, sa)
-        t = turn(lt[0:32, :], lx[0:32, :], x0, x1)
-        return [tt(mn[0:32, :], lt[0:32, 0:16], lt[0:32, 16:32], A.min, t), tt(mn[32:64, :], lt[0:32, 0:16], lt[0:32, 16:32], A.min)]
-
     def picks(codes, scales, win, wins, off, *deps):
         v, a = [], []
-        for k in p["halves"]:
-            v.append(pick(codes[:, 128 * k:128 * k + 128], win, off[:, 8 * k:8 * k + 8], *deps))
-            a.append(spick(scales[:, 128 * k:128 * k + 128], wins, off[:, 8 * k:8 * k + 8], *deps))
+        far, near = p["halves"]
+        for k, n in ((8 * far, 4), (8 * far + 4, 4), (8 * near, 8)):
+            v.append(pick(codes[:, 16 * k:16 * (k + n)], win, off[:, k:k + n], *deps))
+            a.append(spick(scales[:, 16 * k:16 * (k + n)], wins, off[:, k:k + n], *deps))
         return v, a
 
-    v_mn = lists(4, T.cum[:], T.th1, 128, T.jv, T.sv, T.l1, T.lx1, T.lt1, T.mn1, of["s1"], of["v1"], v_c, [])
+    fl = []
+    for v in range(8):
+        o = T.jv[0:32, 132 * v:132 * v + 128]
+        if v < 4:
+            fl.append(ts(o, T.cum[0:32, :], T.th1[0:32, v:v + 1], A.is_le, 2.0, A.mult, v_c))
+        else:
+            fl.append(act(o, T.cum[0:32, :], AF.Sign, v_c, scale=-1.0, bias=T.th1[0:32, v:v + 1]))
+    for v in range(8):
+        t = scan(T.sv[0:32, v:8 * 132:8], T.dp[0:32, :], T.jv[0:32, 132 * v:132 * v + 132], -128.0 if v < 4 else 0.0, A.add, A.add, fl[v])
+    t = turn(T.lt1[0:32, :], T.sv[0:32, 1024:1056], t)
+    v_mn = [tt(T.mn1[32 * k:32 * k + 32, :], T.lt1[0:32, 0:16], T.lt1[0:32, 16:32], A.min, t) for k in range(2)]
     v_o = [ts(T.off1[64 * k:64 * k + 64, :], T.mn1[0:64, :], 0.5, A.mult, 64.0, A.add, v_mn) for k in range(2)]
     a_mn = act(T.mn1[64:128, :], T.mn1[0:64, :], AF.Copy, v_mn)
     v_s1, a_s1 = picks(T.s1c, T.s1s, T.xq[:], T.xs[:], T.off1, v_o)
@@ -305,138 +317,167 @@ def rank_program(g, core, T, topo):
 
     sent = [0]
 
-    def send(key, kind, src_of, dst, *deps):
+    def send(writes, kind, src_of, dst, *deps):
         wait("p", deps)
         tr = []
-        for to, e, first, n in p["out"][key]:
+        for to, e, first, n in writes:
             tr.append(transfer(core, to, e, T.sem[kind], src_of(first, n), dst, topo))
             sent[0] += len(e)
         g.remote_dma_fused(tr, local_sem=T.sem.sent)
 
-    def send_stage(st, codes, scales, land, relay_c, relay_s, dep_c, dep_s):
+    def send_stage(st, codes, scales, land, land_s, relay_c, relay_s, dep_c, dep_s):
         def c_src(first, n):
             return codes[:, 32 * first:32 * (first + n)].bitcast(dt.uint8)
 
-        send("c", "rc" + st, c_src, relay_c[:].bitcast(dt.uint8), dep_c[0])
-        send("s", "rs" + st, lambda first, n: scales[:, 32 * first:32 * (first + n)], relay_s[:], dep_s)
-        send("d", "c" + st, c_src, land[:, w0:w0 + 32].bitcast(dt.uint8), dep_c)
+        def s_src(first, n):
+            return scales[:, 32 * first:32 * (first + n)]
+
+        o = p["out"]
+        for k in range(2):
+            send(o["c"][k:k + 1], "rc" + st, c_src, relay_c[:].bitcast(dt.uint8), dep_c[k])
+            send(o["s"][k:k + 1], "rs" + st, s_src, relay_s[:], dep_s[k])
+        send(o["sn"], "rs" + st, s_src, relay_s[:, 0:32], dep_s)
+        for k in range(3):
+            send(o["dc"][k:k + 1], "c" + st, c_src, land[:, w0:w0 + 32].bitcast(dt.uint8), dep_c)
+        send(o["ds"], "c" + st, s_src, land_s[:, w0:w0 + 32])
 
     for key in ("ka", "kb"):
-        send(key, "rk1", lambda first, n: T.cum[:, 127:128], T.rlk[:], v_c)
-    send_stage("1", T.s1c, T.s1s, T.xh, T.r1c, T.r1s, v_s1, a_s1)
-    send("n1", "rn1", lambda first, n: T.nt[:, first:first + 1], T.rl1[:], a_nt)
+        send(p["out"][key], "rk1", lambda first, n: T.cum[:, 127:128], T.rlk[:], v_c)
+    send_stage("1", T.s1c, T.s1s, T.xh, T.xhs, T.r1c, T.r1s, v_s1, a_s1)
+    send(p["out"]["n1"], "rn1", lambda first, n: T.nt[:, first:first + 1], T.rl1[:], a_nt)
 
-    k_tc += [iota(T.tc[:, 128:160], [[0, 2], [1, 16]], 0, 0), iota(T.tc[:, 160:192], [[0, 2], [4, 8], [1, 2]], 2, 0),
-             iota(T.tc[:, 192:224], [[16, 2], [0, 8], [8, 2]], 0, 1)]
-    k_er = iota(T.er[:], [[2, 8], [0, 2], [1, 2]], 0, 0)
-    k_tri = done("p", g.affine_select(T.tri[:], T.ones[:], [[-1, 128]], A.is_gt, 0.0, 0, 1))
-    xb2, k_xb2 = T.xb1, []
-    if me == 0:
-        xb2, k_xb2 = T.xb2, pairs(T.xb2, [{0: 99, 1: 0}.get(b, b) for b in perm], 2)
     q_w = quant(T.wq[:], T.ws[:], T.wt[:], ld_w)
     ofz1 = T.ofs[:, 16:17]
     z2 = [pick(T.xh[:, a:a + 16], T.xq[:], ofz1) for a in (256, XH_H + 256)]
     nb = me - 1 if me else 1
-    t = [act(T.r2m[:, 544 * h:544 * h + 32], T.r2l[:, 0:32], AF.Copy, ld_2) for h in range(2)]
-    for h in range(2):
-        for c in (64, 80):
-            act(T.r2m[:, 544 * h + 4 * c:544 * h + 4 * c + 4], T.r2l[:, 32:36], AF.Copy)
-    for h in range(2):
-        a_r2 = act(T.r2m[:, 544 * h + 4 * me:544 * h + 4 * me + 4], T.r2l[:, 4 * nb:4 * nb + 4], AF.Copy, t)
+    t = act(T.r2m[:, 0:36], T.r2l[:, 0:36], AF.Copy, ld_2)
     z2 += [spick(T.xhs[:, a:a + 16], T.xs[:], ofz1) for a in (256, XH_H + 256)]
-    k_misc = [sfill(T.d16[:], 16, 0.0), sfill(T.num[:, 256:272], 16, -1.0), sfill(T.neg[:], 16, -1.0), sfill(T.thr[:, 0:2], 2, 0.0),
-              sfill(T.thr[:, 2:4], 2, 1e-37), sfill(T.cw[:, 8:16], 8, 0.0)]
+    k_misc = [sfill(T.num[:, 256:272], 16, -1.0), sfill(T.neg[:], 16, -1.0)]
+    a_r2 = act(T.r2m[:, 4 * me:4 * me + 4], T.r2l[:, 4 * nb:4 * nb + 4], AF.Copy, t)
     for s in range(NR + 1):
         sfill(T.s128[:, 32 * s:min(32 * s + 32, 272)], 32 if s < NR else 16, 128.0 * (s % NR))
     q_m = quant(T.mq[:], T.ms[:], T.r2m[:], a_r2)
-    wait("s", [k_misc])
-    k_d16 = sfill(T.d16[:, 0:16:8], 2, -BIG)
-    k_td = turn(T.td[:], T.tc[:], k_tc)
+    k_tg = turn(T.td[:], T.tc[:], k_tc)
     q_e = [pick(T.eq[:], T.mq[:, 0:128], T.ofe[:], q_m), spick(T.es[:], T.ms[:, 0:128], T.ofe[:], q_m)]
-    k_2 = [ts(of["gl"], T.td[:, 64:65], 0.03125, A.mult, None, None, k_td), ts(T.th2[:], T.td[:, 0:4], 0.5, A.add, None, None),
+    k_2 = [ts(of["gl"], T.td[:, 64:65], 0.03125, A.mult, None, None, k_tg), ts(T.th2[:], T.tb[:, 0:8:2], 0.5, A.mult, 0.5, A.add),
            copy(of["s2"], T.td[:, 32:33]), ts(of["v2"], T.td[:, 32:33], 256.0, A.mult, 255.0, A.add),
            ts(T.ch[:, 0:1], T.td[:, 32:33], float(XH_H), A.mult, 128.0, A.add),
-           ts(of["n2"], T.td[:, 192:193], 0.125, A.mult, None, None),
+           ts(of["n2"], T.td[:, 0:1], 0.125, A.mult, None, None),
+           ts(T.mk[:], T.xa[:], T.tb[:, 32:33], A.not_equal, 2000.0, A.mult),
            ts(T.dm[:], T.er[:], T.td[:, 128:129], A.is_equal, 0.5, A.mult, k_er)]
 
-    n_in = {k: arrivals(k, core, T.cores, topo) for k in KINDS}
-    ready = [("c1", n_in["c1"]), ("s1", n_in["s1"]), v_own, a_own]
+    n_in = {k: arrivals(k, core, T.cores, topo) for k in ("k1", "c1", "s1", "n1", "c2", "s2", "n2")}
+    ready = [v_own, a_own, ("c1", n_in["c1"] + n_in["s1"])]
     d_k = dma("y", T.lk[me, 0:16, 0], T.cum[0:16, 127:128], v_c)
     d_n = dma("y", T.lnd[me, 32 * ime:32 * ime + 32, 0], T.nt[32 * ime:32 * ime + 32, jme // 4:jme // 4 + 1], a_nt)
-    d_c = dma("y", T.crow[0:1, :], T.lk[:, 2 * jme:2 * jme + 2, 0], ("k1", n_in["k1"]), d_k)
-    d_nr = dma("y", T.nrow[0:1, 0:256], T.lnd[:, 32 * ime:32 * ime + 32, 0], ("n1", n_in["n1"]), d_n)
+    d_c = dma("y", T.crow[0:1, :], T.lk[:, 2 * jme:2 * jme + 2, 0], d_k, ("k1", n_in["k1"]))
+    d_nr = dma("y", T.nrow[0:1, 0:256], T.lnd[:, 32 * ime:32 * ime + 32, 0], d_n, ("n1", n_in["n1"]))
     ld_vx = dma("y", T.vxt[:], T.vx[:])
     ld_vh = dma("y", T.vht[:], T.vh[:])
     d_neg = dma("y", T.lwd[me, 16 * jme:16 * jme + 16, 0], T.neg[0:1, :], k_misc)
     wait("p", [d_c])
     g_cnt = done("p", g.partition_broadcast(T.cb[:], T.crow[0:1, :], 128))
+    k_oh32 = iota(T.oh32[:], [[32, 8]], 0, 0)
     wait("p", [d_nr])
     g_num = done("p", g.partition_broadcast(T.num[:, 0:256], T.nrow[0:1, 0:256], 128))
-    k_oh32 = iota(T.oh32[:], [[32, 8]], 0, 0)
 
     def wmm(out, i, a, n):
         return mm(out, T.wq[:, 128 * i:128 * i + 128], T.ws[:, 128 * i:128 * i + 128], T.xh[:, a:a + n], T.xhs[:, a:a + n],
-                  True, True, q_w, ready, v_rm)
+                  True, True, q_w, ready)
 
-    col = {n: T.col[:, 2 * i:2 * i + 2] for i, n in enumerate(("e8", "sc", "F", "base"))}
+    col = {"e8": T.col[:, 0:2], "sc": T.col[:, 4:6], "F": T.col[:, 6:8], "base": T.col[:, 8:10]}
 
     def one(n, h):
         return col[n][:, h:h + 1]
 
-    mw = [wmm(T.pw[:, 512 * i:512 * i + 256], i, 0, 256) for i in range(3)]
-    mw += [wmm(T.pw[:, 1536:1664], 3, 0, 128), wmm(T.pz[:, 0:128], 3, 128, 128)]
-    r0 = ts(T.ht[:, 0:1024:4], T.pw[:, 0:256], 0.0, A.max, 0.0625, A.mult, mw[0])
-    r1 = act(T.ht[:, 1:1024:4], T.pw[:, 512:768], AF.Relu, mw[1], scale=0.0625)
-    r2 = act(T.ht[:, 2:1024:4], T.pw[:, 1024:1280], AF.Relu, mw[2], scale=0.0625)
-    r3b = act(T.ht[:, 515:1024:4], T.pz[:, 0:128], AF.Relu, mw[4], scale=0.0625)
+    bank = [T.pw[:, 512 * i:512 * i + 128] for i in range(4)] + [T.pz[:, 0:128]] + [T.pe[:, 512 * i:512 * i + 128] for i in range(3)]
+    mw = [wmm(bank[k], k % 4, 128 * (k // 4), 128) for k in range(8)]
+    rel = []
+    for k in range(8):
+        o = T.ht[:, 512 * (k // 4) + k % 4:512 * (k // 4) + 512:4]
+        rel.append(ts(o, bank[k], 0.0, A.max, 0.0625, A.mult, mw[k]) if k in (0, 2, 4) else act(o, bank[k], AF.Relu, mw[k], scale=0.0625))
+    q_h = [quant(T.xh[:, XH_H:XH_H + 128], T.xhs[:, XH_H:XH_H + 128], T.ht[:, 0:512], rel[0:4])]
     t = ts(T.cw[:, 0:8], T.cb[:, 0:16:2], 32.0, A.min, 32.0, A.subtract, g_cnt)
-    r3a = ts(T.ht[:, 3:512:4], T.pw[:, 1536:1664], 0.0, A.max, 0.0625, A.mult, mw[3])
-    t = scan(T.cw[:, 16:24], T.zt[:, 0:8], T.cw[:, 0:8], 0.0, A.add, A.add, t)
-    q_h = [quant(T.xh[:, XH_H:XH_H + 128], T.xhs[:, XH_H:XH_H + 128], T.ht[:, 0:512], r0, r1, r2, r3a)]
-    q_h.append(quant(T.xh[:, XH_H + 128:XH_H + 256], T.xhs[:, XH_H + 128:XH_H + 256], T.ht[:, 512:1024], r3b))
+    t = scan(T.cw[:, 16:32], T.zt[:, 0:16], T.cw[:, 0:16], 0.0, A.add, A.add, t)
+    q_h.append(quant(T.xh[:, XH_H + 128:XH_H + 256], T.xhs[:, XH_H + 128:XH_H + 256], T.ht[:, 512:1024], rel))
     t = copy(T.gq[:], T.cw[:].indirect(of["gl"]), t)
-    v_n4 = ts(T.gq[:, 6:8], T.gq[:, 0:2], -1.0, A.mult, T.cw[:, 23:24], A.add, t)
-    v_b = ts(col["base"], T.gq[:, 2:4], T.td[:, 96:97], A.is_le, 1024.0, A.mult)
     m_e, m_r = [], []
     for h in range(2):
         a = XH_H + 128 * h
-        m_e.append(mm(T.pe[:, 0:128], T.xh[:, a:a + 128], T.xhs[:, a:a + 128], T.mq[:, 128 * h:128 * h + 128],
-                      T.ms[:, 128 * h:128 * h + 128], h == 0, h == 1, q_h[h]))
-        m_r.append(mm(T.pe[:, 512 + 512 * h:640 + 512 * h], T.eq[:], T.es[:], T.xh[:, a:a + 128], T.xhs[:, a:a + 128], True, True))
-    row = [T.pe[:, 512 + 512 * h:640 + 512 * h] for h in range(2)]
+        m_e.append(mm(bank[2 * h], T.xh[:, a:a + 128], T.xhs[:, a:a + 128], T.mq[:], T.ms[:], True, True, q_h[h]))
+        m_r.append(mm(bank[2 * h + 1], T.eq[:], T.es[:], T.xh[:, a:a + 128], T.xhs[:, a:a + 128], True, True))
+    row = [bank[1], bank[3]]
 
     def seg(k):
         return T.lt[:, SEG * k:SEG * k + 128]
 
     f = 0.6 * 2.0 ** -23
-    v_e8 = act(col["e8"], T.pe[:, 64:80:8], AF.Copy, m_e[1])
-    a_sc = act(col["sc"], T.pe[:, 64:80:8], AF.Abs, scale=f, bias=1e-37)
-    v_l1 = ts(seg(1), row[0], one("e8", 1), A.is_le, None, None, v_e8, m_r[0])
-    v_r = scan(T.rr[:], T.d16[:], T.pe[:, 0:16], 0.0, A.add, A.max, a_sc)
-    v_g4 = tt(T.g4[:], T.pe[:, 64:96:8], T.thr[:], A.is_ge)
-    a_c0 = act(T.cc[:, 0:128], T.tri[:], AF.Identity, a_sc, k_tri, scale=one("sc", 0), bias=one("e8", 0))
+
+    def keys(h):
+        return [act(one("e8", h), bank[2 * h][:, 8:9], AF.Copy, m_e[h]),
+                act(one("sc", h), bank[2 * h][:, 8:9], AF.Abs, scale=f, bias=1e-37)]
+
+    def bound(h, dep):
+        return act(T.cc[:, 128 * h:128 * h + 128], T.tri[:], AF.Identity, k_tri, dep, scale=one("sc", h), bias=one("e8", h))
+
+    def runmax(h, dep):
+        return scan(T.rr[:, 8 * h:8 * h + 8], T.zt[:, 0:8], bank[2 * h][:, 0:8], -BIG, A.add, A.max, dep)
+
+    def second(h, dep):
+        return act(T.js[:, 8 * h:8 * h + 8], T.rr[:, 8 * h:8 * h + 8], AF.Sign, dep, scale=-1.0, bias=T.rr[:, 8 * h + 7:8 * h + 8],
+                   accum_out=one("F", h))
+
+    def place(h, dep):
+        return ts(T.gw[:, 32 * h:32 * h + 32], xb2[:], one("F", h), A.is_equal, DF - 0.5, A.mult, dep)
+
+    def empty(h, *deps):
+        return [ts(T.lt[:, SEG * h + 128:SEG * h + 129], one("e8", h), 0.0, A.is_equal, T.gq[:, h:h + 1], A.mult, *deps),
+                ts(T.lt[:, SEG * (2 + h) + 128:SEG * (2 + h) + 129], one("e8", h), 0.0, A.is_gt, T.gq[:, 2:3], A.mult)]
+
+    def rank(h, *deps):
+        return scan(T.sa[:, SEG * h:SEG * h + 129], T.lt[:, SEG * h:SEG * h + 129], T.lt[:, SEG * (2 + h):SEG * (2 + h) + 129],
+                    one("base", h), A.add, A.add, *deps)
+
+    def verdict(q):
+        return ts(T.tvv[0:32, 32 + 32 * q:64 + 32 * q], T.gw[32 * q:32 * q + 32, 32:64], T.sa[32 * q:32 * q + 32, SEG + 128:SEG + 129],
+                  A.is_gt, None, None, v_a[1])
+
+    a_k0 = keys(0)
+    a_c0 = bound(0, a_k0)
+    v_r0 = runmax(0, a_k0)
+    empty(0, t)
+    a_b = act(col["base"], T.gq[:, 4:6], AF.Relu, t, scale=-1024.0, bias=T.td[:, 96:97])
+    a_k1 = keys(1)
     a_sg = act(T.sg[:], row[1], AF.Sign, m_r[1], scale=-1.0, bias=one("e8", 0))
-    a_c1 = act(T.cc[:, 128:256], T.tri[:], AF.Identity, scale=one("sc", 1), bias=one("e8", 1))
+    a_c1 = bound(1, a_k1)
+    a_f0 = second(0, v_r0)
     a_l0 = act(seg(0), T.sg[:], AF.Relu, a_sg)
-    for h in range(2):
-        a_f = act(T.js[:, 8 * h:8 * h + 8], T.rr[:, 8 * h:8 * h + 8], AF.Sign, v_r, scale=-1.0, bias=T.rr[:, 8 * h + 7:8 * h + 8], accum_out=one("F", h))
-    v_l2 = tt(seg(2), row[0], T.cc[:, 0:128], A.is_lt, a_c0)
-    v_co = tt(T.lt[:, 128:4 * SEG:SEG], T.g4[:], T.gq[:, 4:8], A.mult, v_g4)
+    v_l2 = tt(seg(2), row[0], T.cc[:, 0:128], A.is_lt, m_r[0], a_c0)
+    v_l1 = ts(seg(1), row[0], one("e8", 1), A.is_le, None, None, a_k1[0])
+    v_r1 = runmax(1, a_k1)
+    a_f1 = second(1, v_r1)
+    empty(1)
     v_l3 = tt(seg(3), row[1], T.cc[:, 128:256], A.is_lt, a_c1)
-    v_a = []
-    for h in (0, 1):
-        v_a.append(scan(T.sa[:, SEG * h:SEG * h + 129], T.lt[:, SEG * h:SEG * h + 129], T.lt[:, SEG * (2 + h):SEG * (2 + h) + 129],
-                        one("base", h), A.add, A.add, v_co, (a_l0, v_l3)[h]))
-    v_g = [ts(T.gw[:, 32 * h:32 * h + 32], xb2[:], one("F", h), A.is_equal, DF - 0.5, A.mult, a_f, k_xb2) for h in range(2)]
-    v_v = [ts(T.tvv[:, 32 * h:32 * h + 32], T.gw[:, 32 * h:32 * h + 32], T.sa[:, SEG * h + 128:SEG * h + 129], A.is_gt, None, None, v_g[h])
-           for h in range(2)]
-    v_t = [turn(T.m2[:, 128 * h:128 * h + 32], T.tvv[:, 32 * h:32 * h + 32], v_v[h]) for h in range(2)]
-    bc = []
-    for q in range(1, 4):
-        bc.append(act(T.m2[0:32, 32 * q:32 * q + 32], T.m2[32 * q:32 * q + 32, 0:32], AF.Copy, v_t[0]))
-        bc.append(copy(T.m2[0:32, 128 + 32 * q:160 + 32 * q], T.m2[32 * q:32 * q + 32, 128:160], v_t[1]))
+    v_g = [place(0, a_f0)]
+    v_a = [rank(0, v_l2, a_l0)]
+    v_g.append(place(1, a_f1))
+    v_a.append(rank(1, v_l3))
+    v_v = ts(T.tvv[:, 0:32], T.gw[:, 0:32], T.sa[:, 128:129], A.is_gt, None, None, v_a[0])
+    verdict(0)
+    v_t = turn(T.m2[:, 0:32], T.tvv[:, 0:32], v_v)
+    verdict(1)
+    bc = [act(T.m2[0:32, 32 * q:32 * q + 32], T.m2[32 * q:32 * q + 32, 0:32], AF.Copy, v_t) for q in range(1, 4)]
+    verdict(2)
+    bc.append(turn(T.m2[0:32, 128:256], T.tvv[0:32, 32:160], verdict(3)))
     v_c2 = scan(T.cum2[0:32, :], T.zt[0:32, 0:256], T.m2[0:32, :], 0.0, A.add, A.add, bc)
-    v_mn = lists(2, T.cum2[:], T.th2, 256, T.jv2, T.sv2, T.l2, T.lx2, T.lt2, T.mn2, of["s2"], of["v2"], v_c2, [])
+    sa = [act(T.js[:, 256 * k:256 * k + 256], T.cum2[:], AF.Sign, v_c2, scale=-1.0, bias=T.th2[:, 2 * k:2 * k + 1], accum_out=T.l2[:, k:k + 1])
+          for k in range(2)]
+    pa = [ts(T.jv2[:, 256 * k:256 * k + 256], T.cum2[:], T.th2[:, 2 * k + 1:2 * k + 2], A.is_le, 2.0, A.mult, v_c2) for k in range(2)]
+    pb = [scan(T.sv2[:, 256 * k:256 * k + 256], T.zt[:], T.jv2[:, 256 * k:256 * k + 256], -256.0, A.add, A.add, pa[k]) for k in range(2)]
+    x0 = tt(T.lx2[:, 0:32:2], T.l2[:, 0:2].indirect(of["s2"]), T.mk[:, 0:32:2], A.add, sa)
+    x1 = tt(T.lx2[:, 1:32:2], T.sv2[:].indirect(of["v2"]), T.mk[:, 1:32:2], A.add, pb)
+    t = turn(T.lt2[0:32, :], T.lx2[0:32, :], x1)
+    v_mn = [tt(T.mn2[32 * k:32 * k + 32, :], T.lt2[0:32, 0:16], T.lt2[0:32, 16:32], A.min, t) for k in range(2)]
     v_o = [ts(T.off2[64 * k:64 * k + 64, :], T.mn2[0:64, :], 0.5, A.mult, T.ch[0:64, 0:1], A.add, v_mn) for k in range(2)]
     a_mn = act(T.mn2[64:128, :], T.mn2[0:64, :], AF.Copy, v_mn)
     v_s2, a_s2 = picks(T.s2c, T.s2s, T.xh[:], T.xhs[:], T.off2, v_o)
@@ -444,30 +485,27 @@ def rank_program(g, core, T, topo):
     t = [tt(T.wa[:], T.s128[:].indirect(T.offw[:, 0:2]), T.dm[:], A.mult, t),
          tt(T.wb[:], T.num[:].indirect(T.offw[:, 0:2]), T.dm[:], A.mult, g_num)]
     v_w = scan(T.wc[:], T.wa[:], T.wb[:], 0.0, A.add, A.add, t)
-    send_stage("2", T.s2c, T.s2s, T.l2c, T.r2c, T.r2s, v_s2, a_s2)
-    send("n2", "rn2", lambda first, n: T.wc[:, 31:32], T.rl2[:], v_w)
+    send_stage("2", T.s2c, T.s2s, T.l2c, T.l2s, T.r2c, T.r2s, v_s2, a_s2)
+    send(p["out"]["n2"], "rn2", lambda first, n: T.wc[:, 31:32], T.rl2[:], v_w)
     q_vx = quant(T.vxq[:], T.vxs[:], T.vxt[:], ld_vx)
     q_vh = quant(T.vhq[:], T.vhs[:], T.vht[:], ld_vh)
     k_ofh = ts(T.ofh[:], T.oh32[:], T.td[:, 160:161], A.add, None, None, k_oh32)
     dz = [pick(T.l2c[:, w0:w0 + 32], T.xq[:], ofz), pick(T.l2c[:, 256:272], T.xq[:], ofz1),
           spick(T.l2s[:, w0:w0 + 32], T.xs[:], ofz), spick(T.l2s[:, 256:272], T.xs[:], ofz1)]
 
-    ready = [("c2", n_in["c2"]), ("s2", n_in["s2"]), dz]
-    out = (T.pz[:, 0:128], T.pw[:, 512:640])
-    my = []
-    for k in range(2):
-        a = 128 * k
-        mm(out[k], T.vxq[:], T.vxs[:], T.l2c[:, a:a + 128], T.l2s[:, a:a + 128], True, False, ready)
-        my.append(mm(out[k], T.vhq[:], T.vhs[:], T.l2c[:, a + 2:a + 130], T.l2s[:, a + 2:a + 130], False, True))
+    ready = dz + [("c2", n_in["c2"] + n_in["s2"])]
+    out = T.pz[:, 0:256]
+    mm(out, T.vxq[:], T.vxs[:], T.l2c[:, 0:256], T.l2s[:, 0:256], True, False, ready)
+    my = mm(out, T.vhq[:], T.vhs[:], T.l2c[:, 2:258], T.l2s[:, 2:258], False, True)
     a_hp = spick(T.hps[:], T.l2s[:, 0:256], T.ofh[:], ready)
     v_hp = pick(T.hp[:], T.l2c[:, 0:256], T.ofh[:], ready)
-    for k in range(2):
-        for r in range(2):
-            v_y = copy(T.ys[:, 64 * k + r:64 * k + 64:2], out[k][:, r:128:4], my[k])
     dma("y", T.oc[:, 0:512], T.hp[:].bitcast(dt.uint8), v_hp)
-    dma("y", T.y[:], T.ys[:], v_y)
     for k in range(4):
-        dma("s", T.osc[4 * k:4 * k + 4, 0:128], T.hps[32 * k:32 * k + 4, 0:128], a_hp)
-    dma("s", T.who[0:1, 0:128], T.lwd[:, 16 * jme:16 * jme + 16, 0], ("n2", n_in["n2"]), d_neg)
+        dma("y" if k == 0 else "s", T.osc[4 * k:4 * k + 4, 0:128], T.hps[32 * k:32 * k + 4, 0:128], a_hp)
+    for r in range(2):
+        v_y = copy(T.ys[:, r:128:2], out[:, r:256:4], my)
+    last = dma("y", T.y[:], T.ys[:], v_y)
+    dma("s", T.who[0:1, 0:128], T.lwd[:, 16 * jme:16 * jme + 16, 0], d_neg, ("n2", n_in["n2"]))
     g.wait_ge(T.sem.sent, sent[0])
-    wait("p", [(s, everything[s]) for s in everything])
+    wait("p", [(s, everything[s]) for s in everything if s != last[0]])
+    wait("p", [last])

from concourse.bass import DstId, RemoteDMATransfer
from concourse.mybir import dt, AluOpType, AxisListType, ActivationFunctionType

F8, U8, U16, BF, F32, I32 = "float8_e4m3fn_x4", "uint8", "uint16", "bfloat16", "float32", "int32"
DF, NR = 64, 8
BIG = 1.0e29
XW = 138
XH_H = 272
SEG = 144


def _sb(w, d):
    return ("sbuf", [128, w], d)


SCRATCH = {
    "xt": _sb(4 * XW, BF), "wt": _sb(2048, BF), "r2l": _sb(48, BF), "r2m": _sb(512, BF),
    "vxt": _sb(512, BF), "vht": _sb(512, BF), "zt": _sb(256, BF), "ht": _sb(1024, BF),
    "xq": _sb(XW, F8), "xs": _sb(XW, U8), "wq": _sb(512, F8), "ws": _sb(512, U8), "mq": _sb(128, F8), "ms": _sb(128, U8),
    "eq": _sb(128, F8), "es": _sb(128, U8), "vxq": _sb(128, F8), "vxs": _sb(128, U8), "vhq": _sb(128, F8), "vhs": _sb(128, U8),
    "s1c": _sb(256, F8), "s1s": _sb(256, U8), "r1c": _sb(64, F8), "r1s": _sb(64, U8), "xh": _sb(544, F8), "xhs": _sb(544, U8),
    "s2c": _sb(256, F8), "s2s": _sb(256, U8), "r2c": _sb(64, F8), "r2s": _sb(64, U8), "l2c": _sb(272, F8), "l2s": _sb(272, U8),
    "hp": _sb(128, F8), "hps": _sb(128, U8),
    "rlk": ("dram", [128, 1], BF), "lk": ("dram", [8, 128, 1], BF), "rl1": ("dram", [128, 1], BF), "lnd": ("dram", [8, 128, 1], BF),
    "rl2": ("dram", [128, 1], F32), "lwd": ("dram", [8, 128, 1], F32),
    "ofs": _sb(24, U16), "ofh": _sb(8, U16), "ofe": _sb(8, U16), "ta": _sb(96, F32), "tb": _sb(96, F32), "tc": _sb(192, F32),
    "td": _sb(192, F32), "ch": _sb(2, F32), "th1": _sb(8, F32), "th2": _sb(4, F32), "xa": _sb(32, F32), "xb1": _sb(32, F32),
    "xb2": _sb(32, F32), "mk": _sb(32, F32), "ones": _sb(128, BF), "tri": _sb(128, BF), "oh32": _sb(8, F32),
    "er": _sb(32, F32), "dm": _sb(32, F32), "s128": _sb(272, BF), "neg": _sb(16, F32),
    "rm": _sb(8, F32), "f1": _sb(8, F32), "oh": _sb(128, BF), "mr": _sb(128, BF), "cum": _sb(128, BF),
    "js": _sb(1024, BF), "jv": _sb(8 * 132, BF), "sv": _sb(8 * 132, BF), "dp": _sb(132, BF), "lt1": _sb(32, BF),
    "mn1": _sb(16, F32), "off1": _sb(16, U16), "nt": _sb(16, BF),
    "crow": _sb(16, BF), "cb": _sb(16, BF), "cw": _sb(32, F32),
    "gq": _sb(16, F32), "nrow": _sb(256, BF), "num": _sb(272, BF),
    "col": _sb(16, F32), "gw": _sb(64, F32), "cc": _sb(256, F32), "lt": _sb(4 * SEG, BF), "sg": _sb(128, BF),
    "sa": _sb(2 * SEG, BF), "rr": _sb(16, F32), "tvv": _sb(160, BF), "m2": _sb(256, BF), "cum2": _sb(256, BF), "jv2": _sb(512, BF),
    "sv2": _sb(512, BF), "l2": _sb(8, F32), "lx2": _sb(32, F32), "lt2": _sb(32, F32), "mn2": _sb(16, F32), "off2": _sb(16, U16),
    "offw": _sb(16, U16), "wa": _sb(32, F32), "wb": _sb(32, F32), "wc": _sb(32, F32),
    "ys": _sb(128, F32),
    "pw": ("psum", [128, 2048], F32), "pe": ("psum", [128, 1536], F32), "pz": ("psum", [128, 512], F32),
}
NDMA = 30
SEMAPHORES = (["kv", "ks", "kt", "kp", "sent", "k1", "c1", "n1", "c2", "n2", "rk1", "rc1", "rs1", "rn1", "rc2", "rs2", "rn2"]
              + ["d%d" % i for i in range(NDMA)])


def split(engines, parts):
    k = 1
    while 2 * k * parts <= len(engines):
        k *= 2
    return [engines[k * i:k * i + k] for i in range(parts)]


def plan(src, cores, topo):
    first = [d for d in cores if d == cores[0] or topo.may_write(cores[0], d)]
    order = first + [d for d in cores if d not in first]
    near = [d for d in order if d == src or topo.may_write(src, d)]
    far = [d for d in order if d not in near]
    direct = [d for d in near if d != src]
    others = sorted((c for c in topo.cores_of(src) if c != src), key=lambda c: (topo.die(c) == topo.die(src), c))
    can = [c for c in others if all(topo.may_write(c, d) for d in far)]
    rest = [c for c in others if c not in can]
    off = topo.engines(src, direct[0])
    every = topo.engines(src, can[0])
    up = [e for e in every if e not in off]
    a, b, c = can[0:2], can[2:4], rest[0:2]
    jf, jn = order.index(far[0]), order.index(near[0])

    def fan(h, tos, base=0):
        es = split(topo.engines(h, tos[0]), len(tos))
        return [(d, es[i], order.index(d) - base) for i, d in enumerate(tos)]

    on = {}
    for k in range(2):
        f2, j = far[2 * k:2 * k + 2], order.index(direct[k])
        on[a[k]] = [("k1", fan(a[k], f2[:1])), ("c1", fan(a[k], f2, jf + 2 * k)), ("c2", fan(a[k], f2, jf + 2 * k))]
        on[b[k]] = [("k1", fan(b[k], f2[1:])), ("s1", fan(b[k], f2, jf + 2 * k)), ("s2", fan(b[k], f2, jf + 2 * k))]
        on[c[k]] = [("k1", fan(c[k], direct[k::2])), ("s1", fan(c[k], direct[k:k + 1], j)), ("s2", fan(c[k], direct[k:k + 1], j))]
    on[b[0]].insert(2, ("n1", fan(b[0], far)))
    on[c[0]].insert(2, ("n1", fan(c[0], direct)))
    on[b[1]].append(("n2", fan(b[1], far + direct)))
    h2, q4, u2 = split(every, 2), split(every, 4), split(up, 2)
    out = {"ka": [(h, q4[i], 0, 0) for i, h in enumerate(a + b)], "kb": [(h, h2[i], 0, 0) for i, h in enumerate(c)],
           "c": [(h, every, jf + 2 * i, 2) for i, h in enumerate(a)], "s": [(h, every, jf + 2 * i, 2) for i, h in enumerate(b)],
           "sn": [(h, h2[i], order.index(direct[i]), 1) for i, h in enumerate(c)],
           "dc": [(d, off, order.index(d), 1) for d in direct], "ds": [(direct[2], off, order.index(direct[2]), 1)],
           "n1": [(b[0], u2[0], jf // 4, 0), (c[0], u2[1], jn // 4, 0)], "n2": [(b[1], up, 0, 0)]}
    return {"order": order, "out": out, "on": on, "halves": (jf // 4, jn // 4)}


def bits(engines):
    v = 0
    for e in engines:
        v |= 1 << e
    return v


def arrivals(kind, core, cores, topo):
    n = 0
    for s in cores:
        if s != core:
            p = plan(s, cores, topo)
            if kind[0] in "cs":
                n += sum(len(e) for d, e, x, y in p["out"]["d" + kind[0]] if d == core)
            for h in p["on"]:
                n += sum(len(e) for k, ws in p["on"][h] if k == kind for d, e, x in ws if d == core)
    return n


def transfer(core, to, engines, sem, src, dst, topo):
    rid, pid = topo.addr(to, core)
    return RemoteDMATransfer(dst_ids=[DstId(rid=rid, pnc=pid)], dma_engine_mask=bits(engines), remote_sem=sem, src=src, dst=dst)


def helper_program(g, core, T, topo):
    home = [c for c in T.cores if c in topo.cores_of(core)]
    if not home:
        return
    src = home[0]
    p = plan(src, T.cores, topo)
    if core not in p["on"]:
        return
    s, sent = T.rank_of(src), 0

    def columns(t, b):
        return t[:, 32 * b:32 * b + 32]

    for kind, writes in p["on"][core]:
        keys = {"k": ("ka", "kb"), "c": ("c",), "s": ("s", "sn"), "n": (kind,)}[kind[0]]
        g.wait_ge(T.sem["r" + kind], sum(len(e) for k in keys for h, e, x, y in p["out"][k] if h == core))
        tr = []
        for d, e, k in writes:
            if kind == "k1":
                a, b = T.rlk[:], T.lk[s]
            elif kind[0] == "n":
                a, b = (T.rl1[:], T.lnd[s]) if kind == "n1" else (T.rl2[:], T.lwd[s])
            elif kind[0] == "s":
                a, b = (columns(T.r1s, k), columns(T.xhs, s)) if kind == "s1" else (columns(T.r2s, k), columns(T.l2s, s))
            else:
                a, b = (columns(T.r1c, k), columns(T.xh, s)) if kind == "c1" else (columns(T.r2c, k), columns(T.l2c, s))
                a, b = a.bitcast(dt.uint8), b.bitcast(dt.uint8)
            tr.append(transfer(core, d, e, T.sem[kind.replace("s", "c")], a, b, topo))
            sent += len(e)
        g.remote_dma_fused(tr, local_sem=T.sem.sent)
    g.wait_ge(T.sem.sent, sent)


def rank_program(g, core, T, topo):
    me = T.rank_of(core)
    if me is None:
        helper_program(g, core, T, topo)
        return
    A, AF = AluOpType, ActivationFunctionType
    eng = {"v": g.vector, "s": g.scalar, "t": g.tensor, "p": g, "y": g.sync}
    cnt = {q: 0 for q in eng}
    seen = {q: {} for q in eng}
    ndma = [0]
    everything = {}
    p = plan(core, T.cores, topo)
    perm = [T.rank_of(d) for d in p["order"]]
    jme = perm.index(me)
    ime = jme % 4
    w0 = 32 * me

    def wait(q, deps):
        need, todo = {}, list(deps)
        for d in todo:
            if isinstance(d, list):
                todo.extend(d)
            else:
                need[d[0]] = max(need.get(d[0], 0), d[1])
        for sem in need:
            if seen[q].get(sem, 0) < need[sem]:
                eng[q].wait_ge(T.sem[sem], need[sem])
                seen[q][sem] = need[sem]

    def done(q, inst):
        cnt[q] += 1
        inst.then_inc(T.sem["k" + q], 1)
        everything["k" + q] = cnt[q]
        return ("k" + q, cnt[q])

    def dma(q, out, in_, *deps):
        wait(q, deps)
        sem = "d%d" % ndma[0]
        ndma[0] += 1
        eng[q].dma_start(out, in_).then_inc(T.sem[sem], 16)
        everything[sem] = 16
        return (sem, 16)

    def ts(out, in0, s1, op0, s2, op1, *deps):
        wait("v", deps)
        if op1 is None:
            return done("v", g.vector.tensor_scalar(out, in0, s1, None, op0))
        return done("v", g.vector.tensor_scalar(out, in0, s1, s2, op0, op1))

    def tt(out, a, b, op, *deps):
        wait("v", deps)
        return done("v", g.vector.tensor_tensor(out, a, b, op))

    def copy(out, in_, *deps):
        wait("v", deps)
        return done("v", g.vector.tensor_copy(out, in_))

    def fill(ap, c, *deps):
        wait("v", deps)
        return done("v", g.vector.memset(ap, c))

    def scan(out, a, b, init, op0, op1, *deps):
        wait("v", deps)
        return done("v", g.vector.tensor_tensor_scan(out, a, b, init, op0, op1))

    def turn(out, in_, *deps):
        wait("v", deps)
        return done("v", g.vector.transpose(out, in_))

    def quant(q, s, in_, *deps):
        wait("v", deps)
        return done("v", g.vector.quantize_mx(q, s, in_))

    def act(out, in_, func, *deps, **kw):
        wait("s", deps)
        return done("s", g.scalar.activation(out, in_, func, **kw))

    def sfill(out, n, c):
        return act(out, T.zt[:, 0:n], AF.Identity, bias=c)

    def mm(out, l, ls, r, rs, start, stop, *deps):
        wait("t", deps)
        return done("t", g.tensor.matmul_mx(out, l, ls, r, rs, start, stop))

    def iota(out, pattern, base, cm):
        return done("p", g.iota(out, pattern, base, cm, allow_small_or_imprecise_dtypes=True))

    def pick(out, win, off, *deps):
        return copy(out.bitcast(dt.uint32), win.bitcast(dt.uint32).indirect(off), *deps)

    def spick(out, win, off, *deps):
        return act(out, win.indirect(off), AF.Copy, *deps)

    ld_x = dma("y", T.xt[:, 0:512], T.x[:])
    ld_r = dma("s", T.xt[:, 520:552], T.rt[:, 0:32])
    ld_w = dma("y", T.wt[:], T.w[:], ld_x)
    ld_2 = dma("y", T.r2l[:, 0:36], T.r2[:, 0:36])

    k_ta = [iota(T.ta[:, 0:32], [[8, 2], [0, 8], [16, 2]], 0, 1), iota(T.ta[:, 32:64], [[1, 2], [0, 16]], 0, 0),
            iota(T.ta[:, 64:96], [[16, 2], [0, 8], [128, 2]], 0, 1)]
    k_xa = iota(T.xa[:], [[0, 2], [1, 2], [0, 8]], 0, 0)
    k_tc = [iota(T.tc[:, 0:32], [[16, 2], [0, 8], [8, 2]], 0, 1), iota(T.tc[:, 32:64], [[0, 8], [1, 2], [0, 2]], 0, 0),
            iota(T.tc[:, 96:128], [[1024, 32]], -31 * 1024, 0)]
    k_tc += [iota(T.tc[:, 64 + 16 * m:80 + 16 * m], [[-480, 4], [256, 2], [128, 2]], 480, 1) for m in range(2)]
    k_tc += [iota(T.tc[:, 128:160], [[0, 2], [1, 16]], 0, 0), iota(T.tc[:, 160:192], [[0, 2], [4, 8], [1, 2]], 2, 0)]
    k_er = iota(T.er[:], [[2, 8], [0, 2], [1, 2]], 0, 0)
    of = {n: T.ofs[:, 2 * i:2 * i + 1] for i, n in enumerate(("s2", "v2", "n1", "n2", "gl"))}
    ofz = T.ofs[:, 16:18]
    k_zt = fill(T.zt[:], 0.0)
    k_z0 = fill(T.xt[:, 512:520], 0.0)
    k_cum = fill(T.cum[:], 0.0)
    k_ones = fill(T.ones[:], 1.0)
    k_ofz = [fill(ofz, 128), fill(T.ofe[:], 8)]
    fill(T.dp[:, 0:128], 0.0)
    for k in range(4):
        fill(T.jv[:, 128 + k:8 * 132:132], 0.0)
    k_cum2 = fill(T.cum2[:], 0.0)
    wait("p", [k_ones])
    k_tri = done("p", g.affine_select(T.tri[:], T.ones[:], [[-1, 128]], A.is_gt, 0.0, 0, 1))
    for k in range(2):
        k_r2m = act(T.r2m[:, 256 * k:256 * k + 256], T.zt[:], AF.Copy, k_zt)
    tabs = [(T.xb1, perm)] + ([] if me else [(T.xb2, [{0: 99, 1: 0}.get(b, b) for b in perm])])
    for tab, vals in tabs:
        t = [sfill(tab[:, 2 * j:2 * j + 2], 2, float(vals[j])) for j in range(NR)]
    k_cw = sfill(T.cw[:, 8:16], 8, 0.0)
    for tab, vals in tabs:
        act(tab[:, 16:32], tab[:, 0:16], AF.Copy, t)
    xb2 = tabs[-1][0]
    k_tb = turn(T.tb[:], T.ta[:], k_ta)

    q_x = quant(T.xq[:], T.xs[:], T.xt[:], k_z0, ld_r, ld_x)
    k_th1 = ts(T.th1[:], T.tb[:, 0:8], 0.5, A.add, None, None, k_tb)
    ts(T.dp[:, 128:129], T.tb[:, 32:33], 2048.0, A.mult, None, None)
    ts(T.dp[:, 129:132:2], T.tb[:, 32:34], -4096.0, A.mult, 2048.0, A.add)
    m_g = mm(T.pz[:, 0:128], T.xq[:, 0:128], T.xs[:, 0:128], T.xq[:, XW - 128:XW], T.xs[:, XW - 128:XW], True, True, q_x)
    v_rm = scan(T.rm[:], T.zt[:, 0:8], T.pz[:, 120:128], -BIG, A.add, A.max, m_g)
    ts(T.dp[:, 130:131], T.tb[:, 32:33], 4096.0, A.mult, -2048.0, A.add)
    k_n1 = ts(of["n1"], T.tb[:, 64:65], 0.0625, A.mult, None, None)
    a_f = act(T.js[:, 0:8], T.rm[:], AF.Sign, v_rm, scale=-1.0, bias=T.rm[:, 7:8], accum_out=T.f1[:, 0:1])
    v_oh = [ts(T.oh[0:32, 32 * q:32 * q + 32], T.xb1[32 * q:32 * q + 32, :], T.f1[32 * q:32 * q + 32, 0:1], A.is_equal, None, None, a_f)
            for q in range(4)]
    v_m = turn(T.mr[0:32, :], T.oh[0:32, :], v_oh)
    v_c = scan(T.cum[0:32, :], T.zt[0:32, 0:128], T.mr[0:32, :], 0.0, A.add, A.add, v_m)

    def picks(codes, scales, win, wins, off, *deps):
        v, a = [], []
        far, near = p["halves"]
        for k, n in ((8 * far, 4), (8 * far + 4, 4), (8 * near, 8)):
            v.append(pick(codes[:, 16 * k:16 * (k + n)], win, off[:, k:k + n], *deps))
            a.append(spick(scales[:, 16 * k:16 * (k + n)], wins, off[:, k:k + n], *deps))
        return v, a

    fl = []
    for v in range(8):
        o = T.jv[0:32, 132 * v:132 * v + 128]
        if v < 4:
            fl.append(ts(o, T.cum[0:32, :], T.th1[0:32, v:v + 1], A.is_le, 2.0, A.mult, v_c))
        else:
            fl.append(act(o, T.cum[0:32, :], AF.Sign, v_c, scale=-1.0, bias=T.th1[0:32, v:v + 1]))
    for v in range(8):
        t = scan(T.sv[0:32, v:8 * 132:8], T.dp[0:32, :], T.jv[0:32, 132 * v:132 * v + 132], -128.0 if v < 4 else 0.0, A.add, A.add, fl[v])
    t = turn(T.lt1[0:32, :], T.sv[0:32, 1024:1056], t)
    v_mn = [tt(T.mn1[32 * k:32 * k + 32, :], T.lt1[0:32, 0:16], T.lt1[0:32, 16:32], A.min, t) for k in range(2)]
    v_o = [ts(T.off1[64 * k:64 * k + 64, :], T.mn1[0:64, :], 0.5, A.mult, 64.0, A.add, v_mn) for k in range(2)]
    a_mn = act(T.mn1[64:128, :], T.mn1[0:64, :], AF.Copy, v_mn)
    v_s1, a_s1 = picks(T.s1c, T.s1s, T.xq[:], T.xs[:], T.off1, v_o)
    v_own = pick(T.xh[:, w0:w0 + 32], T.xq[:], T.off1[:, 2 * jme:2 * jme + 2])
    a_nt = act(T.nt[:], T.mn1[:].indirect(of["n1"]), AF.Identity, a_mn, scale=0.5, bias=64.0)
    a_own = spick(T.xhs[:, w0:w0 + 32], T.xs[:], T.off1[:, 2 * jme:2 * jme + 2])

    sent = [0]

    def send(writes, kind, src_of, dst, *deps):
        wait("p", deps)
        tr = []
        for to, e, first, n in writes:
            tr.append(transfer(core, to, e, T.sem[kind], src_of(first, n), dst, topo))
            sent[0] += len(e)
        g.remote_dma_fused(tr, local_sem=T.sem.sent)

    def send_stage(st, codes, scales, land, land_s, relay_c, relay_s, dep_c, dep_s):
        def c_src(first, n):
            return codes[:, 32 * first:32 * (first + n)].bitcast(dt.uint8)

        def s_src(first, n):
            return scales[:, 32 * first:32 * (first + n)]

        o = p["out"]
        for k in range(2):
            send(o["c"][k:k + 1], "rc" + st, c_src, relay_c[:].bitcast(dt.uint8), dep_c[k])
            send(o["s"][k:k + 1], "rs" + st, s_src, relay_s[:], dep_s[k])
        send(o["sn"], "rs" + st, s_src, relay_s[:, 0:32], dep_s)
        for k in range(3):
            send(o["dc"][k:k + 1], "c" + st, c_src, land[:, w0:w0 + 32].bitcast(dt.uint8), dep_c)
        send(o["ds"], "c" + st, s_src, land_s[:, w0:w0 + 32])

    for key in ("ka", "kb"):
        send(p["out"][key], "rk1", lambda first, n: T.cum[:, 127:128], T.rlk[:], v_c)
    send_stage("1", T.s1c, T.s1s, T.xh, T.xhs, T.r1c, T.r1s, v_s1, a_s1)
    send(p["out"]["n1"], "rn1", lambda first, n: T.nt[:, first:first + 1], T.rl1[:], a_nt)

    q_w = quant(T.wq[:], T.ws[:], T.wt[:], ld_w)
    ofz1 = T.ofs[:, 16:17]
    z2 = [pick(T.xh[:, a:a + 16], T.xq[:], ofz1) for a in (256, XH_H + 256)]
    nb = me - 1 if me else 1
    t = act(T.r2m[:, 0:36], T.r2l[:, 0:36], AF.Copy, ld_2)
    z2 += [spick(T.xhs[:, a:a + 16], T.xs[:], ofz1) for a in (256, XH_H + 256)]
    k_misc = [sfill(T.num[:, 256:272], 16, -1.0), sfill(T.neg[:], 16, -1.0)]
    a_r2 = act(T.r2m[:, 4 * me:4 * me + 4], T.r2l[:, 4 * nb:4 * nb + 4], AF.Copy, t)
    for s in range(NR + 1):
        sfill(T.s128[:, 32 * s:min(32 * s + 32, 272)], 32 if s < NR else 16, 128.0 * (s % NR))
    q_m = quant(T.mq[:], T.ms[:], T.r2m[:], a_r2)
    k_tg = turn(T.td[:], T.tc[:], k_tc)
    q_e = [pick(T.eq[:], T.mq[:, 0:128], T.ofe[:], q_m), spick(T.es[:], T.ms[:, 0:128], T.ofe[:], q_m)]
    k_2 = [ts(of["gl"], T.td[:, 64:65], 0.03125, A.mult, None, None, k_tg), ts(T.th2[:], T.tb[:, 0:8:2], 0.5, A.mult, 0.5, A.add),
           copy(of["s2"], T.td[:, 32:33]), ts(of["v2"], T.td[:, 32:33], 256.0, A.mult, 255.0, A.add),
           ts(T.ch[:, 0:1], T.td[:, 32:33], float(XH_H), A.mult, 128.0, A.add),
           ts(of["n2"], T.td[:, 0:1], 0.125, A.mult, None, None),
           ts(T.mk[:], T.xa[:], T.tb[:, 32:33], A.not_equal, 2000.0, A.mult),
           ts(T.dm[:], T.er[:], T.td[:, 128:129], A.is_equal, 0.5, A.mult, k_er)]

    n_in = {k: arrivals(k, core, T.cores, topo) for k in ("k1", "c1", "s1", "n1", "c2", "s2", "n2")}
    ready = [v_own, a_own, ("c1", n_in["c1"] + n_in["s1"])]
    d_k = dma("y", T.lk[me, 0:16, 0], T.cum[0:16, 127:128], v_c)
    d_n = dma("y", T.lnd[me, 32 * ime:32 * ime + 32, 0], T.nt[32 * ime:32 * ime + 32, jme // 4:jme // 4 + 1], a_nt)
    d_c = dma("y", T.crow[0:1, :], T.lk[:, 2 * jme:2 * jme + 2, 0], d_k, ("k1", n_in["k1"]))
    d_nr = dma("y", T.nrow[0:1, 0:256], T.lnd[:, 32 * ime:32 * ime + 32, 0], d_n, ("n1", n_in["n1"]))
    ld_vx = dma("y", T.vxt[:], T.vx[:])
    ld_vh = dma("y", T.vht[:], T.vh[:])
    d_neg = dma("y", T.lwd[me, 16 * jme:16 * jme + 16, 0], T.neg[0:1, :], k_misc)
    wait("p", [d_c])
    g_cnt = done("p", g.partition_broadcast(T.cb[:], T.crow[0:1, :], 128))
    k_oh32 = iota(T.oh32[:], [[32, 8]], 0, 0)
    wait("p", [d_nr])
    g_num = done("p", g.partition_broadcast(T.num[:, 0:256], T.nrow[0:1, 0:256], 128))

    def wmm(out, i, a, n):
        return mm(out, T.wq[:, 128 * i:128 * i + 128], T.ws[:, 128 * i:128 * i + 128], T.xh[:, a:a + n], T.xhs[:, a:a + n],
                  True, True, q_w, ready)

    col = {"e8": T.col[:, 0:2], "sc": T.col[:, 4:6], "F": T.col[:, 6:8], "base": T.col[:, 8:10]}

    def one(n, h):
        return col[n][:, h:h + 1]

    bank = [T.pw[:, 512 * i:512 * i + 128] for i in range(4)] + [T.pz[:, 0:128]] + [T.pe[:, 512 * i:512 * i + 128] for i in range(3)]
    mw = [wmm(bank[k], k % 4, 128 * (k // 4), 128) for k in range(8)]
    rel = []
    for k in range(8):
        o = T.ht[:, 512 * (k // 4) + k % 4:512 * (k // 4) + 512:4]
        rel.append(ts(o, bank[k], 0.0, A.max, 0.0625, A.mult, mw[k]) if k in (0, 2, 4) else act(o, bank[k], AF.Relu, mw[k], scale=0.0625))
    q_h = [quant(T.xh[:, XH_H:XH_H + 128], T.xhs[:, XH_H:XH_H + 128], T.ht[:, 0:512], rel[0:4])]
    t = ts(T.cw[:, 0:8], T.cb[:, 0:16:2], 32.0, A.min, 32.0, A.subtract, g_cnt)
    t = scan(T.cw[:, 16:32], T.zt[:, 0:16], T.cw[:, 0:16], 0.0, A.add, A.add, t)
    q_h.append(quant(T.xh[:, XH_H + 128:XH_H + 256], T.xhs[:, XH_H + 128:XH_H + 256], T.ht[:, 512:1024], rel))
    t = copy(T.gq[:], T.cw[:].indirect(of["gl"]), t)
    m_e, m_r = [], []
    for h in range(2):
        a = XH_H + 128 * h
        m_e.append(mm(bank[2 * h], T.xh[:, a:a + 128], T.xhs[:, a:a + 128], T.mq[:], T.ms[:], True, True, q_h[h]))
        m_r.append(mm(bank[2 * h + 1], T.eq[:], T.es[:], T.xh[:, a:a + 128], T.xhs[:, a:a + 128], True, True))
    row = [bank[1], bank[3]]

    def seg(k):
        return T.lt[:, SEG * k:SEG * k + 128]

    f = 0.6 * 2.0 ** -23

    def keys(h):
        return [act(one("e8", h), bank[2 * h][:, 8:9], AF.Copy, m_e[h]),
                act(one("sc", h), bank[2 * h][:, 8:9], AF.Abs, scale=f, bias=1e-37)]

    def bound(h, dep):
        return act(T.cc[:, 128 * h:128 * h + 128], T.tri[:], AF.Identity, k_tri, dep, scale=one("sc", h), bias=one("e8", h))

    def runmax(h, dep):
        return scan(T.rr[:, 8 * h:8 * h + 8], T.zt[:, 0:8], bank[2 * h][:, 0:8], -BIG, A.add, A.max, dep)

    def second(h, dep):
        return act(T.js[:, 8 * h:8 * h + 8], T.rr[:, 8 * h:8 * h + 8], AF.Sign, dep, scale=-1.0, bias=T.rr[:, 8 * h + 7:8 * h + 8],
                   accum_out=one("F", h))

    def place(h, dep):
        return ts(T.gw[:, 32 * h:32 * h + 32], xb2[:], one("F", h), A.is_equal, DF - 0.5, A.mult, dep)

    def empty(h, *deps):
        return [ts(T.lt[:, SEG * h + 128:SEG * h + 129], one("e8", h), 0.0, A.is_equal, T.gq[:, h:h + 1], A.mult, *deps),
                ts(T.lt[:, SEG * (2 + h) + 128:SEG * (2 + h) + 129], one("e8", h), 0.0, A.is_gt, T.gq[:, 2:3], A.mult)]

    def rank(h, *deps):
        return scan(T.sa[:, SEG * h:SEG * h + 129], T.lt[:, SEG * h:SEG * h + 129], T.lt[:, SEG * (2 + h):SEG * (2 + h) + 129],
                    one("base", h), A.add, A.add, *deps)

    def verdict(q):
        return ts(T.tvv[0:32, 32 + 32 * q:64 + 32 * q], T.gw[32 * q:32 * q + 32, 32:64], T.sa[32 * q:32 * q + 32, SEG + 128:SEG + 129],
                  A.is_gt, None, None, v_a[1])

    a_k0 = keys(0)
    a_c0 = bound(0, a_k0)
    v_r0 = runmax(0, a_k0)
    empty(0, t)
    a_b = act(col["base"], T.gq[:, 4:6], AF.Relu, t, scale=-1024.0, bias=T.td[:, 96:97])
    a_k1 = keys(1)
    a_sg = act(T.sg[:], row[1], AF.Sign, m_r[1], scale=-1.0, bias=one("e8", 0))
    a_c1 = bound(1, a_k1)
    a_f0 = second(0, v_r0)
    a_l0 = act(seg(0), T.sg[:], AF.Relu, a_sg)
    v_l2 = tt(seg(2), row[0], T.cc[:, 0:128], A.is_lt, m_r[0], a_c0)
    v_l1 = ts(seg(1), row[0], one("e8", 1), A.is_le, None, None, a_k1[0])
    v_r1 = runmax(1, a_k1)
    a_f1 = second(1, v_r1)
    empty(1)
    v_l3 = tt(seg(3), row[1], T.cc[:, 128:256], A.is_lt, a_c1)
    v_g = [place(0, a_f0)]
    v_a = [rank(0, v_l2, a_l0)]
    v_g.append(place(1, a_f1))
    v_a.append(rank(1, v_l3))
    v_v = ts(T.tvv[:, 0:32], T.gw[:, 0:32], T.sa[:, 128:129], A.is_gt, None, None, v_a[0])
    verdict(0)
    v_t = turn(T.m2[:, 0:32], T.tvv[:, 0:32], v_v)
    verdict(1)
    bc = [act(T.m2[0:32, 32 * q:32 * q + 32], T.m2[32 * q:32 * q + 32, 0:32], AF.Copy, v_t) for q in range(1, 4)]
    verdict(2)
    bc.append(turn(T.m2[0:32, 128:256], T.tvv[0:32, 32:160], verdict(3)))
    v_c2 = scan(T.cum2[0:32, :], T.zt[0:32, 0:256], T.m2[0:32, :], 0.0, A.add, A.add, bc)
    sa = [act(T.js[:, 256 * k:256 * k + 256], T.cum2[:], AF.Sign, v_c2, scale=-1.0, bias=T.th2[:, 2 * k:2 * k + 1], accum_out=T.l2[:, k:k + 1])
          for k in range(2)]
    pa = [ts(T.jv2[:, 256 * k:256 * k + 256], T.cum2[:], T.th2[:, 2 * k + 1:2 * k + 2], A.is_le, 2.0, A.mult, v_c2) for k in range(2)]
    pb = [scan(T.sv2[:, 256 * k:256 * k + 256], T.zt[:], T.jv2[:, 256 * k:256 * k + 256], -256.0, A.add, A.add, pa[k]) for k in range(2)]
    x0 = tt(T.lx2[:, 0:32:2], T.l2[:, 0:2].indirect(of["s2"]), T.mk[:, 0:32:2], A.add, sa)
    x1 = tt(T.lx2[:, 1:32:2], T.sv2[:].indirect(of["v2"]), T.mk[:, 1:32:2], A.add, pb)
    t = turn(T.lt2[0:32, :], T.lx2[0:32, :], x1)
    v_mn = [tt(T.mn2[32 * k:32 * k + 32, :], T.lt2[0:32, 0:16], T.lt2[0:32, 16:32], A.min, t) for k in range(2)]
    v_o = [ts(T.off2[64 * k:64 * k + 64, :], T.mn2[0:64, :], 0.5, A.mult, T.ch[0:64, 0:1], A.add, v_mn) for k in range(2)]
    a_mn = act(T.mn2[64:128, :], T.mn2[0:64, :], AF.Copy, v_mn)
    v_s2, a_s2 = picks(T.s2c, T.s2s, T.xh[:], T.xhs[:], T.off2, v_o)
    t = ts(T.offw[:], T.mn2[:].indirect(of["n2"]), 0.5, A.mult, 128.0, A.add, a_mn)
    t = [tt(T.wa[:], T.s128[:].indirect(T.offw[:, 0:2]), T.dm[:], A.mult, t),
         tt(T.wb[:], T.num[:].indirect(T.offw[:, 0:2]), T.dm[:], A.mult, g_num)]
    v_w = scan(T.wc[:], T.wa[:], T.wb[:], 0.0, A.add, A.add, t)
    send_stage("2", T.s2c, T.s2s, T.l2c, T.l2s, T.r2c, T.r2s, v_s2, a_s2)
    send(p["out"]["n2"], "rn2", lambda first, n: T.wc[:, 31:32], T.rl2[:], v_w)
    q_vx = quant(T.vxq[:], T.vxs[:], T.vxt[:], ld_vx)
    q_vh = quant(T.vhq[:], T.vhs[:], T.vht[:], ld_vh)
    k_ofh = ts(T.ofh[:], T.oh32[:], T.td[:, 160:161], A.add, None, None, k_oh32)
    dz = [pick(T.l2c[:, w0:w0 + 32], T.xq[:], ofz), pick(T.l2c[:, 256:272], T.xq[:], ofz1),
          spick(T.l2s[:, w0:w0 + 32], T.xs[:], ofz), spick(T.l2s[:, 256:272], T.xs[:], ofz1)]

    ready = dz + [("c2", n_in["c2"] + n_in["s2"])]
    out = T.pz[:, 0:256]
    mm(out, T.vxq[:], T.vxs[:], T.l2c[:, 0:256], T.l2s[:, 0:256], True, False, ready)
    my = mm(out, T.vhq[:], T.vhs[:], T.l2c[:, 2:258], T.l2s[:, 2:258], False, True)
    a_hp = spick(T.hps[:], T.l2s[:, 0:256], T.ofh[:], ready)
    v_hp = pick(T.hp[:], T.l2c[:, 0:256], T.ofh[:], ready)
    dma("y", T.oc[:, 0:512], T.hp[:].bitcast(dt.uint8), v_hp)
    for k in range(4):
        dma("y" if k == 0 else "s", T.osc[4 * k:4 * k + 4, 0:128], T.hps[32 * k:32 * k + 4, 0:128], a_hp)
    for r in range(2):
        v_y = copy(T.ys[:, r:128:2], out[:, r:256:4], my)
    last = dma("y", T.y[:], T.ys[:], v_y)
    dma("s", T.who[0:1, 0:128], T.lwd[:, 16 * jme:16 * jme + 16, 0], d_neg, ("n2", n_in["n2"]))
    g.wait_ge(T.sem.sent, sent[0])
    wait("p", [(s, everything[s]) for s in everything if s != last[0]])
    wait("p", [last])
